import numpy as np
import ml_dtypes


def mxq(x, axis, fmt="e4m3"):
    dtype, down = {"e4m3": (ml_dtypes.float8_e4m3fn, 7), "e5m2": (ml_dtypes.float8_e5m2, 14)}[fmt]
    v = np.moveaxis(np.asarray(x, np.float32).astype(ml_dtypes.bfloat16).astype(np.float64), axis, -1)
    blocks = v.reshape(v.shape[:-1] + (-1, 32))
    amax = np.abs(blocks).max(-1, keepdims=True)
    byte = np.maximum(np.where(amax > 0, np.frexp(amax)[1] - 1 + 127, 0) - down, 1)
    scale = np.exp2(byte - 127.0)
    codes = (blocks / scale).astype(np.float32).astype(dtype).astype(np.float64)
    return np.moveaxis((codes * scale).reshape(v.shape), -1, axis)


WIDE = False


def mx_kscale(k):
    if not WIDE:
        return np.ones(k)
    levels = np.array([10, -10, 5, -5, 0])
    if k % 512:
        return np.exp2(np.random.permutation(np.resize(levels, k // 32))).repeat(32)
    a = np.empty((k // 512, 16))
    for p in range(k // 512):
        a[p, :8] = np.random.permutation(np.resize(levels, 8))
        for g in range(8):
            far = levels[np.abs(levels - a[p, g]) >= 10]
            a[p, g + 8] = far[np.random.randint(len(far))]
    return np.exp2(a.ravel()).repeat(32)


BF16 = ml_dtypes.bfloat16


def bf(x):
    return np.asarray(x, np.float32).astype(BF16)


def f64(x):
    return np.asarray(x).astype(np.float64)


E2M1 = np.array([0.0, 0.5, 1.0, 1.5, 2.0, 3.0, 4.0, 6.0, -0.0, -0.5, -1.0, -1.5, -2.0, -3.0, -4.0, -6.0])


def pack_weight(w, fmt):
    k, n = w.shape
    w = f64(bf(w)).reshape(k // 32, 32, n)
    amax = np.abs(w).max(1)
    if fmt == "e4m3":
        byte = np.frexp(amax)[1] - 1 + 127 - 7
    else:
        mant, ex = np.frexp(amax / 6.0)
        byte = np.where(mant > 0.5, ex, ex - 1) + 127
    byte = np.clip(np.where(amax > 0, byte, 1), 1, 254)
    scaled = (w * np.exp2(127.0 - byte)[:, None, :]).reshape(k, n).astype(np.float32)
    by_word = np.ascontiguousarray(scaled.reshape(k // 512, 128, 4, n).transpose(0, 1, 3, 2))
    if fmt == "e4m3":
        words = by_word.astype(ml_dtypes.float8_e4m3fn).view(np.uint8)
    else:
        c = by_word.astype(ml_dtypes.float4_e2m1fn).view(np.uint8) & 0xF
        words = c[..., 0::2] | (c[..., 1::2] << 4)
    return np.ascontiguousarray(words), np.ascontiguousarray(byte.astype(np.uint8).reshape(k // 512, 16, n))


def unpack_weight(words, scales, fmt):
    g, p, n, _ = words.shape
    if fmt == "e4m3":
        vals = np.ascontiguousarray(words).view(ml_dtypes.float8_e4m3fn).astype(np.float64)
    else:
        nib = np.empty((g, p, n, 4), np.uint8)
        nib[..., 0::2] = words & 0xF
        nib[..., 1::2] = words >> 4
        vals = E2M1[nib]
    vals = vals * np.repeat(np.exp2(scales.astype(np.float64) - 127.0), 8, axis=1)[..., None]
    return vals.transpose(0, 1, 3, 2).reshape(g * 512, n)
def pack4(w):
    words, scales = pack_weight(w, "e2m1")
    return words.reshape(words.shape[0], 128, -1), scales


def unpack4(words, scales):
    return unpack_weight(words.reshape(words.shape[0], 128, -1, 2), scales, "e2m1")


P, R, T = 1024, 1024, 2048


def setup_inputs():
    r, s, t = mx_kscale(R), mx_kscale(T), mx_kscale(P)
    gain = np.random.uniform(0.8, 1.25, P)
    lam = np.random.uniform(0.5, 1.5, R)
    f = np.random.standard_normal((R, P)) / np.sqrt(R) * gain
    a_words, a_scales = pack4(f * lam[:, None] * r[:, None])
    b_words, b_scales = pack4(f / r[:, None] * t)
    z = 1.5 * np.random.standard_normal((T, P)) / np.sqrt(T)
    wt = np.random.uniform(0.5, 1.5, T)
    return {"a_words": a_words, "a_scales": a_scales,
            "b_words": b_words, "b_scales": b_scales,
            "xw": bf(z * wt[:, None] * s[:, None] / t),
            "x": bf(z / s[:, None]),
            "d": bf((f * f * lam[:, None]).sum(axis=0))}


def reference(a_words, a_scales, b_words, b_scales, xw, x, d):
    a = unpack4(a_words, a_scales)
    b = unpack4(b_words, b_scales)
    omega = a.T @ b
    cov = mxq(f64(xw), 0, "e4m3").T @ mxq(f64(x), 0, "e4m3")
    y = mxq(omega, 1, "e4m3") @ mxq(cov, 0, "e4m3")
    return y + y.T - np.diag(1.0 / f64(d))

@@ -1,0 +1,457 @@
+from contextlib import ExitStack
+
+import concourse.mybir as mybir
+from concourse.masks import make_identity
+
+FLOPS = 2 * 1024 * 1024 * (1024 + 2048 + 1024)
+
+F32 = mybir.dt.float32
+BF16 = mybir.dt.bfloat16
+I32 = mybir.dt.int32
+U32 = mybir.dt.uint32
+U8 = mybir.dt.uint8
+FP8X4 = mybir.dt.float8_e4m3fn_x4
+FP4X4 = mybir.dt.float4_e2m1fn_x4
+ALU = mybir.AluOpType
+
+P = 128
+
+
+def tile_concord_precision_gradient_s12_kernel(tc, a_words, a_scales, b_words, b_scales, xw, x, d, out):
+    nc = tc.nc
+    with ExitStack() as ctx:
+        keep = ctx.enter_context(tc.tile_pool(name="keep", bufs=1))
+        work = ctx.enter_context(tc.tile_pool(name="work", bufs=5))
+        psum = ctx.enter_context(tc.psum_pool(name="psum", bufs=8))
+        ctx.enter_context(tc.manual_schedule())
+
+        def kt(name, shape, dt):
+            t = keep.tile(shape, dt, name=name, tag=name, align_bytes=64)
+            return t
+
+        def bank():
+            t = psum.tile([P, 512], F32, name="bank", tag="bank")
+            return t
+
+        def copy(eng, dst, src):
+            if eng == "S":
+                nc.scalar.copy(out=dst, in_=src)
+            else:
+                nc.vector.tensor_copy(out=dst, in_=src)
+
+        a_codes = [kt("a_codes%d" % h, [P, 2, 1024], U8) for h in range(2)]
+        a_sc = kt("a_sc", [P, 2, 1024], U8)
+        b_raw = [kt("b_raw%d" % h, [P, 2, 1024], U8) for h in range(2)]
+        b_codes = [kt("b_codes%d" % h, [P, 2, 1024], U8) for h in range(2)]
+        b_scr = kt("b_scr", [P, 2, 1024], U8)
+        b_sc = kt("b_sc", [P, 2, 1024], U8)
+        w_rawf = {c: kt("w_raw%d" % c, [P, 4, 1024], BF16) for c in range(1, 4)}
+        w_raw = {(h, 0): kt("w_raw0%d" % h, [P, 4, 512], BF16) for h in range(2)}
+        x_raw = {(h, c): kt("x_raw%d%d" % (h, c), [P, 4, 512], BF16) for c in range(4) for h in range(2)}
+        w_codes = {(h, c): kt("w_codes%d%d" % (h, c), [P, 512], U32) for h in range(2) for c in range(4)}
+        w_sc = {(h, c): kt("w_sc%d%d" % (h, c), [P, 512], U8) for h in range(2) for c in range(4)}
+        x_codes = {(h, c): kt("x_codes%d%d" % (h, c), [P, 512], U32) for h in range(2) for c in range(4)}
+        x_sc = {(h, c): kt("x_sc%d%d" % (h, c), [P, 512], U8) for h in range(2) for c in range(4)}
+        o_codes = kt("o_codes", [P, 2, 1024], U32)
+        o_sc = kt("o_sc", [P, 2, 1024], U8)
+        c_codes = kt("c_codes", [P, 2, 1024], U32)
+        c_sc = kt("c_sc", [P, 2, 1024], U8)
+        og = {(h, q): kt("og%d%d" % (h, q), [P, 512, 4], BF16) for h in range(2) for q in range(2)}
+        kg = {(h, l): kt("kg%d%d" % (h, l), [P, 512, 4], BF16) for h in range(2) for l in range(2)}
+        gs = {(0, b): kt("gs0%d" % b, [P, 128 * (b + 1)], F32) for b in range(4)}
+        for b in range(4, 8):
+            gs[1, b] = kt("gs1%d" % b, [P, 512], F32)
+            gs[2, b] = kt("gs2%d" % b, [P, 128 * (b - 3)], F32)
+        ut = {(0, a): kt("ut0%d" % a, [P, 512], F32) for a in range(4)}
+        for a in range(3):
+            ut[2, a] = kt("ut2%d" % a, [P, 128 * (3 - a)], F32)
+        for a in range(4, 7):
+            ut[1, a] = kt("ut1%d" % a, [P, 128 * (7 - a)], F32)
+        identx = kt("identx", [P, 512], F32)
+        ident = identx[:, 384:512]
+        d_row = kt("d_row", [P, 128], BF16)
+        d_f32 = kt("d_f32", [P, 128], F32)
+        d_rec = kt("d_rec", [P, 8], F32)
+        d_neg = kt("d_neg", [P, 8], F32)
+        grp = {}
+        ps = {}
+
+        nc.vector.memset(b_scr[:].bitcast(I32), 0)
+        nc.vector.memset(a_sc[:].bitcast(I32), 0)
+
+        def load_b(h):
+            nc.sync.dma_start(out=b_raw[h][:].bitcast(I32), in_=b_words[:, :, h * 1024 : (h + 1) * 1024].bitcast(I32).rearrange("g p n -> p g n"))
+
+        def load_a(q):
+            nc.sync.dma_start(out=a_codes[q][:].bitcast(I32), in_=a_words[:, :, q * 1024 : (q + 1) * 1024].bitcast(I32).rearrange("g p n -> p g n"))
+
+        def load_sc(eng, dst, src):
+            for q in range(4):
+                eng.dma_start(out=dst[32 * q : 32 * q + 4, :, :].bitcast(I32), in_=src[:, 4 * q : 4 * q + 4, :].bitcast(I32).rearrange("g q n -> q g n"))
+
+        def load_w(c):
+            nc.sync.dma_start(out=w_rawf[c][:], in_=xw[c * 512 : (c + 1) * 512, :].rearrange("(p j) w -> p j w", j=4))
+
+        def load_k(dst, src, h, c):
+            nc.sync.dma_start(out=dst[h, c][:], in_=src[c * 512 : (c + 1) * 512, h * 512 : (h + 1) * 512].rearrange("(p j) w -> p j w", j=4))
+
+        load_a(0)
+        load_sc(nc.sync, a_sc, a_scales)
+        load_sc(nc.sync, b_scr, b_scales)
+        load_b(0)
+        load_k(x_raw, x, 0, 0)
+        load_w(2)
+        load_b(1)
+        load_w(1)
+        load_a(1)
+        load_k(w_raw, xw, 0, 0)
+        load_k(w_raw, xw, 1, 0)
+        load_k(x_raw, x, 0, 1)
+        load_k(x_raw, x, 0, 3)
+        load_k(x_raw, x, 0, 2)
+        load_w(3)
+        load_k(x_raw, x, 1, 0)
+        load_k(x_raw, x, 1, 2)
+        load_k(x_raw, x, 1, 1)
+        load_k(x_raw, x, 1, 3)
+        nc.gpsimd.memset(d_row[:], 0.0)
+        nc.gpsimd.dma_start(out=d_row[0:8, :], in_=d.rearrange("(a p) -> a p", p=128))
+        nc.gpsimd.memset(identx[:], 0.0)
+        make_identity(nc, ident)
+        nc.gpsimd.tensor_copy(out=d_f32[:], in_=d_row[:])
+
+        def pS():
+            nc.vector.tensor_copy(
+                out=b_sc[:].bitcast(I32).rearrange("p g (h u s) -> p g h u s", h=2, u=4),
+                in_=b_scr[:].bitcast(I32).rearrange("p g (h s u) -> p g h u s", h=2, u=4),
+            )
+
+        def pB(h):
+            nc.vector.tensor_copy(
+                out=b_codes[h][:].bitcast(I32).rearrange("p g (u s w) -> p g u s w", u=4, w=2),
+                in_=b_raw[h][:].bitcast(I32).rearrange("p g (s u w) -> p g u s w", u=4, w=2),
+            )
+
+        def Om(h, ib):
+            t = bank()
+            ps["O", h, ib] = t
+            for u in range(4):
+                for g in range(2):
+                    nc.tensor.matmul_mx(
+                        out=t[:, u * 128 : (u + 1) * 128],
+                        lhsT=b_codes[h][:, g, u * 256 : (u + 1) * 256].bitcast(FP4X4),
+                        lhsT_scale=b_sc[:, g, h * 512 + u * 128 : h * 512 + (u + 1) * 128],
+                        rhs=a_codes[ib // 4][:, g, (ib % 4) * 256 : (ib % 4 + 1) * 256].bitcast(FP4X4),
+                        rhs_scale=a_sc[:, g, ib * 128 : (ib + 1) * 128],
+                        start=(g == 0),
+                        stop=(g == 1),
+                    )
+
+        def eO(h, ib, E):
+            n0 = (ib % 4) * 128
+            copy(E, og[h, ib // 4][:, n0 : n0 + 128, :], ps["O", h, ib][:].rearrange("p (u n) -> p n u", u=4))
+
+        def qO(h, q):
+            nc.vector.quantize_mx(out=o_codes[:, h, q * 512 : (q + 1) * 512].bitcast(FP8X4), scales=o_sc[:, h, q * 512 : (q + 1) * 512], in_=og[h, q][:].rearrange("p n t -> p (n t)"))
+
+        def i(k, h, c, E):
+            t = work.tile([P, 2048], BF16, name="grp", tag="grp", align_bytes=64)
+            grp[k, h, c] = t
+            if k == "W":
+                copy(E, t[:].rearrange("p (u s w j) -> p u s j w", u=4, s=32, w=4), (w_rawf[c][:, :, h * 512 : (h + 1) * 512] if c else w_raw[h, 0][:]).rearrange("p j (s u w) -> p u s j w", u=4, w=4))
+            else:
+                copy(E, t[:].rearrange("p (a w j) -> p a j w", w=4, j=4), x_raw[h, c][:].rearrange("p j (a w) -> p a j w", w=4))
+
+        def q(k, h, c):
+            co, sc = (w_codes, w_sc) if k == "W" else (x_codes, x_sc)
+            nc.vector.quantize_mx(out=co[h, c][:].bitcast(FP8X4), scales=sc[h, c][:], in_=grp[k, h, c][:])
+
+        def K(h, l, p, f, c):
+            if c == 0:
+                ps["K", h, l, p, f] = bank()
+            t = ps["K", h, l, p, f]
+            for e in range(2):
+                u = 2 * p + e
+                nc.tensor.matmul_mx(
+                    out=t[:, e * 256 : (e + 1) * 256],
+                    lhsT=w_codes[h, c][:, u * 128 : (u + 1) * 128].bitcast(FP8X4),
+                    lhsT_scale=w_sc[h, c][:, u * 128 : (u + 1) * 128],
+                    rhs=x_codes[l, c][:, f * 256 : (f + 1) * 256].bitcast(FP8X4),
+                    rhs_scale=x_sc[l, c][:, f * 256 : (f + 1) * 256],
+                    start=(c == 0 and e == 0),
+                    stop=(c == 3 and e == 1),
+                )
+
+        def eK(h, l, p, f, E):
+            copy(E, kg[h, l][:, f * 256 : (f + 1) * 256, 2 * p : 2 * p + 2], ps["K", h, l, p, f][:].rearrange("p (u n) -> p n u", u=2))
+
+        def qK(h, l, f):
+            lo = l * 512 + f * 256
+            nc.vector.quantize_mx(out=c_codes[:, h, lo : lo + 256].bitcast(FP8X4), scales=c_sc[:, h, lo : lo + 256], in_=kg[h, l][:, f * 256 : (f + 1) * 256, :].rearrange("p n t -> p (n t)"))
+
+        def span(p, b):
+            return (512, 128 * (b - 3)) if p == 2 else (0, 512) if p == 1 else (0, 128 * (b + 1))
+
+        def G(p, b):
+            t = bank()
+            ps["G", p, b] = t
+            lo, n = span(p, b)
+            bs = slice(b * 128, (b + 1) * 128)
+            for o, w in ([(0, 256), (256, 128)] if n == 384 else [(0, n)]):
+                ns = slice(lo + o, lo + o + w)
+                step = 0
+                for h in range(2):
+                    for lc, ls, rc, rs in ((o_codes, o_sc, c_codes, c_sc), (c_codes, c_sc, o_codes, o_sc)):
+                        nc.tensor.matmul_mx(
+                            out=t[:, o : o + w],
+                            lhsT=lc[:, h, bs].bitcast(FP8X4),
+                            lhsT_scale=ls[:, h, bs],
+                            rhs=rc[:, h, ns].bitcast(FP8X4),
+                            rhs_scale=rs[:, h, ns],
+                            start=(step == 0),
+                            stop=(step == 3),
+                        )
+                        step += 1
+
+        def eG(p, b, E):
+            lo, n = span(p, b)
+            t = ps["G", p, b]
+            g = gs[p, b]
+            if p == 1:
+                copy(E, g[:], t[:])
+            else:
+                z = 384 - (b * 128 - lo)
+                nc.vector.scalar_tensor_tensor(out=g[:], in0=identx[:, z : z + n], scalar=d_neg[:, b : b + 1], in1=t[:, 0:n], op0=ALU.mult, op1=ALU.add)
+            nc.sync.dma_start(out=out[b * 128 : (b + 1) * 128, lo : lo + n], in_=g[:])
+
+        def tr_strips(p, a):
+            return range(4, 8) if p == 0 else range(a + 1, 8) if p == 1 else range(a + 1, 4)
+
+        def Tr(p, a):
+            t = bank()
+            ps["T", p, a] = t
+            for m, b in enumerate(tr_strips(p, a)):
+                src = gs[1, b][:, a * 128 : (a + 1) * 128] if p == 0 else gs[0, b][:, a * 128 : (a + 1) * 128] if p == 2 else gs[2, b][:, a * 128 - 512 : a * 128 - 384]
+                nc.tensor.transpose(t[:, m * 128 : (m + 1) * 128], src, ident)
+
+        def eT(p, a, E):
+            u = ut[p, a]
+            n = 128 * len(tr_strips(p, a))
+            hi = 512 if p == 2 else 1024
+            copy(E, u[:], ps["T", p, a][:, 0:n])
+            nc.sync.dma_start(out=out[a * 128 : (a + 1) * 128, hi - n : hi], in_=u[:])
+
+        def dT():
+            t = bank()
+            ps["d"] = t
+            nc.tensor.transpose(t[:, 0:128], d_f32[:], ident)
+
+        def dN():
+            nc.vector.reciprocal(out=d_rec[:], in_=ps["d"][:, 0:8])
+            nc.vector.tensor_scalar(out=d_neg[:], in0=d_rec[:], scalar1=-1.0, scalar2=None, op0=ALU.mult)
+
+        pB(0)
+        pS()
+        Om(0, 2)
+        i("X", 0, 0, "V")
+        Om(0, 3)
+        eO(0, 2, "S")
+        q("X", 0, 0)
+        i("W", 0, 2, "V")
+        i("W", 1, 2, "S")
+        Om(0, 1)
+        Om(0, 0)
+        pB(1)
+        q("W", 0, 2)
+        Om(1, 1)
+        eO(0, 3, "S")
+        Om(1, 3)
+        q("W", 1, 2)
+        eO(1, 1, "S")
+        i("W", 0, 1, "V")
+        Om(1, 2)
+        i("W", 1, 1, "S")
+        Om(1, 5)
+        eO(1, 2, "V")
+        Om(0, 4)
+        q("W", 0, 1)
+        Om(1, 7)
+        i("W", 0, 0, "V")
+        eO(0, 4, "S")
+        Om(1, 6)
+        eO(0, 0, "S")
+        Om(1, 0)
+        q("W", 1, 1)
+        eO(0, 1, "S")
+        Om(1, 4)
+        i("W", 1, 0, "V")
+        eO(1, 0, "S")
+        Om(0, 7)
+        eO(1, 6, "S")
+        q("W", 0, 0)
+        Om(0, 6)
+        eO(1, 4, "S")
+        i("X", 0, 1, "V")
+        eO(1, 3, "S")
+        K(0, 0, 1, 0, 0)
+        K(0, 0, 1, 1, 0)
+        eO(0, 7, "S")
+        Om(0, 5)
+        q("W", 1, 0)
+        i("X", 0, 2, "S")
+        q("X", 0, 1)
+        K(1, 0, 1, 0, 0)
+        K(1, 0, 0, 0, 0)
+        eO(0, 6, "V")
+        K(0, 0, 1, 1, 1)
+        i("X", 0, 3, "V")
+        K(0, 0, 0, 1, 0)
+        K(1, 0, 1, 0, 1)
+        eO(1, 7, "S")
+        K(1, 0, 0, 0, 1)
+        K(0, 0, 0, 1, 1)
+        eO(0, 5, "S")
+        q("X", 0, 2)
+        K(1, 0, 0, 1, 0)
+        K(1, 0, 0, 1, 1)
+        i("W", 1, 3, "S")
+        i("W", 0, 3, "V")
+        K(1, 0, 1, 0, 2)
+        K(0, 0, 1, 1, 2)
+        K(0, 0, 1, 0, 1)
+        K(1, 0, 1, 1, 0)
+        q("X", 0, 3)
+        K(1, 0, 0, 1, 2)
+        K(0, 0, 1, 0, 2)
+        K(0, 0, 0, 1, 2)
+        q("W", 0, 3)
+        K(1, 0, 1, 1, 1)
+        eO(1, 5, "S")
+        K(1, 0, 0, 0, 2)
+        q("W", 1, 3)
+        K(0, 0, 1, 1, 3)
+        i("X", 1, 1, "S")
+        K(1, 0, 1, 1, 2)
+        i("X", 1, 0, "V")
+        K(1, 0, 1, 1, 3)
+        K(1, 0, 0, 0, 3)
+        K(0, 0, 0, 0, 0)
+        K(1, 0, 0, 1, 3)
+        eK(1, 0, 1, 1, "V")
+        K(0, 0, 0, 0, 1)
+        K(1, 0, 1, 0, 3)
+        K(0, 0, 0, 0, 2)
+        q("X", 1, 0)
+        K(0, 0, 0, 0, 3)
+        eK(1, 0, 1, 0, "S")
+        K(0, 0, 0, 1, 3)
+        q("X", 1, 1)
+        K(1, 1, 1, 0, 0)
+        eK(1, 0, 0, 1, "S")
+        K(1, 1, 1, 1, 0)
+        i("X", 1, 2, "V")
+        K(1, 1, 1, 1, 1)
+        K(0, 0, 1, 0, 3)
+        eK(1, 0, 0, 0, "S")
+        K(1, 1, 1, 0, 1)
+        K(1, 1, 0, 0, 0)
+        K(1, 1, 0, 0, 1)
+        eK(0, 0, 1, 0, "S")
+        q("X", 1, 2)
+        K(0, 1, 1, 0, 0)
+        K(0, 1, 1, 0, 1)
+        i("X", 1, 3, "V")
+        eK(0, 0, 0, 0, "S")
+        K(1, 1, 1, 0, 2)
+        K(0, 1, 1, 0, 2)
+        K(0, 1, 1, 1, 0)
+        eK(0, 0, 0, 1, "S")
+        K(0, 1, 1, 1, 1)
+        qO(0, 0)
+        K(0, 1, 0, 0, 0)
+        K(0, 1, 1, 1, 2)
+        eK(0, 0, 1, 1, "S")
+        K(0, 1, 0, 0, 1)
+        q("X", 1, 3)
+        K(0, 1, 0, 1, 0)
+        K(0, 1, 0, 0, 2)
+        qK(0, 0, 0)
+        K(0, 1, 0, 1, 1)
+        qK(1, 0, 0)
+        K(0, 1, 1, 0, 3)
+        qK(1, 0, 1)
+        K(0, 1, 0, 0, 3)
+        eK(0, 1, 1, 0, "S")
+        qO(0, 1)
+        dT()
+        K(1, 1, 1, 0, 3)
+        K(1, 1, 0, 0, 2)
+        eK(0, 1, 0, 0, "V")
+        K(0, 1, 0, 1, 2)
+        eK(1, 1, 1, 0, "S")
+        K(1, 1, 0, 1, 0)
+        K(0, 1, 1, 1, 3)
+        qK(0, 0, 1)
+        K(1, 1, 0, 0, 3)
+        eK(0, 1, 1, 1, "S")
+        qO(1, 0)
+        K(1, 1, 1, 1, 2)
+        K(1, 1, 1, 1, 3)
+        qK(0, 1, 0)
+        K(0, 1, 0, 1, 3)
+        eK(1, 1, 0, 0, "S")
+        K(1, 1, 0, 1, 1)
+        dN()
+        qO(1, 1)
+        K(1, 1, 0, 1, 2)
+        G(0, 2)
+        eK(0, 1, 0, 1, "S")
+        qK(1, 1, 0)
+        G(2, 5)
+        eK(1, 1, 1, 1, "S")
+        eG(0, 2, "V")
+        K(1, 1, 0, 1, 3)
+        G(1, 5)
+        eK(1, 1, 0, 1, "S")
+        G(1, 4)
+        qK(1, 1, 1)
+        qK(0, 1, 1)
+        eG(1, 5, "V")
+        G(1, 7)
+        eG(1, 4, "S")
+        eG(2, 5, "V")
+        G(1, 6)
+        eG(1, 7, "V")
+        G(2, 7)
+        eG(1, 6, "V")
+        Tr(0, 3)
+        eG(2, 7, "V")
+        Tr(0, 1)
+        eT(0, 3, "V")
+        G(2, 6)
+        eT(0, 1, "S")
+        Tr(0, 2)
+        eG(2, 6, "V")
+        Tr(0, 0)
+        eT(0, 2, "S")
+        G(0, 3)
+        eT(0, 0, "V")
+        Tr(1, 6)
+        eG(0, 3, "V")
+        Tr(1, 5)
+        eT(1, 6, "S")
+        G(0, 1)
+        eT(1, 5, "V")
+        Tr(2, 1)
+        eG(0, 1, "V")
+        Tr(1, 4)
+        eT(2, 1, "S")
+        Tr(2, 2)
+        eT(1, 4, "V")
+        Tr(2, 0)
+        eT(2, 2, "S")
+        G(2, 4)
+        eT(2, 0, "V")
+        G(0, 0)
+        eG(2, 4, "V")
+        eG(0, 0, "V")

@@ -15,13 +15,18 @@ FP4X4 = mybir.dt.float4_e2m1fn_x4
 ALU = mybir.AluOpType
 
 P = 128
+HALVES = 2
+SLOTS = 4
+CHUNKS = 4
+STAGES = 4
+W = 256
 
 
 def tile_concord_precision_gradient_s12_kernel(tc, a_words, a_scales, b_words, b_scales, xw, x, d, out):
     nc = tc.nc
     with ExitStack() as ctx:
         keep = ctx.enter_context(tc.tile_pool(name="keep", bufs=1))
-        work = ctx.enter_context(tc.tile_pool(name="work", bufs=5))
+        work = ctx.enter_context(tc.tile_pool(name="work", bufs=4))
         psum = ctx.enter_context(tc.psum_pool(name="psum", bufs=8))
         ctx.enter_context(tc.manual_schedule())
 
@@ -39,419 +44,330 @@ def tile_concord_precision_gradient_s12_kernel(tc, a_words, a_scales, b_words, b
             else:
                 nc.vector.tensor_copy(out=dst, in_=src)
 
-        a_codes = [kt("a_codes%d" % h, [P, 2, 1024], U8) for h in range(2)]
+        a_codes = [kt("a_codes%d" % q, [P, 2, 1024], U8) for q in range(2)]
         a_sc = kt("a_sc", [P, 2, 1024], U8)
-        b_raw = [kt("b_raw%d" % h, [P, 2, 1024], U8) for h in range(2)]
-        b_codes = [kt("b_codes%d" % h, [P, 2, 1024], U8) for h in range(2)]
-        b_scr = kt("b_scr", [P, 2, 1024], U8)
+        b_raw = [kt("b_raw%d" % h, [P, 2, 1024], U8) for h in range(HALVES)]
+        b_codes = [kt("b_codes%d" % h, [P, 2, 1024], U8) for h in range(HALVES)]
+        b_sc_raw = kt("b_sc_raw", [P, 2, 1024], U8)
         b_sc = kt("b_sc", [P, 2, 1024], U8)
-        w_rawf = {c: kt("w_raw%d" % c, [P, 4, 1024], BF16) for c in range(1, 4)}
-        w_raw = {(h, 0): kt("w_raw0%d" % h, [P, 4, 512], BF16) for h in range(2)}
-        x_raw = {(h, c): kt("x_raw%d%d" % (h, c), [P, 4, 512], BF16) for c in range(4) for h in range(2)}
-        w_codes = {(h, c): kt("w_codes%d%d" % (h, c), [P, 512], U32) for h in range(2) for c in range(4)}
-        w_sc = {(h, c): kt("w_sc%d%d" % (h, c), [P, 512], U8) for h in range(2) for c in range(4)}
-        x_codes = {(h, c): kt("x_codes%d%d" % (h, c), [P, 512], U32) for h in range(2) for c in range(4)}
-        x_sc = {(h, c): kt("x_sc%d%d" % (h, c), [P, 512], U8) for h in range(2) for c in range(4)}
-        o_codes = kt("o_codes", [P, 2, 1024], U32)
-        o_sc = kt("o_sc", [P, 2, 1024], U8)
-        c_codes = kt("c_codes", [P, 2, 1024], U32)
-        c_sc = kt("c_sc", [P, 2, 1024], U8)
-        og = {(h, q): kt("og%d%d" % (h, q), [P, 512, 4], BF16) for h in range(2) for q in range(2)}
-        kg = {(h, l): kt("kg%d%d" % (h, l), [P, 512, 4], BF16) for h in range(2) for l in range(2)}
-        gs = {(0, b): kt("gs0%d" % b, [P, 128 * (b + 1)], F32) for b in range(4)}
-        for b in range(4, 8):
-            gs[1, b] = kt("gs1%d" % b, [P, 512], F32)
-            gs[2, b] = kt("gs2%d" % b, [P, 128 * (b - 3)], F32)
-        ut = {(0, a): kt("ut0%d" % a, [P, 512], F32) for a in range(4)}
-        for a in range(3):
-            ut[2, a] = kt("ut2%d" % a, [P, 128 * (3 - a)], F32)
-        for a in range(4, 7):
-            ut[1, a] = kt("ut1%d" % a, [P, 128 * (7 - a)], F32)
-        identx = kt("identx", [P, 512], F32)
-        ident = identx[:, 384:512]
-        d_row = kt("d_row", [P, 128], BF16)
-        d_f32 = kt("d_f32", [P, 128], F32)
+        w_first = [kt("w_first%d" % h, [P, SLOTS, 512], BF16) for h in range(HALVES)]
+        w_raw = {c: kt("w_raw%d" % c, [P, SLOTS, 1024], BF16) for c in range(1, CHUNKS)}
+        x_raw = {(s, c): kt("x_raw%d%d" % (s, c), [P, SLOTS, W], BF16) for s in range(STAGES) for c in range(CHUNKS)}
+        w_codes = {(h, c): kt("w_codes%d%d" % (h, c), [P, 512], U32) for h in range(HALVES) for c in range(CHUNKS)}
+        w_sc = {(h, c): kt("w_sc%d%d" % (h, c), [P, 512], U8) for h in range(HALVES) for c in range(CHUNKS)}
+        x_codes = {(s, c): kt("x_codes%d%d" % (s, c), [P, W], U32) for s in range(STAGES) for c in range(CHUNKS)}
+        x_sc = {(s, c): kt("x_sc%d%d" % (s, c), [P, W], U8) for s in range(STAGES) for c in range(CHUNKS)}
+        o_codes = [kt("o_codes%d" % h, [P, 1024], U32) for h in range(HALVES)]
+        o_sc = [kt("o_sc%d" % h, [P, 1024], U8) for h in range(HALVES)]
+        c_codes = [kt("c_codes%d" % h, [P, 1024], U32) for h in range(HALVES)]
+        c_sc = [kt("c_sc%d" % h, [P, 1024], U8) for h in range(HALVES)]
+        o_grp = {(h, s): kt("o_grp%d%d" % (h, s), [P, W, SLOTS], BF16) for h in range(HALVES) for s in range(STAGES)}
+        c_grp = {(h, s): kt("c_grp%d%d" % (h, s), [P, W, SLOTS], BF16) for h in range(HALVES) for s in range(STAGES)}
+        ident_wide = kt("ident_wide", [P, 3 * P], F32)
+        ident = ident_wide[:, P : 2 * P]
+        d_rows = kt("d_rows", [P, 256], BF16)
+        d_turned = kt("d_turned", [P, 256], BF16)
         d_rec = kt("d_rec", [P, 8], F32)
         d_neg = kt("d_neg", [P, 8], F32)
         grp = {}
         ps = {}
+        g_sb = {}
 
-        nc.vector.memset(b_scr[:].bitcast(I32), 0)
-        nc.vector.memset(a_sc[:].bitcast(I32), 0)
+        def load_codes(eng, dst, src, h):
+            eng.dma_start(out=dst[:].bitcast(I32), in_=src[:, :, h * 1024 : (h + 1) * 1024].bitcast(I32).rearrange("g p n -> p g n"))
 
-        def load_b(h):
-            nc.sync.dma_start(out=b_raw[h][:].bitcast(I32), in_=b_words[:, :, h * 1024 : (h + 1) * 1024].bitcast(I32).rearrange("g p n -> p g n"))
-
-        def load_a(q):
-            nc.sync.dma_start(out=a_codes[q][:].bitcast(I32), in_=a_words[:, :, q * 1024 : (q + 1) * 1024].bitcast(I32).rearrange("g p n -> p g n"))
-
-        def load_sc(eng, dst, src):
+        def load_scales(dst, src):
             for q in range(4):
-                eng.dma_start(out=dst[32 * q : 32 * q + 4, :, :].bitcast(I32), in_=src[:, 4 * q : 4 * q + 4, :].bitcast(I32).rearrange("g q n -> q g n"))
+                nc.sync.dma_start(out=dst[32 * q : 32 * q + 4, :, :].bitcast(I32), in_=src[:, 4 * q : 4 * q + 4, :].bitcast(I32).rearrange("g q n -> q g n"))
 
-        def load_w(c):
-            nc.sync.dma_start(out=w_rawf[c][:], in_=xw[c * 512 : (c + 1) * 512, :].rearrange("(p j) w -> p j w", j=4))
+        def load_rows(dst, src, c, lo, n):
+            nc.sync.dma_start(out=dst[:], in_=src[c * 512 : (c + 1) * 512, lo : lo + n].rearrange("(p j) w -> p j w", j=SLOTS))
 
-        def load_k(dst, src, h, c):
-            nc.sync.dma_start(out=dst[h, c][:], in_=src[c * 512 : (c + 1) * 512, h * 512 : (h + 1) * 512].rearrange("(p j) w -> p j w", j=4))
-
-        load_a(0)
-        load_sc(nc.sync, a_sc, a_scales)
-        load_sc(nc.sync, b_scr, b_scales)
-        load_b(0)
-        load_k(x_raw, x, 0, 0)
-        load_w(2)
-        load_b(1)
-        load_w(1)
-        load_a(1)
-        load_k(w_raw, xw, 0, 0)
-        load_k(w_raw, xw, 1, 0)
-        load_k(x_raw, x, 0, 1)
-        load_k(x_raw, x, 0, 3)
-        load_k(x_raw, x, 0, 2)
-        load_w(3)
-        load_k(x_raw, x, 1, 0)
-        load_k(x_raw, x, 1, 2)
-        load_k(x_raw, x, 1, 1)
-        load_k(x_raw, x, 1, 3)
-        nc.gpsimd.memset(d_row[:], 0.0)
-        nc.gpsimd.dma_start(out=d_row[0:8, :], in_=d.rearrange("(a p) -> a p", p=128))
-        nc.gpsimd.memset(identx[:], 0.0)
-        make_identity(nc, ident)
-        nc.gpsimd.tensor_copy(out=d_f32[:], in_=d_row[:])
-
-        def pS():
+        def sort_b_scales():
             nc.vector.tensor_copy(
                 out=b_sc[:].bitcast(I32).rearrange("p g (h u s) -> p g h u s", h=2, u=4),
-                in_=b_scr[:].bitcast(I32).rearrange("p g (h s u) -> p g h u s", h=2, u=4),
+                in_=b_sc_raw[:].bitcast(I32).rearrange("p g (h s u) -> p g h u s", h=2, u=4),
             )
 
-        def pB(h):
+        def sort_b_codes(h):
             nc.vector.tensor_copy(
                 out=b_codes[h][:].bitcast(I32).rearrange("p g (u s w) -> p g u s w", u=4, w=2),
                 in_=b_raw[h][:].bitcast(I32).rearrange("p g (s u w) -> p g u s w", u=4, w=2),
             )
 
-        def Om(h, ib):
+        def omega(h, b):
             t = bank()
-            ps["O", h, ib] = t
-            for u in range(4):
+            ps["O", h, b] = t
+            for u in range(SLOTS):
                 for g in range(2):
                     nc.tensor.matmul_mx(
-                        out=t[:, u * 128 : (u + 1) * 128],
+                        out=t[:, u * P : (u + 1) * P],
                         lhsT=b_codes[h][:, g, u * 256 : (u + 1) * 256].bitcast(FP4X4),
-                        lhsT_scale=b_sc[:, g, h * 512 + u * 128 : h * 512 + (u + 1) * 128],
-                        rhs=a_codes[ib // 4][:, g, (ib % 4) * 256 : (ib % 4 + 1) * 256].bitcast(FP4X4),
-                        rhs_scale=a_sc[:, g, ib * 128 : (ib + 1) * 128],
+                        lhsT_scale=b_sc[:, g, h * 512 + u * P : h * 512 + (u + 1) * P],
+                        rhs=a_codes[b // 4][:, g, (b % 4) * 256 : (b % 4 + 1) * 256].bitcast(FP4X4),
+                        rhs_scale=a_sc[:, g, b * P : (b + 1) * P],
                         start=(g == 0),
                         stop=(g == 1),
                     )
 
-        def eO(h, ib, E):
-            n0 = (ib % 4) * 128
-            copy(E, og[h, ib // 4][:, n0 : n0 + 128, :], ps["O", h, ib][:].rearrange("p (u n) -> p n u", u=4))
+        def omega_out(h, b, eng):
+            lo = (b % 2) * P
+            copy(eng, o_grp[h, b // 2][:, lo : lo + P, :], ps["O", h, b][:].rearrange("p (u n) -> p n u", u=SLOTS))
 
-        def qO(h, q):
-            nc.vector.quantize_mx(out=o_codes[:, h, q * 512 : (q + 1) * 512].bitcast(FP8X4), scales=o_sc[:, h, q * 512 : (q + 1) * 512], in_=og[h, q][:].rearrange("p n t -> p (n t)"))
+        def omega_quant(h, s):
+            nc.vector.quantize_mx(out=o_codes[h][:, s * W : (s + 1) * W].bitcast(FP8X4), scales=o_sc[h][:, s * W : (s + 1) * W], in_=o_grp[h, s][:].rearrange("p n t -> p (n t)"))
 
-        def i(k, h, c, E):
-            t = work.tile([P, 2048], BF16, name="grp", tag="grp", align_bytes=64)
-            grp[k, h, c] = t
-            if k == "W":
-                copy(E, t[:].rearrange("p (u s w j) -> p u s j w", u=4, s=32, w=4), (w_rawf[c][:, :, h * 512 : (h + 1) * 512] if c else w_raw[h, 0][:]).rearrange("p j (s u w) -> p u s j w", u=4, w=4))
-            else:
-                copy(E, t[:].rearrange("p (a w j) -> p a j w", w=4, j=4), x_raw[h, c][:].rearrange("p j (a w) -> p a j w", w=4))
+        def w_weave(h, c, eng):
+            t = work.tile([P, 2048], BF16, name="w_grp", tag="w_grp", align_bytes=64)
+            grp["W", h, c] = t
+            src = w_raw[c][:, :, h * 512 : (h + 1) * 512] if c else w_first[h][:]
+            copy(eng, t[:].rearrange("p (u s w j) -> p u s j w", u=4, s=32, w=4), src.rearrange("p j (s u w) -> p u s j w", u=4, w=4))
 
-        def q(k, h, c):
-            co, sc = (w_codes, w_sc) if k == "W" else (x_codes, x_sc)
-            nc.vector.quantize_mx(out=co[h, c][:].bitcast(FP8X4), scales=sc[h, c][:], in_=grp[k, h, c][:])
+        def w_quant(h, c):
+            nc.vector.quantize_mx(out=w_codes[h, c][:].bitcast(FP8X4), scales=w_sc[h, c][:], in_=grp["W", h, c][:])
 
-        def K(h, l, p, f, c):
-            if c == 0:
-                ps["K", h, l, p, f] = bank()
-            t = ps["K", h, l, p, f]
-            for e in range(2):
-                u = 2 * p + e
-                nc.tensor.matmul_mx(
-                    out=t[:, e * 256 : (e + 1) * 256],
-                    lhsT=w_codes[h, c][:, u * 128 : (u + 1) * 128].bitcast(FP8X4),
-                    lhsT_scale=w_sc[h, c][:, u * 128 : (u + 1) * 128],
-                    rhs=x_codes[l, c][:, f * 256 : (f + 1) * 256].bitcast(FP8X4),
-                    rhs_scale=x_sc[l, c][:, f * 256 : (f + 1) * 256],
-                    start=(c == 0 and e == 0),
-                    stop=(c == 3 and e == 1),
-                )
+        def x_weave(s, c, eng):
+            t = work.tile([P, SLOTS * W], BF16, name="x_grp", tag="x_grp", align_bytes=64)
+            grp["X", s, c] = t
+            copy(eng, t[:].rearrange("p (a w j) -> p a j w", w=4, j=4), x_raw[s, c][:].rearrange("p j (a w) -> p a j w", w=4))
 
-        def eK(h, l, p, f, E):
-            copy(E, kg[h, l][:, f * 256 : (f + 1) * 256, 2 * p : 2 * p + 2], ps["K", h, l, p, f][:].rearrange("p (u n) -> p n u", u=2))
+        def x_quant(s, c):
+            nc.vector.quantize_mx(out=x_codes[s, c][:].bitcast(FP8X4), scales=x_sc[s, c][:], in_=grp["X", s, c][:])
 
-        def qK(h, l, f):
-            lo = l * 512 + f * 256
-            nc.vector.quantize_mx(out=c_codes[:, h, lo : lo + 256].bitcast(FP8X4), scales=c_sc[:, h, lo : lo + 256], in_=kg[h, l][:, f * 256 : (f + 1) * 256, :].rearrange("p n t -> p (n t)"))
-
-        def span(p, b):
-            return (512, 128 * (b - 3)) if p == 2 else (0, 512) if p == 1 else (0, 128 * (b + 1))
-
-        def G(p, b):
-            t = bank()
-            ps["G", p, b] = t
-            lo, n = span(p, b)
-            bs = slice(b * 128, (b + 1) * 128)
-            for o, w in ([(0, 256), (256, 128)] if n == 384 else [(0, n)]):
-                ns = slice(lo + o, lo + o + w)
-                step = 0
-                for h in range(2):
-                    for lc, ls, rc, rs in ((o_codes, o_sc, c_codes, c_sc), (c_codes, c_sc, o_codes, o_sc)):
+        def cov(s, chunks, halves):
+            for h, pair in [(h, pair) for h in halves for pair in range(2)]:
+                for c in chunks:
+                    if c == 0:
+                        ps["C", s, h, pair] = bank()
+                    t = ps["C", s, h, pair]
+                    for e in range(2):
+                        u = 2 * pair + e
                         nc.tensor.matmul_mx(
-                            out=t[:, o : o + w],
-                            lhsT=lc[:, h, bs].bitcast(FP8X4),
-                            lhsT_scale=ls[:, h, bs],
-                            rhs=rc[:, h, ns].bitcast(FP8X4),
-                            rhs_scale=rs[:, h, ns],
-                            start=(step == 0),
-                            stop=(step == 3),
+                            out=t[:, e * W : (e + 1) * W],
+                            lhsT=w_codes[h, c][:, u * P : (u + 1) * P].bitcast(FP8X4),
+                            lhsT_scale=w_sc[h, c][:, u * P : (u + 1) * P],
+                            rhs=x_codes[s, c][:].bitcast(FP8X4),
+                            rhs_scale=x_sc[s, c][:],
+                            start=(c == 0 and e == 0),
+                            stop=(c == CHUNKS - 1 and e == 1),
                         )
-                        step += 1
 
-        def eG(p, b, E):
-            lo, n = span(p, b)
-            t = ps["G", p, b]
-            g = gs[p, b]
-            if p == 1:
-                copy(E, g[:], t[:])
-            else:
-                z = 384 - (b * 128 - lo)
-                nc.vector.scalar_tensor_tensor(out=g[:], in0=identx[:, z : z + n], scalar=d_neg[:, b : b + 1], in1=t[:, 0:n], op0=ALU.mult, op1=ALU.add)
-            nc.sync.dma_start(out=out[b * 128 : (b + 1) * 128, lo : lo + n], in_=g[:])
+        def cov_out(s, h, pair, eng):
+            copy(eng, c_grp[h, s][:, :, 2 * pair : 2 * pair + 2], ps["C", s, h, pair][:].rearrange("p (u n) -> p n u", u=2))
 
-        def tr_strips(p, a):
-            return range(4, 8) if p == 0 else range(a + 1, 8) if p == 1 else range(a + 1, 4)
+        def cov_quant(s, h):
+            nc.vector.quantize_mx(out=c_codes[h][:, s * W : (s + 1) * W].bitcast(FP8X4), scales=c_sc[h][:, s * W : (s + 1) * W], in_=c_grp[h, s][:].rearrange("p n t -> p (n t)"))
 
-        def Tr(p, a):
+        def grad(dst, b, lo, n):
+            rows = slice(b * P, (b + 1) * P)
+            cols = slice(lo, lo + n)
+            step = 0
+            for h in range(HALVES):
+                for lc, ls, rc, rs in ((o_codes, o_sc, c_codes, c_sc), (c_codes, c_sc, o_codes, o_sc)):
+                    nc.tensor.matmul_mx(
+                        out=dst,
+                        lhsT=lc[h][:, rows].bitcast(FP8X4),
+                        lhsT_scale=ls[h][:, rows],
+                        rhs=rc[h][:, cols].bitcast(FP8X4),
+                        rhs_scale=rs[h][:, cols],
+                        start=(step == 0),
+                        stop=(step == 3),
+                    )
+                    step += 1
+
+        def wide(b):
             t = bank()
-            ps["T", p, a] = t
-            for m, b in enumerate(tr_strips(p, a)):
-                src = gs[1, b][:, a * 128 : (a + 1) * 128] if p == 0 else gs[0, b][:, a * 128 : (a + 1) * 128] if p == 2 else gs[2, b][:, a * 128 - 512 : a * 128 - 384]
-                nc.tensor.transpose(t[:, m * 128 : (m + 1) * 128], src, ident)
+            ps["wide", b] = t
+            grad(t[:], b, 0, 512)
 
-        def eT(p, a, E):
-            u = ut[p, a]
-            n = 128 * len(tr_strips(p, a))
-            hi = 512 if p == 2 else 1024
-            copy(E, u[:], ps["T", p, a][:, 0:n])
-            nc.sync.dma_start(out=out[a * 128 : (a + 1) * 128, hi - n : hi], in_=u[:])
+        def wide_out(b, eng):
+            g = kt("g_wide%d" % b, [P, 512], F32)
+            g_sb["wide", b] = g
+            copy(eng, g[:], ps["wide", b][:])
+            nc.sync.dma_start(out=out[b * P : (b + 1) * P, 0:512], in_=g[:])
 
-        def dT():
+        def square(s, r):
             t = bank()
-            ps["d"] = t
-            nc.tensor.transpose(t[:, 0:128], d_f32[:], ident)
+            ps["square", s, r] = t
+            for e in range(2):
+                grad(t[:, e * W : (e + 1) * W], 2 * s + e, r * W, W)
 
-        def dN():
-            nc.vector.reciprocal(out=d_rec[:], in_=ps["d"][:, 0:8])
+        def store_square(g, s, r):
+            nc.sync.dma_start(out=out[s * W : (s + 1) * W, r * W : (r + 1) * W].rearrange("(e p) c -> p e c", e=2), in_=g[:].rearrange("p (e c) -> p e c", e=2))
+
+        def square_out(s, r, eng):
+            g = kt("g_square%d%d" % (s, r), [P, 512], F32)
+            g_sb["square", s, r] = g
+            copy(eng, g[:], ps["square", s, r][:])
+            store_square(g, s, r)
+
+        def diag_out(s):
+            g = kt("g_diag%d" % s, [P, 512], F32)
+            for e in range(2):
+                z = P - e * P
+                nc.vector.scalar_tensor_tensor(
+                    out=g[:, e * W : (e + 1) * W],
+                    in0=ident_wide[:, z : z + W],
+                    scalar=d_neg[:, 2 * s + e : 2 * s + e + 1],
+                    in1=ps["square", s, s][:, e * W : (e + 1) * W],
+                    op0=ALU.mult,
+                    op1=ALU.add,
+                )
+            store_square(g, s, s)
+
+        def lower_tile(b, m):
+            s, e = divmod(b, 2)
+            if s >= 2 and m < 4:
+                return g_sb["wide", b][:, m * P : (m + 1) * P]
+            return g_sb["square", s, m // 2][:, e * W + (m % 2) * P : e * W + (m % 2 + 1) * P]
+
+        def mirror(r, s):
+            t = bank()
+            ps["mirror", r, s] = t
+            for e in range(2):
+                for f in range(2):
+                    nc.tensor.transpose(t[:, e * W + f * P : e * W + (f + 1) * P], lower_tile(2 * s + f, 2 * r + e), ident)
+
+        def mirror_out(r, s, eng):
+            g = kt("g_mirror%d%d" % (r, s), [P, 512], F32)
+            copy(eng, g[:], ps["mirror", r, s][:])
+            store_square(g, r, s)
+
+        def diagonal_constants():
+            nc.vector.transpose(out=d_turned[:], in_=d_rows[:])
+            nc.vector.reciprocal(out=d_rec[:], in_=d_turned[:, 0:256:32])
             nc.vector.tensor_scalar(out=d_neg[:], in0=d_rec[:], scalar1=-1.0, scalar2=None, op0=ALU.mult)
 
-        pB(0)
-        pS()
-        Om(0, 2)
-        i("X", 0, 0, "V")
-        Om(0, 3)
-        eO(0, 2, "S")
-        q("X", 0, 0)
-        i("W", 0, 2, "V")
-        i("W", 1, 2, "S")
-        Om(0, 1)
-        Om(0, 0)
-        pB(1)
-        q("W", 0, 2)
-        Om(1, 1)
-        eO(0, 3, "S")
-        Om(1, 3)
-        q("W", 1, 2)
-        eO(1, 1, "S")
-        i("W", 0, 1, "V")
-        Om(1, 2)
-        i("W", 1, 1, "S")
-        Om(1, 5)
-        eO(1, 2, "V")
-        Om(0, 4)
-        q("W", 0, 1)
-        Om(1, 7)
-        i("W", 0, 0, "V")
-        eO(0, 4, "S")
-        Om(1, 6)
-        eO(0, 0, "S")
-        Om(1, 0)
-        q("W", 1, 1)
-        eO(0, 1, "S")
-        Om(1, 4)
-        i("W", 1, 0, "V")
-        eO(1, 0, "S")
-        Om(0, 7)
-        eO(1, 6, "S")
-        q("W", 0, 0)
-        Om(0, 6)
-        eO(1, 4, "S")
-        i("X", 0, 1, "V")
-        eO(1, 3, "S")
-        K(0, 0, 1, 0, 0)
-        K(0, 0, 1, 1, 0)
-        eO(0, 7, "S")
-        Om(0, 5)
-        q("W", 1, 0)
-        i("X", 0, 2, "S")
-        q("X", 0, 1)
-        K(1, 0, 1, 0, 0)
-        K(1, 0, 0, 0, 0)
-        eO(0, 6, "V")
-        K(0, 0, 1, 1, 1)
-        i("X", 0, 3, "V")
-        K(0, 0, 0, 1, 0)
-        K(1, 0, 1, 0, 1)
-        eO(1, 7, "S")
-        K(1, 0, 0, 0, 1)
-        K(0, 0, 0, 1, 1)
-        eO(0, 5, "S")
-        q("X", 0, 2)
-        K(1, 0, 0, 1, 0)
-        K(1, 0, 0, 1, 1)
-        i("W", 1, 3, "S")
-        i("W", 0, 3, "V")
-        K(1, 0, 1, 0, 2)
-        K(0, 0, 1, 1, 2)
-        K(0, 0, 1, 0, 1)
-        K(1, 0, 1, 1, 0)
-        q("X", 0, 3)
-        K(1, 0, 0, 1, 2)
-        K(0, 0, 1, 0, 2)
-        K(0, 0, 0, 1, 2)
-        q("W", 0, 3)
-        K(1, 0, 1, 1, 1)
-        eO(1, 5, "S")
-        K(1, 0, 0, 0, 2)
-        q("W", 1, 3)
-        K(0, 0, 1, 1, 3)
-        i("X", 1, 1, "S")
-        K(1, 0, 1, 1, 2)
-        i("X", 1, 0, "V")
-        K(1, 0, 1, 1, 3)
-        K(1, 0, 0, 0, 3)
-        K(0, 0, 0, 0, 0)
-        K(1, 0, 0, 1, 3)
-        eK(1, 0, 1, 1, "V")
-        K(0, 0, 0, 0, 1)
-        K(1, 0, 1, 0, 3)
-        K(0, 0, 0, 0, 2)
-        q("X", 1, 0)
-        K(0, 0, 0, 0, 3)
-        eK(1, 0, 1, 0, "S")
-        K(0, 0, 0, 1, 3)
-        q("X", 1, 1)
-        K(1, 1, 1, 0, 0)
-        eK(1, 0, 0, 1, "S")
-        K(1, 1, 1, 1, 0)
-        i("X", 1, 2, "V")
-        K(1, 1, 1, 1, 1)
-        K(0, 0, 1, 0, 3)
-        eK(1, 0, 0, 0, "S")
-        K(1, 1, 1, 0, 1)
-        K(1, 1, 0, 0, 0)
-        K(1, 1, 0, 0, 1)
-        eK(0, 0, 1, 0, "S")
-        q("X", 1, 2)
-        K(0, 1, 1, 0, 0)
-        K(0, 1, 1, 0, 1)
-        i("X", 1, 3, "V")
-        eK(0, 0, 0, 0, "S")
-        K(1, 1, 1, 0, 2)
-        K(0, 1, 1, 0, 2)
-        K(0, 1, 1, 1, 0)
-        eK(0, 0, 0, 1, "S")
-        K(0, 1, 1, 1, 1)
-        qO(0, 0)
-        K(0, 1, 0, 0, 0)
-        K(0, 1, 1, 1, 2)
-        eK(0, 0, 1, 1, "S")
-        K(0, 1, 0, 0, 1)
-        q("X", 1, 3)
-        K(0, 1, 0, 1, 0)
-        K(0, 1, 0, 0, 2)
-        qK(0, 0, 0)
-        K(0, 1, 0, 1, 1)
-        qK(1, 0, 0)
-        K(0, 1, 1, 0, 3)
-        qK(1, 0, 1)
-        K(0, 1, 0, 0, 3)
-        eK(0, 1, 1, 0, "S")
-        qO(0, 1)
-        dT()
-        K(1, 1, 1, 0, 3)
-        K(1, 1, 0, 0, 2)
-        eK(0, 1, 0, 0, "V")
-        K(0, 1, 0, 1, 2)
-        eK(1, 1, 1, 0, "S")
-        K(1, 1, 0, 1, 0)
-        K(0, 1, 1, 1, 3)
-        qK(0, 0, 1)
-        K(1, 1, 0, 0, 3)
-        eK(0, 1, 1, 1, "S")
-        qO(1, 0)
-        K(1, 1, 1, 1, 2)
-        K(1, 1, 1, 1, 3)
-        qK(0, 1, 0)
-        K(0, 1, 0, 1, 3)
-        eK(1, 1, 0, 0, "S")
-        K(1, 1, 0, 1, 1)
-        dN()
-        qO(1, 1)
-        K(1, 1, 0, 1, 2)
-        G(0, 2)
-        eK(0, 1, 0, 1, "S")
-        qK(1, 1, 0)
-        G(2, 5)
-        eK(1, 1, 1, 1, "S")
-        eG(0, 2, "V")
-        K(1, 1, 0, 1, 3)
-        G(1, 5)
-        eK(1, 1, 0, 1, "S")
-        G(1, 4)
-        qK(1, 1, 1)
-        qK(0, 1, 1)
-        eG(1, 5, "V")
-        G(1, 7)
-        eG(1, 4, "S")
-        eG(2, 5, "V")
-        G(1, 6)
-        eG(1, 7, "V")
-        G(2, 7)
-        eG(1, 6, "V")
-        Tr(0, 3)
-        eG(2, 7, "V")
-        Tr(0, 1)
-        eT(0, 3, "V")
-        G(2, 6)
-        eT(0, 1, "S")
-        Tr(0, 2)
-        eG(2, 6, "V")
-        Tr(0, 0)
-        eT(0, 2, "S")
-        G(0, 3)
-        eT(0, 0, "V")
-        Tr(1, 6)
-        eG(0, 3, "V")
-        Tr(1, 5)
-        eT(1, 6, "S")
-        G(0, 1)
-        eT(1, 5, "V")
-        Tr(2, 1)
-        eG(0, 1, "V")
-        Tr(1, 4)
-        eT(2, 1, "S")
-        Tr(2, 2)
-        eT(1, 4, "V")
-        Tr(2, 0)
-        eT(2, 2, "S")
-        G(2, 4)
-        eT(2, 0, "V")
-        G(0, 0)
-        eG(2, 4, "V")
-        eG(0, 0, "V")
+        nc.vector.memset(b_sc_raw[:].bitcast(I32), 0)
+        nc.vector.memset(a_sc[:].bitcast(I32), 0)
+        nc.gpsimd.memset(d_rows[:], 0.0)
+        nc.gpsimd.dma_start(out=d_rows[0:P:32, :].rearrange("q (b a) -> q b a", a=32), in_=d.rearrange("(b q a) -> q b a", q=4, a=32))
+        nc.gpsimd.memset(ident_wide[:], 0.0)
+        make_identity(nc, ident, nomemset=True)
+
+        load_codes(nc.sync, b_raw[0], b_words, 0)
+        load_scales(b_sc_raw, b_scales)
+        load_scales(a_sc, a_scales)
+        load_codes(nc.sync, a_codes[0], a_words, 0)
+        for h in range(HALVES):
+            load_rows(w_first[h], xw, 0, h * 512, 512)
+        load_codes(nc.sync, a_codes[1], a_words, 1)
+        load_rows(x_raw[0, 0], x, 0, 0, W)
+        load_codes(nc.sync, b_raw[1], b_words, 1)
+        for c in range(1, CHUNKS):
+            load_rows(w_raw[c], xw, c, 0, 1024)
+            load_rows(x_raw[0, c], x, c, 0, W)
+            load_rows(x_raw[1, c - 1], x, c - 1, W, W)
+        load_rows(x_raw[1, CHUNKS - 1], x, CHUNKS - 1, W, W)
+        for s in range(2, STAGES):
+            for c in range(CHUNKS):
+                load_rows(x_raw[s, c], x, c, s * W, W)
+
+        last = CHUNKS - 1
+        sort_b_codes(0)
+        sort_b_scales()
+        diagonal_constants()
+        for c in range(CHUNKS):
+            h, lo = divmod(4 * c, 8)
+            for b in range(lo, lo + 4):
+                omega(h, b)
+                omega_out(h, b, "S")
+            w_weave(0, c, "V")
+            if c < last:
+                x_weave(0, c, "S")
+                w_weave(1, c, "V")
+            else:
+                w_weave(1, c, "S")
+                x_weave(0, c, "V")
+            w_quant(0, c)
+            if c == 0:
+                sort_b_codes(1)
+            else:
+                x_weave(1, c - 1, "V" if c < last else "S")
+            if c < last:
+                w_quant(1, c)
+                x_quant(0, c)
+            else:
+                x_quant(0, c)
+                w_quant(1, c)
+            if c:
+                x_quant(1, c - 1)
+        x_weave(1, last, "S")
+        x_weave(2, 0, "V")
+        x_quant(1, last)
+
+        for c in range(CHUNKS + 1):
+            if c < CHUNKS:
+                cov(0, [c], range(HALVES))
+            if c:
+                cov(1, [c - 1], range(HALVES))
+
+        def cov_leave(s, engines):
+            for h in range(HALVES):
+                for pair in range(2):
+                    cov_out(s, h, pair, engines[h])
+
+        def supply(s, first):
+            for c in range(first, CHUNKS):
+                x_weave(s, c, "V")
+                if c:
+                    x_quant(s, c - 1)
+            x_quant(s, last)
+
+        cov_leave(0, "SS")
+        cov_leave(1, "SS")
+        supply(2, 1)
+        for c in range(CHUNKS):
+            cov(2, [c], range(HALVES))
+        for s in range(2):
+            for h in range(HALVES):
+                omega_quant(h, s)
+            for h in range(HALVES):
+                cov_quant(s, h)
+        square(0, 0)
+        square(1, 0)
+        square(1, 1)
+        x_weave(3, 0, "V")
+        x_weave(3, 1, "V")
+        x_quant(3, 0)
+        diag_out(0)
+        x_weave(3, 2, "V")
+        x_quant(3, 1)
+        square_out(1, 0, "V")
+        mirror(0, 1)
+        cov_leave(2, "SS")
+        x_weave(3, 3, "S")
+        x_quant(3, 2)
+        diag_out(1)
+        x_quant(3, 3)
+        mirror_out(0, 1, "S")
+        for h in range(HALVES):
+            cov(3, range(CHUNKS), [h])
+        for h in range(HALVES):
+            omega_quant(h, 2)
+        for h in range(HALVES):
+            cov_quant(2, h)
+        for h in range(HALVES):
+            omega_quant(h, 3)
+        cov_leave(3, "SS")
+        cov_quant(3, 0)
+        wide(4)
+        wide_out(4, "V")
+        cov_quant(3, 1)
+        wide(5)
+        wide_out(5, "S")
+        square(2, 2)
+        diag_out(2)
+        for r in range(2):
+            mirror(r, 2)
+            mirror_out(r, 2, "SV"[r])
+        for e in range(2):
+            wide(6 + e)
+            wide_out(6 + e, "SV"[e])
+        square(3, 2)
+        square_out(3, 2, "S")
+        for r in range(3):
+            mirror(r, 3)
+            mirror_out(r, 3, "VSV"[r])
+        square(3, 3)
+        diag_out(3)

@@ -20,6 +20,8 @@ SLOTS = 4
 CHUNKS = 4
 STAGES = 4
 W = 256
+NARROW_STAGES = 0
+LAG = 1
 
 
 def tile_concord_precision_gradient_s12_kernel(tc, a_words, a_scales, b_words, b_scales, xw, x, d, out):
@@ -46,7 +48,7 @@ def tile_concord_precision_gradient_s12_kernel(tc, a_words, a_scales, b_words, b
 
         a_codes = [kt("a_codes%d" % q, [P, 2, 1024], U8) for q in range(2)]
         a_sc = kt("a_sc", [P, 2, 1024], U8)
-        b_raw = [kt("b_raw%d" % h, [P, 2, 1024], U8) for h in range(HALVES)]
+        b_raw = kt("b_raw", [P, 2, 2048], U8)
         b_codes = [kt("b_codes%d" % h, [P, 2, 1024], U8) for h in range(HALVES)]
         b_sc_raw = kt("b_sc_raw", [P, 2, 1024], U8)
         b_sc = kt("b_sc", [P, 2, 1024], U8)
@@ -76,9 +78,9 @@ def tile_concord_precision_gradient_s12_kernel(tc, a_words, a_scales, b_words, b
         def load_codes(eng, dst, src, h):
             eng.dma_start(out=dst[:].bitcast(I32), in_=src[:, :, h * 1024 : (h + 1) * 1024].bitcast(I32).rearrange("g p n -> p g n"))
 
-        def load_scales(dst, src):
-            for q in range(4):
-                nc.sync.dma_start(out=dst[32 * q : 32 * q + 4, :, :].bitcast(I32), in_=src[:, 4 * q : 4 * q + 4, :].bitcast(I32).rearrange("g q n -> q g n"))
+        def load_scales(eng, dst, src, quadrants):
+            for q in quadrants:
+                eng.dma_start(out=dst[32 * q : 32 * q + 4, :, :].bitcast(I32), in_=src[:, 4 * q : 4 * q + 4, :].bitcast(I32).rearrange("g q n -> q g n"))
 
         def load_rows(dst, src, c, lo, n):
             nc.sync.dma_start(out=dst[:], in_=src[c * 512 : (c + 1) * 512, lo : lo + n].rearrange("(p j) w -> p j w", j=SLOTS))
@@ -92,7 +94,7 @@ def tile_concord_precision_gradient_s12_kernel(tc, a_words, a_scales, b_words, b
         def sort_b_codes(h):
             nc.vector.tensor_copy(
                 out=b_codes[h][:].bitcast(I32).rearrange("p g (u s w) -> p g u s w", u=4, w=2),
-                in_=b_raw[h][:].bitcast(I32).rearrange("p g (s u w) -> p g u s w", u=4, w=2),
+                in_=b_raw[:, :, h * 1024 : (h + 1) * 1024].bitcast(I32).rearrange("p g (s u w) -> p g u s w", u=4, w=2),
             )
 
         def omega(h, b):
@@ -135,25 +137,30 @@ def tile_concord_precision_gradient_s12_kernel(tc, a_words, a_scales, b_words, b
             nc.vector.quantize_mx(out=x_codes[s, c][:].bitcast(FP8X4), scales=x_sc[s, c][:], in_=grp["X", s, c][:])
 
         def cov(s, chunks, halves):
-            for h, pair in [(h, pair) for h in halves for pair in range(2)]:
+            n = P if s < NARROW_STAGES else W
+            sums = 512 // n
+            for h, k in [(h, k) for h in halves for k in range(2)]:
                 for c in chunks:
                     if c == 0:
-                        ps["C", s, h, pair] = bank()
-                    t = ps["C", s, h, pair]
-                    for e in range(2):
-                        u = 2 * pair + e
+                        ps["C", s, h, k] = bank()
+                    t = ps["C", s, h, k]
+                    for e in range(sums):
+                        u, lo = (e, k * P) if n == P else (2 * k + e, 0)
                         nc.tensor.matmul_mx(
-                            out=t[:, e * W : (e + 1) * W],
+                            out=t[:, e * n : (e + 1) * n],
                             lhsT=w_codes[h, c][:, u * P : (u + 1) * P].bitcast(FP8X4),
                             lhsT_scale=w_sc[h, c][:, u * P : (u + 1) * P],
-                            rhs=x_codes[s, c][:].bitcast(FP8X4),
-                            rhs_scale=x_sc[s, c][:],
+                            rhs=x_codes[s, c][:, lo : lo + n].bitcast(FP8X4),
+                            rhs_scale=x_sc[s, c][:, lo : lo + n],
                             start=(c == 0 and e == 0),
-                            stop=(c == CHUNKS - 1 and e == 1),
+                            stop=(c == CHUNKS - 1 and e == sums - 1),
                         )
 
-        def cov_out(s, h, pair, eng):
-            copy(eng, c_grp[h, s][:, :, 2 * pair : 2 * pair + 2], ps["C", s, h, pair][:].rearrange("p (u n) -> p n u", u=2))
+        def cov_out(s, h, k, eng):
+            if s < NARROW_STAGES:
+                copy(eng, c_grp[h, s][:, k * P : (k + 1) * P, :], ps["C", s, h, k][:].rearrange("p (u n) -> p n u", u=SLOTS))
+            else:
+                copy(eng, c_grp[h, s][:, :, 2 * k : 2 * k + 2], ps["C", s, h, k][:].rearrange("p (u n) -> p n u", u=2))
 
         def cov_quant(s, h):
             nc.vector.quantize_mx(out=c_codes[h][:, s * W : (s + 1) * W].bitcast(FP8X4), scales=c_sc[h][:, s * W : (s + 1) * W], in_=c_grp[h, s][:].rearrange("p n t -> p (n t)"))
@@ -162,8 +169,8 @@ def tile_concord_precision_gradient_s12_kernel(tc, a_words, a_scales, b_words, b
             rows = slice(b * P, (b + 1) * P)
             cols = slice(lo, lo + n)
             step = 0
-            for h in range(HALVES):
-                for lc, ls, rc, rs in ((o_codes, o_sc, c_codes, c_sc), (c_codes, c_sc, o_codes, o_sc)):
+            for lc, ls, rc, rs in ((o_codes, o_sc, c_codes, c_sc), (c_codes, c_sc, o_codes, o_sc)):
+                for h in range(HALVES):
                     nc.tensor.matmul_mx(
                         out=dst,
                         lhsT=lc[h][:, rows].bitcast(FP8X4),
@@ -215,6 +222,15 @@ def tile_concord_precision_gradient_s12_kernel(tc, a_words, a_scales, b_words, b
                 )
             store_square(g, s, s)
 
+        def diag_row(b):
+            s, e = divmod(b, 2)
+            t = bank()
+            grad(t[:, 0:W], b, s * W, W)
+            g = kt("g_last%d" % b, [P, W], F32)
+            z = P - e * P
+            nc.vector.scalar_tensor_tensor(out=g[:], in0=ident_wide[:, z : z + W], scalar=d_neg[:, b : b + 1], in1=t[:, 0:W], op0=ALU.mult, op1=ALU.add)
+            nc.sync.dma_start(out=out[b * P : (b + 1) * P, s * W : (s + 1) * W], in_=g[:])
+
         def lower_tile(b, m):
             s, e = divmod(b, 2)
             if s >= 2 and m < 4:
@@ -233,74 +249,88 @@ def tile_concord_precision_gradient_s12_kernel(tc, a_words, a_scales, b_words, b
             copy(eng, g[:], ps["mirror", r, s][:])
             store_square(g, r, s)
 
-        def diagonal_constants():
-            nc.vector.transpose(out=d_turned[:], in_=d_rows[:])
-            nc.vector.reciprocal(out=d_rec[:], in_=d_turned[:, 0:256:32])
-            nc.vector.tensor_scalar(out=d_neg[:], in0=d_rec[:], scalar1=-1.0, scalar2=None, op0=ALU.mult)
-
         nc.vector.memset(b_sc_raw[:].bitcast(I32), 0)
-        nc.vector.memset(a_sc[:].bitcast(I32), 0)
+        nc.gpsimd.memset(a_sc[:].bitcast(I32), 0)
+        load_scales(nc.gpsimd, a_sc, a_scales, range(2))
         nc.gpsimd.memset(d_rows[:], 0.0)
         nc.gpsimd.dma_start(out=d_rows[0:P:32, :].rearrange("q (b a) -> q b a", a=32), in_=d.rearrange("(b q a) -> q b a", q=4, a=32))
         nc.gpsimd.memset(ident_wide[:], 0.0)
         make_identity(nc, ident, nomemset=True)
 
-        load_codes(nc.sync, b_raw[0], b_words, 0)
-        load_scales(b_sc_raw, b_scales)
-        load_scales(a_sc, a_scales)
+        nc.sync.dma_start(out=b_raw[:].bitcast(I32), in_=b_words.bitcast(I32).rearrange("g p n -> p g n"))
+        load_scales(nc.sync, b_sc_raw, b_scales, range(4))
+        load_scales(nc.sync, a_sc, a_scales, range(2, 4))
         load_codes(nc.sync, a_codes[0], a_words, 0)
-        for h in range(HALVES):
-            load_rows(w_first[h], xw, 0, h * 512, 512)
+        load_rows(w_first[0], xw, 0, 0, 512)
+        load_rows(w_first[1], xw, 0, 512, 512)
         load_codes(nc.sync, a_codes[1], a_words, 1)
         load_rows(x_raw[0, 0], x, 0, 0, W)
-        load_codes(nc.sync, b_raw[1], b_words, 1)
-        for c in range(1, CHUNKS):
-            load_rows(w_raw[c], xw, c, 0, 1024)
-            load_rows(x_raw[0, c], x, c, 0, W)
-            load_rows(x_raw[1, c - 1], x, c - 1, W, W)
-        load_rows(x_raw[1, CHUNKS - 1], x, CHUNKS - 1, W, W)
+        for c in range(1, CHUNKS + LAG):
+            if c < CHUNKS:
+                load_rows(w_raw[c], xw, c, 0, 1024)
+                load_rows(x_raw[0, c], x, c, 0, W)
+            if c >= LAG:
+                load_rows(x_raw[1, c - LAG], x, c - LAG, W, W)
         for s in range(2, STAGES):
             for c in range(CHUNKS):
                 load_rows(x_raw[s, c], x, c, s * W, W)
 
         last = CHUNKS - 1
+
+        def omega_run(first, n, eng="S"):
+            for k in range(first, first + n):
+                omega(k // 8, k % 8)
+                omega_out(k // 8, k % 8, eng)
+
         sort_b_codes(0)
         sort_b_scales()
-        diagonal_constants()
-        for c in range(CHUNKS):
-            h, lo = divmod(4 * c, 8)
-            for b in range(lo, lo + 4):
-                omega(h, b)
-                omega_out(h, b, "S")
-            w_weave(0, c, "V")
-            if c < last:
-                x_weave(0, c, "S")
-                w_weave(1, c, "V")
-            else:
-                w_weave(1, c, "S")
-                x_weave(0, c, "V")
-            w_quant(0, c)
-            if c == 0:
-                sort_b_codes(1)
-            else:
-                x_weave(1, c - 1, "V" if c < last else "S")
-            if c < last:
-                w_quant(1, c)
-                x_quant(0, c)
-            else:
-                x_quant(0, c)
-                w_quant(1, c)
-            if c:
-                x_quant(1, c - 1)
-        x_weave(1, last, "S")
+        sort_b_codes(1)
+        w_weave(0, 0, "V")
+        w_weave(1, 0, "V")
+        w_quant(0, 0)
+        nc.vector.transpose(out=d_turned[:], in_=d_rows[:])
+        x_weave(0, 0, "V")
+        w_quant(1, 0)
+        nc.vector.reciprocal(out=d_rec[:], in_=d_turned[:, 0:256:32])
+        x_quant(0, 0)
+        omega_run(0, 6)
+        w_weave(1, 1, "S")
+        w_weave(0, 1, "V")
+        nc.vector.tensor_scalar(out=d_neg[:], in0=d_rec[:], scalar1=-1.0, scalar2=None, op0=ALU.mult)
+        x_weave(0, 1, "V")
+        w_quant(0, 1)
+        omega_run(6, 2)
+        x_weave(1, 0, "S")
+        x_quant(0, 1)
+        w_quant(1, 1)
+        w_weave(0, 2, "V")
+        omega_run(8, 3)
+        x_weave(0, 2, "S")
+        x_quant(1, 0)
+        w_weave(1, 2, "V")
+        w_quant(0, 2)
+        omega_run(11, 5)
+        x_weave(1, 1, "V")
+        w_quant(1, 2)
+        x_quant(0, 2)
+        w_weave(1, 3, "S")
+        w_weave(0, 3, "V")
+        x_quant(1, 1)
+        x_weave(0, 3, "V")
+        w_quant(0, 3)
+        x_weave(1, 2, "V")
+        x_quant(0, 3)
+        w_quant(1, 3)
+        x_weave(1, 3, "S")
         x_weave(2, 0, "V")
-        x_quant(1, last)
+        x_quant(1, 2)
+        x_quant(1, 3)
 
-        for c in range(CHUNKS + 1):
+        for c in range(CHUNKS + LAG):
             if c < CHUNKS:
                 cov(0, [c], range(HALVES))
-            if c:
-                cov(1, [c - 1], range(HALVES))
+            if c >= LAG:
+                cov(1, [c - LAG], range(HALVES))
 
         def cov_leave(s, engines):
             for h in range(HALVES):
@@ -356,18 +386,19 @@ def tile_concord_precision_gradient_s12_kernel(tc, a_words, a_scales, b_words, b
         cov_quant(3, 1)
         wide(5)
         wide_out(5, "S")
-        square(2, 2)
-        diag_out(2)
+        wide(6)
+        wide_out(6, "V")
         for r in range(2):
             mirror(r, 2)
             mirror_out(r, 2, "SV"[r])
-        for e in range(2):
-            wide(6 + e)
-            wide_out(6 + e, "SV"[e])
+        wide(7)
+        wide_out(7, "S")
         square(3, 2)
-        square_out(3, 2, "S")
+        square_out(3, 2, "V")
         for r in range(3):
             mirror(r, 3)
-            mirror_out(r, 3, "VSV"[r])
-        square(3, 3)
-        diag_out(3)
+            mirror_out(r, 3, "SVS"[r])
+        square(2, 2)
+        diag_out(2)
+        for b in range(6, 8):
+            diag_row(b)

@@ -48,13 +48,13 @@ def tile_concord_precision_gradient_s12_kernel(tc, a_words, a_scales, b_words, b
 
         a_codes = [kt("a_codes%d" % q, [P, 2, 1024], U8) for q in range(2)]
         a_sc = kt("a_sc", [P, 2, 1024], U8)
-        b_raw = kt("b_raw", [P, 2, 2048], U8)
+        b_raw = [kt("b_raw%d" % h, [P, 2, 1024], U8) for h in range(HALVES)]
         b_codes = [kt("b_codes%d" % h, [P, 2, 1024], U8) for h in range(HALVES)]
         b_sc_raw = kt("b_sc_raw", [P, 2, 1024], U8)
         b_sc = kt("b_sc", [P, 2, 1024], U8)
-        w_first = [kt("w_first%d" % h, [P, SLOTS, 512], BF16) for h in range(HALVES)]
-        w_raw = {c: kt("w_raw%d" % c, [P, SLOTS, 1024], BF16) for c in range(1, CHUNKS)}
-        x_raw = {(s, c): kt("x_raw%d%d" % (s, c), [P, SLOTS, W], BF16) for s in range(STAGES) for c in range(CHUNKS)}
+        w_raw = {(h, c): kt("w_raw%d%d" % (h, c), [P, SLOTS, 512], BF16) for h in range(HALVES) for c in range(CHUNKS)}
+        x_first = [kt("x_first%d" % c, [P, SLOTS, 2 * W], BF16) for c in range(CHUNKS)]
+        x_raw = {(s, c): kt("x_raw%d%d" % (s, c), [P, SLOTS, W], BF16) for s in range(2, STAGES) for c in range(CHUNKS)}
         w_codes = {(h, c): kt("w_codes%d%d" % (h, c), [P, 512], U32) for h in range(HALVES) for c in range(CHUNKS)}
         w_sc = {(h, c): kt("w_sc%d%d" % (h, c), [P, 512], U8) for h in range(HALVES) for c in range(CHUNKS)}
         x_codes = {(s, c): kt("x_codes%d%d" % (s, c), [P, W], U32) for s in range(STAGES) for c in range(CHUNKS)}
@@ -94,7 +94,7 @@ def tile_concord_precision_gradient_s12_kernel(tc, a_words, a_scales, b_words, b
         def sort_b_codes(h):
             nc.vector.tensor_copy(
                 out=b_codes[h][:].bitcast(I32).rearrange("p g (u s w) -> p g u s w", u=4, w=2),
-                in_=b_raw[:, :, h * 1024 : (h + 1) * 1024].bitcast(I32).rearrange("p g (s u w) -> p g u s w", u=4, w=2),
+                in_=b_raw[h][:].bitcast(I32).rearrange("p g (s u w) -> p g u s w", u=4, w=2),
             )
 
         def omega(h, b):
@@ -122,7 +122,7 @@ def tile_concord_precision_gradient_s12_kernel(tc, a_words, a_scales, b_words, b
         def w_weave(h, c, eng):
             t = work.tile([P, 2048], BF16, name="w_grp", tag="w_grp", align_bytes=64)
             grp["W", h, c] = t
-            src = w_raw[c][:, :, h * 512 : (h + 1) * 512] if c else w_first[h][:]
+            src = w_raw[h, c][:]
             copy(eng, t[:].rearrange("p (u s w j) -> p u s j w", u=4, s=32, w=4), src.rearrange("p j (s u w) -> p u s j w", u=4, w=4))
 
         def w_quant(h, c):
@@ -131,7 +131,8 @@ def tile_concord_precision_gradient_s12_kernel(tc, a_words, a_scales, b_words, b
         def x_weave(s, c, eng):
             t = work.tile([P, SLOTS * W], BF16, name="x_grp", tag="x_grp", align_bytes=64)
             grp["X", s, c] = t
-            copy(eng, t[:].rearrange("p (a w j) -> p a j w", w=4, j=4), x_raw[s, c][:].rearrange("p j (a w) -> p a j w", w=4))
+            src = x_first[c][:, :, s * W : (s + 1) * W] if s < 2 else x_raw[s, c][:]
+            copy(eng, t[:].rearrange("p (a w j) -> p a j w", w=4, j=4), src.rearrange("p j (a w) -> p a j w", w=4))
 
         def x_quant(s, c):
             nc.vector.quantize_mx(out=x_codes[s, c][:].bitcast(FP8X4), scales=x_sc[s, c][:], in_=grp["X", s, c][:])
@@ -250,27 +251,25 @@ def tile_concord_precision_gradient_s12_kernel(tc, a_words, a_scales, b_words, b
             store_square(g, r, s)
 
         nc.vector.memset(b_sc_raw[:].bitcast(I32), 0)
-        nc.gpsimd.memset(a_sc[:].bitcast(I32), 0)
-        load_scales(nc.gpsimd, a_sc, a_scales, range(2))
+        nc.vector.memset(a_sc[:].bitcast(I32), 0)
         nc.gpsimd.memset(d_rows[:], 0.0)
         nc.gpsimd.dma_start(out=d_rows[0:P:32, :].rearrange("q (b a) -> q b a", a=32), in_=d.rearrange("(b q a) -> q b a", q=4, a=32))
         nc.gpsimd.memset(ident_wide[:], 0.0)
         make_identity(nc, ident, nomemset=True)
 
-        nc.sync.dma_start(out=b_raw[:].bitcast(I32), in_=b_words.bitcast(I32).rearrange("g p n -> p g n"))
+        load_codes(nc.sync, b_raw[0], b_words, 0)
         load_scales(nc.sync, b_sc_raw, b_scales, range(4))
-        load_scales(nc.sync, a_sc, a_scales, range(2, 4))
+        load_scales(nc.sync, a_sc, a_scales, range(4))
         load_codes(nc.sync, a_codes[0], a_words, 0)
-        load_rows(w_first[0], xw, 0, 0, 512)
-        load_rows(w_first[1], xw, 0, 512, 512)
-        load_codes(nc.sync, a_codes[1], a_words, 1)
-        load_rows(x_raw[0, 0], x, 0, 0, W)
-        for c in range(1, CHUNKS + LAG):
+        for c in range(CHUNKS + 1):
             if c < CHUNKS:
-                load_rows(w_raw[c], xw, c, 0, 1024)
-                load_rows(x_raw[0, c], x, c, 0, W)
-            if c >= LAG:
-                load_rows(x_raw[1, c - LAG], x, c - LAG, W, W)
+                load_rows(w_raw[0, c], xw, c, 0, 512)
+                load_rows(x_first[c], x, c, 0, 2 * W)
+            if c == 0:
+                load_codes(nc.sync, a_codes[1], a_words, 1)
+                load_codes(nc.sync, b_raw[1], b_words, 1)
+            else:
+                load_rows(w_raw[1, c - 1], xw, c - 1, 512, 512)
         for s in range(2, STAGES):
             for c in range(CHUNKS):
                 load_rows(x_raw[s, c], x, c, s * W, W)
@@ -282,61 +281,6 @@ def tile_concord_precision_gradient_s12_kernel(tc, a_words, a_scales, b_words, b
                 omega(k // 8, k % 8)
                 omega_out(k // 8, k % 8, eng)
 
-        sort_b_codes(0)
-        sort_b_scales()
-        sort_b_codes(1)
-        w_weave(0, 0, "V")
-        w_weave(1, 0, "V")
-        w_quant(0, 0)
-        nc.vector.transpose(out=d_turned[:], in_=d_rows[:])
-        x_weave(0, 0, "V")
-        w_quant(1, 0)
-        nc.vector.reciprocal(out=d_rec[:], in_=d_turned[:, 0:256:32])
-        x_quant(0, 0)
-        omega_run(0, 6)
-        w_weave(1, 1, "S")
-        w_weave(0, 1, "V")
-        nc.vector.tensor_scalar(out=d_neg[:], in0=d_rec[:], scalar1=-1.0, scalar2=None, op0=ALU.mult)
-        x_weave(0, 1, "V")
-        w_quant(0, 1)
-        omega_run(6, 2)
-        x_weave(1, 0, "S")
-        x_quant(0, 1)
-        w_quant(1, 1)
-        w_weave(0, 2, "V")
-        omega_run(8, 3)
-        x_weave(0, 2, "S")
-        x_quant(1, 0)
-        w_weave(1, 2, "V")
-        w_quant(0, 2)
-        omega_run(11, 5)
-        x_weave(1, 1, "V")
-        w_quant(1, 2)
-        x_quant(0, 2)
-        w_weave(1, 3, "S")
-        w_weave(0, 3, "V")
-        x_quant(1, 1)
-        x_weave(0, 3, "V")
-        w_quant(0, 3)
-        x_weave(1, 2, "V")
-        x_quant(0, 3)
-        w_quant(1, 3)
-        x_weave(1, 3, "S")
-        x_weave(2, 0, "V")
-        x_quant(1, 2)
-        x_quant(1, 3)
-
-        for c in range(CHUNKS + LAG):
-            if c < CHUNKS:
-                cov(0, [c], range(HALVES))
-            if c >= LAG:
-                cov(1, [c - LAG], range(HALVES))
-
-        def cov_leave(s, engines):
-            for h in range(HALVES):
-                for pair in range(2):
-                    cov_out(s, h, pair, engines[h])
-
         def supply(s, first):
             for c in range(first, CHUNKS):
                 x_weave(s, c, "V")
@@ -344,8 +288,63 @@ def tile_concord_precision_gradient_s12_kernel(tc, a_words, a_scales, b_words, b
                     x_quant(s, c - 1)
             x_quant(s, last)
 
-        cov_leave(0, "SS")
-        cov_leave(1, "SS")
+        def cov_leave(s, engines):
+            for h in range(HALVES):
+                for pair in range(2):
+                    cov_out(s, h, pair, engines[h])
+
+        sort_b_codes(0)
+        sort_b_scales()
+        w_weave(0, 0, "V")
+        nc.vector.transpose(out=d_turned[:], in_=d_rows[:])
+        w_quant(0, 0)
+        nc.vector.reciprocal(out=d_rec[:], in_=d_turned[:, 0:256:32])
+        x_weave(0, 0, "V")
+        nc.vector.tensor_scalar(out=d_neg[:], in0=d_rec[:], scalar1=-1.0, scalar2=None, op0=ALU.mult)
+        x_weave(1, 0, "V")
+        x_quant(0, 0)
+        sort_b_codes(1)
+        x_quant(1, 0)
+        w_weave(0, 1, "V")
+        x_weave(0, 1, "V")
+        w_quant(0, 1)
+        x_weave(1, 1, "V")
+        x_quant(0, 1)
+        omega_run(0, 8)
+        w_weave(1, 0, "S")
+        omega_run(8, 3)
+        x_quant(1, 1)
+        w_weave(0, 2, "V")
+        x_weave(0, 2, "V")
+        w_quant(0, 2)
+        x_weave(1, 2, "V")
+        omega_run(11, 5)
+        w_quant(1, 0)
+        x_quant(0, 2)
+        w_weave(1, 1, "V")
+        x_quant(1, 2)
+        w_weave(0, 3, "V")
+        w_quant(1, 1)
+        x_weave(0, 3, "S")
+        x_weave(1, 3, "S")
+        w_weave(1, 3, "S")
+        w_quant(0, 3)
+        x_quant(0, 3)
+        w_weave(1, 2, "V")
+        x_quant(1, 3)
+        w_quant(1, 2)
+        x_weave(2, 0, "V")
+        w_quant(1, 3)
+
+        for c in range(CHUNKS + 1):
+            for h in range(HALVES):
+                if 0 <= c - h < CHUNKS:
+                    for s in range(2):
+                        cov(s, [c - h], [h])
+        for h in range(HALVES):
+            for s in range(2):
+                for pair in range(2):
+                    cov_out(s, h, pair, "S")
         supply(2, 1)
         for c in range(CHUNKS):
             cov(2, [c], range(HALVES))

@@ -52,7 +52,8 @@ def tile_concord_precision_gradient_s12_kernel(tc, a_words, a_scales, b_words, b
         b_codes = [kt("b_codes%d" % h, [P, 2, 1024], U8) for h in range(HALVES)]
         b_sc_raw = kt("b_sc_raw", [P, 2, 1024], U8)
         b_sc = kt("b_sc", [P, 2, 1024], U8)
-        w_raw = {(h, c): kt("w_raw%d%d" % (h, c), [P, SLOTS, 512], BF16) for h in range(HALVES) for c in range(CHUNKS)}
+        w_first = [kt("w_first%d" % h, [P, SLOTS, 512], BF16) for h in range(HALVES)]
+        w_raw = {c: kt("w_raw%d" % c, [P, SLOTS, 1024], BF16) for c in range(1, CHUNKS)}
         x_first = [kt("x_first%d" % c, [P, SLOTS, 2 * W], BF16) for c in range(CHUNKS)]
         x_raw = {(s, c): kt("x_raw%d%d" % (s, c), [P, SLOTS, W], BF16) for s in range(2, STAGES) for c in range(CHUNKS)}
         w_codes = {(h, c): kt("w_codes%d%d" % (h, c), [P, 512], U32) for h in range(HALVES) for c in range(CHUNKS)}
@@ -86,10 +87,12 @@ def tile_concord_precision_gradient_s12_kernel(tc, a_words, a_scales, b_words, b
             nc.sync.dma_start(out=dst[:], in_=src[c * 512 : (c + 1) * 512, lo : lo + n].rearrange("(p j) w -> p j w", j=SLOTS))
 
         def sort_b_scales():
-            nc.vector.tensor_copy(
-                out=b_sc[:].bitcast(I32).rearrange("p g (h u s) -> p g h u s", h=2, u=4),
-                in_=b_sc_raw[:].bitcast(I32).rearrange("p g (h s u) -> p g h u s", h=2, u=4),
-            )
+            for q in range(4):
+                rows = slice(32 * q, 32 * q + 4)
+                nc.vector.tensor_copy(
+                    out=b_sc[rows].bitcast(I32).rearrange("p g (h u s) -> p g h u s", h=2, u=4),
+                    in_=b_sc_raw[rows].bitcast(I32).rearrange("p g (h s u) -> p g h u s", h=2, u=4),
+                )
 
         def sort_b_codes(h):
             nc.vector.tensor_copy(
@@ -122,7 +125,7 @@ def tile_concord_precision_gradient_s12_kernel(tc, a_words, a_scales, b_words, b
         def w_weave(h, c, eng):
             t = work.tile([P, 2048], BF16, name="w_grp", tag="w_grp", align_bytes=64)
             grp["W", h, c] = t
-            src = w_raw[h, c][:]
+            src = w_raw[c][:, :, h * 512 : (h + 1) * 512] if c else w_first[h][:]
             copy(eng, t[:].rearrange("p (u s w j) -> p u s j w", u=4, s=32, w=4), src.rearrange("p j (s u w) -> p u s j w", u=4, w=4))
 
         def w_quant(h, c):
@@ -250,26 +253,28 @@ def tile_concord_precision_gradient_s12_kernel(tc, a_words, a_scales, b_words, b
             copy(eng, g[:], ps["mirror", r, s][:])
             store_square(g, r, s)
 
-        nc.vector.memset(b_sc_raw[:].bitcast(I32), 0)
         nc.vector.memset(a_sc[:].bitcast(I32), 0)
+        nc.vector.memset(b_sc[:].bitcast(I32), 0)
         nc.gpsimd.memset(d_rows[:], 0.0)
         nc.gpsimd.dma_start(out=d_rows[0:P:32, :].rearrange("q (b a) -> q b a", a=32), in_=d.rearrange("(b q a) -> q b a", q=4, a=32))
         nc.gpsimd.memset(ident_wide[:], 0.0)
         make_identity(nc, ident, nomemset=True)
 
-        load_codes(nc.sync, b_raw[0], b_words, 0)
         load_scales(nc.sync, b_sc_raw, b_scales, range(4))
-        load_scales(nc.sync, a_sc, a_scales, range(4))
+        load_scales(nc.sync, a_sc, a_scales, range(2))
+        load_codes(nc.sync, b_raw[0], b_words, 0)
         load_codes(nc.sync, a_codes[0], a_words, 0)
-        for c in range(CHUNKS + 1):
-            if c < CHUNKS:
-                load_rows(w_raw[0, c], xw, c, 0, 512)
-                load_rows(x_first[c], x, c, 0, 2 * W)
-            if c == 0:
-                load_codes(nc.sync, a_codes[1], a_words, 1)
+        load_scales(nc.sync, a_sc, a_scales, range(2, 4))
+        load_rows(w_first[0], xw, 0, 0, 512)
+        load_rows(x_first[0], x, 0, 0, 2 * W)
+        load_codes(nc.sync, a_codes[1], a_words, 1)
+        for c in range(1, CHUNKS):
+            load_rows(w_raw[c], xw, c, 0, 1024)
+            if c == 1:
                 load_codes(nc.sync, b_raw[1], b_words, 1)
-            else:
-                load_rows(w_raw[1, c - 1], xw, c - 1, 512, 512)
+            load_rows(x_first[c], x, c, 0, 2 * W)
+            if c == 1:
+                load_rows(w_first[1], xw, 0, 512, 512)
         for s in range(2, STAGES):
             for c in range(CHUNKS):
                 load_rows(x_raw[s, c], x, c, s * W, W)
@@ -293,8 +298,8 @@ def tile_concord_precision_gradient_s12_kernel(tc, a_words, a_scales, b_words, b
                 for pair in range(2):
                     cov_out(s, h, pair, engines[h])
 
-        sort_b_codes(0)
         sort_b_scales()
+        sort_b_codes(0)
         w_weave(0, 0, "V")
         nc.vector.transpose(out=d_turned[:], in_=d_rows[:])
         w_quant(0, 0)
@@ -303,34 +308,34 @@ def tile_concord_precision_gradient_s12_kernel(tc, a_words, a_scales, b_words, b
         nc.vector.tensor_scalar(out=d_neg[:], in0=d_rec[:], scalar1=-1.0, scalar2=None, op0=ALU.mult)
         x_weave(1, 0, "V")
         x_quant(0, 0)
-        sort_b_codes(1)
         x_quant(1, 0)
         w_weave(0, 1, "V")
-        x_weave(0, 1, "V")
+        sort_b_codes(1)
+        omega_run(0, 6)
+        w_weave(1, 1, "S")
         w_quant(0, 1)
+        x_weave(0, 1, "V")
         x_weave(1, 1, "V")
         x_quant(0, 1)
-        omega_run(0, 8)
-        w_weave(1, 0, "S")
-        omega_run(8, 3)
         x_quant(1, 1)
+        w_weave(1, 0, "V")
+        w_quant(1, 1)
         w_weave(0, 2, "V")
+        w_quant(1, 0)
+        omega_run(6, 6)
+        x_weave(1, 2, "S")
+        omega_run(12, 4)
         x_weave(0, 2, "V")
         w_quant(0, 2)
-        x_weave(1, 2, "V")
-        omega_run(11, 5)
-        w_quant(1, 0)
         x_quant(0, 2)
-        w_weave(1, 1, "V")
-        x_quant(1, 2)
         w_weave(0, 3, "V")
-        w_quant(1, 1)
-        x_weave(0, 3, "S")
+        x_quant(1, 2)
         x_weave(1, 3, "S")
         w_weave(1, 3, "S")
+        x_weave(0, 3, "V")
         w_quant(0, 3)
-        x_quant(0, 3)
         w_weave(1, 2, "V")
+        x_quant(0, 3)
         x_quant(1, 3)
         w_quant(1, 2)
         x_weave(2, 0, "V")
@@ -346,58 +351,39 @@ def tile_concord_precision_gradient_s12_kernel(tc, a_words, a_scales, b_words, b
                 for pair in range(2):
                     cov_out(s, h, pair, "S")
         supply(2, 1)
-        for c in range(CHUNKS):
-            cov(2, [c], range(HALVES))
-        for s in range(2):
+        supply(3, 0)
+        for s in range(2, STAGES):
+            for c in range(CHUNKS):
+                cov(s, [c], range(HALVES))
+            cov_leave(s, "SS")
+        for s in range(STAGES):
             for h in range(HALVES):
                 omega_quant(h, s)
-            for h in range(HALVES):
-                cov_quant(s, h)
-        square(0, 0)
+            if s < 3:
+                for h in range(HALVES):
+                    cov_quant(s, h)
         square(1, 0)
-        square(1, 1)
-        x_weave(3, 0, "V")
-        x_weave(3, 1, "V")
-        x_quant(3, 0)
-        diag_out(0)
-        x_weave(3, 2, "V")
-        x_quant(3, 1)
         square_out(1, 0, "V")
-        mirror(0, 1)
-        cov_leave(2, "SS")
-        x_weave(3, 3, "S")
-        x_quant(3, 2)
-        diag_out(1)
-        x_quant(3, 3)
-        mirror_out(0, 1, "S")
+        for b in range(4, 6):
+            wide(b)
+            wide_out(b, "V")
         for h in range(HALVES):
-            cov(3, range(CHUNKS), [h])
-        for h in range(HALVES):
-            omega_quant(h, 2)
-        for h in range(HALVES):
-            cov_quant(2, h)
-        for h in range(HALVES):
-            omega_quant(h, 3)
-        cov_leave(3, "SS")
-        cov_quant(3, 0)
-        wide(4)
-        wide_out(4, "V")
-        cov_quant(3, 1)
-        wide(5)
-        wide_out(5, "S")
-        wide(6)
-        wide_out(6, "V")
-        for r in range(2):
-            mirror(r, 2)
-            mirror_out(r, 2, "SV"[r])
-        wide(7)
-        wide_out(7, "S")
+            cov_quant(3, h)
+        square(0, 0)
+        diag_out(0)
+        for r, s, eng in ((0, 1, "S"), (0, 2, "V"), (1, 2, "S")):
+            mirror(r, s)
+            mirror_out(r, s, eng)
+        for b in range(6, 8):
+            wide(b)
+            wide_out(b, "VS"[b % 2])
         square(3, 2)
-        square_out(3, 2, "V")
+        square_out(3, 2, "S")
         for r in range(3):
             mirror(r, 3)
-            mirror_out(r, 3, "SVS"[r])
-        square(2, 2)
-        diag_out(2)
+            mirror_out(r, 3, "VSV"[r])
+        for s in range(1, 3):
+            square(s, s)
+            diag_out(s)
         for b in range(6, 8):
             diag_row(b)

@@ -51,7 +51,7 @@ def tile_concord_precision_gradient_s12_kernel(tc, a_words, a_scales, b_words, b
         b_raw = [kt("b_raw%d" % h, [P, 2, 1024], U8) for h in range(HALVES)]
         b_codes = [kt("b_codes%d" % h, [P, 2, 1024], U8) for h in range(HALVES)]
         b_sc_raw = kt("b_sc_raw", [P, 2, 1024], U8)
-        b_sc = kt("b_sc", [P, 2, 1024], U8)
+        b_sc = [kt("b_sc%d" % h, [P, 2, 512], U8) for h in range(HALVES)]
         w_first = [kt("w_first%d" % h, [P, SLOTS, 512], BF16) for h in range(HALVES)]
         w_raw = {c: kt("w_raw%d" % c, [P, SLOTS, 1024], BF16) for c in range(1, CHUNKS)}
         x_first = [kt("x_first%d" % c, [P, SLOTS, 2 * W], BF16) for c in range(CHUNKS)]
@@ -80,18 +80,19 @@ def tile_concord_precision_gradient_s12_kernel(tc, a_words, a_scales, b_words, b
             eng.dma_start(out=dst[:].bitcast(I32), in_=src[:, :, h * 1024 : (h + 1) * 1024].bitcast(I32).rearrange("g p n -> p g n"))
 
         def load_scales(eng, dst, src, quadrants):
-            for q in quadrants:
-                eng.dma_start(out=dst[32 * q : 32 * q + 4, :, :].bitcast(I32), in_=src[:, 4 * q : 4 * q + 4, :].bitcast(I32).rearrange("g q n -> q g n"))
+            for r in quadrants:
+                eng.dma_start(out=dst[r:P:32, :, :].bitcast(I32), in_=src[:, r:16:4, :].bitcast(I32).rearrange("g q n -> q g n"))
 
         def load_rows(dst, src, c, lo, n):
             nc.sync.dma_start(out=dst[:], in_=src[c * 512 : (c + 1) * 512, lo : lo + n].rearrange("(p j) w -> p j w", j=SLOTS))
 
-        def sort_b_scales():
+        def sort_b_scales(h):
+            cols = slice(h * 512, (h + 1) * 512)
             for q in range(4):
                 rows = slice(32 * q, 32 * q + 4)
                 nc.vector.tensor_copy(
-                    out=b_sc[rows].bitcast(I32).rearrange("p g (h u s) -> p g h u s", h=2, u=4),
-                    in_=b_sc_raw[rows].bitcast(I32).rearrange("p g (h s u) -> p g h u s", h=2, u=4),
+                    out=b_sc[h][rows].bitcast(I32).rearrange("p g (u s) -> p g u s", u=4),
+                    in_=b_sc_raw[rows, :, cols].bitcast(I32).rearrange("p g (s u) -> p g u s", u=4),
                 )
 
         def sort_b_codes(h):
@@ -108,7 +109,7 @@ def tile_concord_precision_gradient_s12_kernel(tc, a_words, a_scales, b_words, b
                     nc.tensor.matmul_mx(
                         out=t[:, u * P : (u + 1) * P],
                         lhsT=b_codes[h][:, g, u * 256 : (u + 1) * 256].bitcast(FP4X4),
-                        lhsT_scale=b_sc[:, g, h * 512 + u * P : h * 512 + (u + 1) * P],
+                        lhsT_scale=b_sc[h][:, g, u * P : (u + 1) * P],
                         rhs=a_codes[b // 4][:, g, (b % 4) * 256 : (b % 4 + 1) * 256].bitcast(FP4X4),
                         rhs_scale=a_sc[:, g, b * P : (b + 1) * P],
                         start=(g == 0),
@@ -254,7 +255,8 @@ def tile_concord_precision_gradient_s12_kernel(tc, a_words, a_scales, b_words, b
             store_square(g, r, s)
 
         nc.vector.memset(a_sc[:].bitcast(I32), 0)
-        nc.vector.memset(b_sc[:].bitcast(I32), 0)
+        for h in range(HALVES):
+            nc.vector.memset(b_sc[h][:].bitcast(I32), 0)
         nc.gpsimd.memset(d_rows[:], 0.0)
         nc.gpsimd.dma_start(out=d_rows[0:P:32, :].rearrange("q (b a) -> q b a", a=32), in_=d.rearrange("(b q a) -> q b a", q=4, a=32))
         nc.gpsimd.memset(ident_wide[:], 0.0)
@@ -298,8 +300,9 @@ def tile_concord_precision_gradient_s12_kernel(tc, a_words, a_scales, b_words, b
                 for pair in range(2):
                     cov_out(s, h, pair, engines[h])
 
-        sort_b_scales()
+        sort_b_scales(0)
         sort_b_codes(0)
+        sort_b_scales(1)
         w_weave(0, 0, "V")
         nc.vector.transpose(out=d_turned[:], in_=d_rows[:])
         w_quant(0, 0)

@@ -52,8 +52,7 @@ def tile_concord_precision_gradient_s12_kernel(tc, a_words, a_scales, b_words, b
         b_codes = [kt("b_codes%d" % h, [P, 2, 1024], U8) for h in range(HALVES)]
         b_sc_raw = kt("b_sc_raw", [P, 2, 1024], U8)
         b_sc = [kt("b_sc%d" % h, [P, 2, 512], U8) for h in range(HALVES)]
-        w_first = [kt("w_first%d" % h, [P, SLOTS, 512], BF16) for h in range(HALVES)]
-        w_raw = {c: kt("w_raw%d" % c, [P, SLOTS, 1024], BF16) for c in range(1, CHUNKS)}
+        w_raw = {(h, c): kt("w_raw%d%d" % (h, c), [P, SLOTS, 512], BF16) for h in range(HALVES) for c in range(CHUNKS)}
         x_first = [kt("x_first%d" % c, [P, SLOTS, 2 * W], BF16) for c in range(CHUNKS)]
         x_raw = {(s, c): kt("x_raw%d%d" % (s, c), [P, SLOTS, W], BF16) for s in range(2, STAGES) for c in range(CHUNKS)}
         w_codes = {(h, c): kt("w_codes%d%d" % (h, c), [P, 512], U32) for h in range(HALVES) for c in range(CHUNKS)}
@@ -126,7 +125,7 @@ def tile_concord_precision_gradient_s12_kernel(tc, a_words, a_scales, b_words, b
         def w_weave(h, c, eng):
             t = work.tile([P, 2048], BF16, name="w_grp", tag="w_grp", align_bytes=64)
             grp["W", h, c] = t
-            src = w_raw[c][:, :, h * 512 : (h + 1) * 512] if c else w_first[h][:]
+            src = w_raw[h, c][:]
             copy(eng, t[:].rearrange("p (u s w j) -> p u s j w", u=4, s=32, w=4), src.rearrange("p j (s u w) -> p u s j w", u=4, w=4))
 
         def w_quant(h, c):
@@ -267,16 +266,15 @@ def tile_concord_precision_gradient_s12_kernel(tc, a_words, a_scales, b_words, b
         load_codes(nc.sync, b_raw[0], b_words, 0)
         load_codes(nc.sync, a_codes[0], a_words, 0)
         load_scales(nc.sync, a_sc, a_scales, range(2, 4))
-        load_rows(w_first[0], xw, 0, 0, 512)
-        load_rows(x_first[0], x, 0, 0, 2 * W)
-        load_codes(nc.sync, a_codes[1], a_words, 1)
-        for c in range(1, CHUNKS):
-            load_rows(w_raw[c], xw, c, 0, 1024)
-            if c == 1:
+        for c in range(CHUNKS + 1):
+            if c < CHUNKS:
+                load_rows(w_raw[0, c], xw, c, 0, 512)
+                load_rows(x_first[c], x, c, 0, 2 * W)
+            if c == 0:
+                load_codes(nc.sync, a_codes[1], a_words, 1)
                 load_codes(nc.sync, b_raw[1], b_words, 1)
-            load_rows(x_first[c], x, c, 0, 2 * W)
-            if c == 1:
-                load_rows(w_first[1], xw, 0, 512, 512)
+            else:
+                load_rows(w_raw[1, c - 1], xw, c - 1, 512, 512)
         for s in range(2, STAGES):
             for c in range(CHUNKS):
                 load_rows(x_raw[s, c], x, c, s * W, W)
@@ -309,36 +307,37 @@ def tile_concord_precision_gradient_s12_kernel(tc, a_words, a_scales, b_words, b
         nc.vector.reciprocal(out=d_rec[:], in_=d_turned[:, 0:256:32])
         x_weave(0, 0, "V")
         nc.vector.tensor_scalar(out=d_neg[:], in0=d_rec[:], scalar1=-1.0, scalar2=None, op0=ALU.mult)
-        x_weave(1, 0, "V")
+        omega_run(0, 1)
+        x_weave(1, 0, "S")
         x_quant(0, 0)
-        x_quant(1, 0)
-        w_weave(0, 1, "V")
         sort_b_codes(1)
-        omega_run(0, 6)
-        w_weave(1, 1, "S")
-        w_quant(0, 1)
+        w_weave(0, 1, "V")
+        x_quant(1, 0)
         x_weave(0, 1, "V")
+        w_quant(0, 1)
         x_weave(1, 1, "V")
         x_quant(0, 1)
+        omega_run(1, 7)
+        w_weave(1, 0, "S")
+        omega_run(8, 3)
         x_quant(1, 1)
-        w_weave(1, 0, "V")
-        w_quant(1, 1)
         w_weave(0, 2, "V")
-        w_quant(1, 0)
-        omega_run(6, 6)
-        x_weave(1, 2, "S")
-        omega_run(12, 4)
         x_weave(0, 2, "V")
         w_quant(0, 2)
+        x_weave(1, 2, "V")
+        omega_run(11, 5)
+        w_quant(1, 0)
         x_quant(0, 2)
-        w_weave(0, 3, "V")
+        w_weave(1, 1, "V")
         x_quant(1, 2)
+        w_weave(0, 3, "V")
+        w_quant(1, 1)
+        x_weave(0, 3, "S")
         x_weave(1, 3, "S")
         w_weave(1, 3, "S")
-        x_weave(0, 3, "V")
         w_quant(0, 3)
-        w_weave(1, 2, "V")
         x_quant(0, 3)
+        w_weave(1, 2, "V")
         x_quant(1, 3)
         w_quant(1, 2)
         x_weave(2, 0, "V")

@@ -20,8 +20,6 @@ SLOTS = 4
 CHUNKS = 4
 STAGES = 4
 W = 256
-NARROW_STAGES = 0
-LAG = 1
 
 
 def tile_concord_precision_gradient_s12_kernel(tc, a_words, a_scales, b_words, b_scales, xw, x, d, out):
@@ -75,12 +73,12 @@ def tile_concord_precision_gradient_s12_kernel(tc, a_words, a_scales, b_words, b
         ps = {}
         g_sb = {}
 
-        def load_codes(eng, dst, src, h):
-            eng.dma_start(out=dst[:].bitcast(I32), in_=src[:, :, h * 1024 : (h + 1) * 1024].bitcast(I32).rearrange("g p n -> p g n"))
+        def load_codes(dst, src, h):
+            nc.sync.dma_start(out=dst[:].bitcast(I32), in_=src[:, :, h * 1024 : (h + 1) * 1024].bitcast(I32).rearrange("g p n -> p g n"))
 
-        def load_scales(eng, dst, src, quadrants):
-            for r in quadrants:
-                eng.dma_start(out=dst[r:P:32, :, :].bitcast(I32), in_=src[:, r:16:4, :].bitcast(I32).rearrange("g q n -> q g n"))
+        def load_scales(dst, src, rows):
+            for r in rows:
+                nc.sync.dma_start(out=dst[r:P:32, :, :].bitcast(I32), in_=src[:, r:16:4, :].bitcast(I32).rearrange("g q n -> q g n"))
 
         def load_rows(dst, src, c, lo, n):
             nc.sync.dma_start(out=dst[:], in_=src[c * 512 : (c + 1) * 512, lo : lo + n].rearrange("(p j) w -> p j w", j=SLOTS))
@@ -115,18 +113,18 @@ def tile_concord_precision_gradient_s12_kernel(tc, a_words, a_scales, b_words, b
                         stop=(g == 1),
                     )
 
-        def omega_out(h, b, eng):
+        def omega_out(h, b):
             lo = (b % 2) * P
-            copy(eng, o_grp[h, b // 2][:, lo : lo + P, :], ps["O", h, b][:].rearrange("p (u n) -> p n u", u=SLOTS))
+            copy("S", o_grp[h, b // 2][:, lo : lo + P, :], ps["O", h, b][:].rearrange("p (u n) -> p n u", u=SLOTS))
 
         def omega_quant(h, s):
             nc.vector.quantize_mx(out=o_codes[h][:, s * W : (s + 1) * W].bitcast(FP8X4), scales=o_sc[h][:, s * W : (s + 1) * W], in_=o_grp[h, s][:].rearrange("p n t -> p (n t)"))
 
-        def w_weave(h, c, eng):
-            t = work.tile([P, 2048], BF16, name="w_grp", tag="w_grp", align_bytes=64)
-            grp["W", h, c] = t
-            src = w_raw[h, c][:]
-            copy(eng, t[:].rearrange("p (u s w j) -> p u s j w", u=4, s=32, w=4), src.rearrange("p j (s u w) -> p u s j w", u=4, w=4))
+        def w_weave(h, c, eng, slots=slice(0, SLOTS)):
+            if ("W", h, c) not in grp:
+                grp["W", h, c] = work.tile([P, 2048], BF16, name="w_grp", tag="w_grp", align_bytes=64)
+            dst = grp["W", h, c][:].rearrange("p (u s w j) -> p u s j w", u=4, s=32, w=4)
+            copy(eng, dst[:, slots], w_raw[h, c][:].rearrange("p j (s u w) -> p u s j w", u=4, w=4)[:, slots])
 
         def w_quant(h, c):
             nc.vector.quantize_mx(out=w_codes[h, c][:].bitcast(FP8X4), scales=w_sc[h, c][:], in_=grp["W", h, c][:])
@@ -140,31 +138,25 @@ def tile_concord_precision_gradient_s12_kernel(tc, a_words, a_scales, b_words, b
         def x_quant(s, c):
             nc.vector.quantize_mx(out=x_codes[s, c][:].bitcast(FP8X4), scales=x_sc[s, c][:], in_=grp["X", s, c][:])
 
-        def cov(s, chunks, halves):
-            n = P if s < NARROW_STAGES else W
-            sums = 512 // n
-            for h, k in [(h, k) for h in halves for k in range(2)]:
-                for c in chunks:
-                    if c == 0:
-                        ps["C", s, h, k] = bank()
-                    t = ps["C", s, h, k]
-                    for e in range(sums):
-                        u, lo = (e, k * P) if n == P else (2 * k + e, 0)
-                        nc.tensor.matmul_mx(
-                            out=t[:, e * n : (e + 1) * n],
-                            lhsT=w_codes[h, c][:, u * P : (u + 1) * P].bitcast(FP8X4),
-                            lhsT_scale=w_sc[h, c][:, u * P : (u + 1) * P],
-                            rhs=x_codes[s, c][:, lo : lo + n].bitcast(FP8X4),
-                            rhs_scale=x_sc[s, c][:, lo : lo + n],
-                            start=(c == 0 and e == 0),
-                            stop=(c == CHUNKS - 1 and e == sums - 1),
-                        )
+        def cov(s, c, h):
+            for pair in range(2):
+                if c == 0:
+                    ps["C", s, h, pair] = bank()
+                for e in range(2):
+                    u = 2 * pair + e
+                    nc.tensor.matmul_mx(
+                        out=ps["C", s, h, pair][:, e * W : (e + 1) * W],
+                        lhsT=w_codes[h, c][:, u * P : (u + 1) * P].bitcast(FP8X4),
+                        lhsT_scale=w_sc[h, c][:, u * P : (u + 1) * P],
+                        rhs=x_codes[s, c][:].bitcast(FP8X4),
+                        rhs_scale=x_sc[s, c][:],
+                        start=(c == 0 and e == 0),
+                        stop=(c == CHUNKS - 1 and e == 1),
+                    )
 
-        def cov_out(s, h, k, eng):
-            if s < NARROW_STAGES:
-                copy(eng, c_grp[h, s][:, k * P : (k + 1) * P, :], ps["C", s, h, k][:].rearrange("p (u n) -> p n u", u=SLOTS))
-            else:
-                copy(eng, c_grp[h, s][:, :, 2 * k : 2 * k + 2], ps["C", s, h, k][:].rearrange("p (u n) -> p n u", u=2))
+        def cov_out(s, h):
+            for pair in range(2):
+                copy("S", c_grp[h, s][:, :, 2 * pair : 2 * pair + 2], ps["C", s, h, pair][:].rearrange("p (u n) -> p n u", u=2))
 
         def cov_quant(s, h):
             nc.vector.quantize_mx(out=c_codes[h][:, s * W : (s + 1) * W].bitcast(FP8X4), scales=c_sc[h][:, s * W : (s + 1) * W], in_=c_grp[h, s][:].rearrange("p n t -> p (n t)"))
@@ -261,18 +253,18 @@ def tile_concord_precision_gradient_s12_kernel(tc, a_words, a_scales, b_words, b
         nc.gpsimd.memset(ident_wide[:], 0.0)
         make_identity(nc, ident, nomemset=True)
 
-        load_scales(nc.sync, b_sc_raw, b_scales, range(4))
-        load_scales(nc.sync, a_sc, a_scales, range(2))
-        load_codes(nc.sync, b_raw[0], b_words, 0)
-        load_codes(nc.sync, a_codes[0], a_words, 0)
-        load_scales(nc.sync, a_sc, a_scales, range(2, 4))
+        load_scales(b_sc_raw, b_scales, range(4))
+        load_scales(a_sc, a_scales, range(2))
+        load_codes(b_raw[0], b_words, 0)
+        load_codes(a_codes[0], a_words, 0)
+        load_scales(a_sc, a_scales, range(2, 4))
         for c in range(CHUNKS + 1):
             if c < CHUNKS:
                 load_rows(w_raw[0, c], xw, c, 0, 512)
                 load_rows(x_first[c], x, c, 0, 2 * W)
             if c == 0:
-                load_codes(nc.sync, a_codes[1], a_words, 1)
-                load_codes(nc.sync, b_raw[1], b_words, 1)
+                load_codes(a_codes[1], a_words, 1)
+                load_codes(b_raw[1], b_words, 1)
             else:
                 load_rows(w_raw[1, c - 1], xw, c - 1, 512, 512)
         for s in range(2, STAGES):
@@ -281,10 +273,10 @@ def tile_concord_precision_gradient_s12_kernel(tc, a_words, a_scales, b_words, b
 
         last = CHUNKS - 1
 
-        def omega_run(first, n, eng="S"):
+        def omega_run(first, n):
             for k in range(first, first + n):
                 omega(k // 8, k % 8)
-                omega_out(k // 8, k % 8, eng)
+                omega_out(k // 8, k % 8)
 
         def supply(s, first):
             for c in range(first, CHUNKS):
@@ -293,77 +285,68 @@ def tile_concord_precision_gradient_s12_kernel(tc, a_words, a_scales, b_words, b
                     x_quant(s, c - 1)
             x_quant(s, last)
 
-        def cov_leave(s, engines):
-            for h in range(HALVES):
-                for pair in range(2):
-                    cov_out(s, h, pair, engines[h])
-
         sort_b_scales(0)
         sort_b_codes(0)
         sort_b_scales(1)
-        w_weave(0, 0, "V")
-        nc.vector.transpose(out=d_turned[:], in_=d_rows[:])
-        w_quant(0, 0)
-        nc.vector.reciprocal(out=d_rec[:], in_=d_turned[:, 0:256:32])
-        x_weave(0, 0, "V")
-        nc.vector.tensor_scalar(out=d_neg[:], in0=d_rec[:], scalar1=-1.0, scalar2=None, op0=ALU.mult)
-        omega_run(0, 1)
-        x_weave(1, 0, "S")
-        x_quant(0, 0)
-        sort_b_codes(1)
-        w_weave(0, 1, "V")
-        x_quant(1, 0)
-        x_weave(0, 1, "V")
-        w_quant(0, 1)
-        x_weave(1, 1, "V")
-        x_quant(0, 1)
-        omega_run(1, 7)
-        w_weave(1, 0, "S")
-        omega_run(8, 3)
-        x_quant(1, 1)
-        w_weave(0, 2, "V")
-        x_weave(0, 2, "V")
-        w_quant(0, 2)
-        x_weave(1, 2, "V")
-        omega_run(11, 5)
-        w_quant(1, 0)
-        x_quant(0, 2)
-        w_weave(1, 1, "V")
-        x_quant(1, 2)
-        w_weave(0, 3, "V")
-        w_quant(1, 1)
-        x_weave(0, 3, "S")
-        x_weave(1, 3, "S")
-        w_weave(1, 3, "S")
-        w_quant(0, 3)
-        x_quant(0, 3)
-        w_weave(1, 2, "V")
-        x_quant(1, 3)
-        w_quant(1, 2)
-        x_weave(2, 0, "V")
-        w_quant(1, 3)
+
+        need = []
+        for c in range(CHUNKS + 1):
+            if c < CHUNKS:
+                need += [("W", 0, c), ("X", 0, c), ("X", 1, c)]
+            if c:
+                need += [("W", 1, c - 1)]
+        need += [("X", 2, 0)]
+        banks_before = {("X", 1, 0): 1, ("W", 1, 0): 7, ("X", 0, last): 8, ("X", 1, last): 0}
+        shared = [("W", 1, last - 1), ("W", 1, last)]
+        between = {
+            1: lambda: nc.vector.transpose(out=d_turned[:], in_=d_rows[:]),
+            2: lambda: (sort_b_codes(1), nc.vector.reciprocal(out=d_rec[:], in_=d_turned[:, 0:256:32])),
+            4: lambda: nc.vector.tensor_scalar(out=d_neg[:], in0=d_rec[:], scalar1=-1.0, scalar2=None, op0=ALU.mult),
+        }
+        done = 0
+        woven = []
+        for k, item in enumerate(need):
+            weave = w_weave if item[0] == "W" else x_weave
+            if k in between:
+                between[k]()
+            if item in banks_before:
+                omega_run(done, banks_before[item])
+                done += banks_before[item]
+                weave(*item[1:], "S")
+            else:
+                if item in shared:
+                    weave(*item[1:], "S", slice(2, 4))
+                    weave(*item[1:], "V", slice(0, 2))
+                else:
+                    weave(*item[1:], "V")
+                for kind, a, c in woven:
+                    (w_quant if kind == "W" else x_quant)(a, c)
+                woven = []
+            woven.append(item)
 
         for c in range(CHUNKS + 1):
             for h in range(HALVES):
                 if 0 <= c - h < CHUNKS:
                     for s in range(2):
-                        cov(s, [c - h], [h])
+                        cov(s, c - h, h)
         for h in range(HALVES):
             for s in range(2):
-                for pair in range(2):
-                    cov_out(s, h, pair, "S")
+                cov_out(s, h)
         supply(2, 1)
         supply(3, 0)
         for s in range(2, STAGES):
             for c in range(CHUNKS):
-                cov(s, [c], range(HALVES))
-            cov_leave(s, "SS")
+                for h in range(HALVES):
+                    cov(s, c, h)
+            for h in range(HALVES):
+                cov_out(s, h)
         for s in range(STAGES):
             for h in range(HALVES):
                 omega_quant(h, s)
             if s < 3:
                 for h in range(HALVES):
                     cov_quant(s, h)
+
         square(1, 0)
         square_out(1, 0, "V")
         for b in range(4, 6):
@@ -379,8 +362,13 @@ def tile_concord_precision_gradient_s12_kernel(tc, a_words, a_scales, b_words, b
         for b in range(6, 8):
             wide(b)
             wide_out(b, "VS"[b % 2])
-        square(3, 2)
-        square_out(3, 2, "S")
+        g = kt("g_square32", [P, 512], F32)
+        g_sb["square", 3, 2] = g
+        for e in range(2):
+            t = bank()
+            grad(t[:, 0:W], 6 + e, 2 * W, W)
+            copy("S", g[:, e * W : (e + 1) * W], t[:, 0:W])
+        store_square(g, 3, 2)
         for r in range(3):
             mirror(r, 3)
             mirror_out(r, 3, "VSV"[r])

@@ -218,14 +218,12 @@ def tile_concord_precision_gradient_s12_kernel(tc, a_words, a_scales, b_words, b
                 )
             store_square(g, s, s)
 
-        def diag_row(b):
+        def diag_row(b, dst):
             s, e = divmod(b, 2)
             t = bank()
             grad(t[:, 0:W], b, s * W, W)
-            g = kt("g_last%d" % b, [P, W], F32)
             z = P - e * P
-            nc.vector.scalar_tensor_tensor(out=g[:], in0=ident_wide[:, z : z + W], scalar=d_neg[:, b : b + 1], in1=t[:, 0:W], op0=ALU.mult, op1=ALU.add)
-            nc.sync.dma_start(out=out[b * P : (b + 1) * P, s * W : (s + 1) * W], in_=g[:])
+            nc.vector.scalar_tensor_tensor(out=dst, in0=ident_wide[:, z : z + W], scalar=d_neg[:, b : b + 1], in1=t[:, 0:W], op0=ALU.mult, op1=ALU.add)
 
         def lower_tile(b, m):
             s, e = divmod(b, 2)
@@ -236,8 +234,8 @@ def tile_concord_precision_gradient_s12_kernel(tc, a_words, a_scales, b_words, b
         def mirror(r, s):
             t = bank()
             ps["mirror", r, s] = t
-            for e in range(2):
-                for f in range(2):
+            for f in range(2):
+                for e in range(2):
                     nc.tensor.transpose(t[:, e * W + f * P : e * W + (f + 1) * P], lower_tile(2 * s + f, 2 * r + e), ident)
 
         def mirror_out(r, s, eng):
@@ -361,7 +359,7 @@ def tile_concord_precision_gradient_s12_kernel(tc, a_words, a_scales, b_words, b
             mirror_out(r, s, eng)
         for b in range(6, 8):
             wide(b)
-            wide_out(b, "VS"[b % 2])
+            wide_out(b, "SV"[b % 2])
         g = kt("g_square32", [P, 512], F32)
         g_sb["square", 3, 2] = g
         for e in range(2):
@@ -369,11 +367,16 @@ def tile_concord_precision_gradient_s12_kernel(tc, a_words, a_scales, b_words, b
             grad(t[:, 0:W], 6 + e, 2 * W, W)
             copy("S", g[:, e * W : (e + 1) * W], t[:, 0:W])
         store_square(g, 3, 2)
+        g = kt("g_diag1", [P, 512], F32)
+        diag_row(2, g[:, 0:W])
         for r in range(3):
             mirror(r, 3)
-            mirror_out(r, 3, "VSV"[r])
-        for s in range(1, 3):
-            square(s, s)
-            diag_out(s)
+            mirror_out(r, 3, "SVS"[r])
+        diag_row(3, g[:, W : 2 * W])
+        store_square(g, 1, 1)
+        square(2, 2)
+        diag_out(2)
         for b in range(6, 8):
-            diag_row(b)
+            g = kt("g_last%d" % b, [P, W], F32)
+            diag_row(b, g[:])
+            nc.sync.dma_start(out=out[b * P : (b + 1) * P, 3 * W : 4 * W], in_=g[:])

@@ -20,22 +20,33 @@ SLOTS = 4
 CHUNKS = 4
 STAGES = 4
 W = 256
+EARLY = 0
+WARM = 8
+LOADS = "sBw cB0 sAwa cA0 sAwb W00 cA1 X00 cB1 W01+ X01 W10 W02 X02 W03+ X03 W12 Y20 Y21 Y22 Y23 Y30 Y31 Y32 Y33"
+V_ORDER = "s0 c0 s1 wW00 d0 qW00 d1 wX0002 c1 wX0024 d2 qX00 wW01 wX0102 qW01 wX0124 qX0102 wW10 qX0124 qW11 wW0202 qW10 wX0202 qW02 qX0202 wW0302 qX0224 wX0302 qW03 qX0302 wW1302 qX0324 wW1202 qW13 wY2002 qW12 wY2024 qY2002 wY2102 qY2024 wY2124 qY2102 wY3002 qY2124 wY3024 qY3002 wY31 qY3024 O002 qY31 O102 C002 C102 O024 O124 C023 C123 g0 g1 g2 C034 C134 g3 g5 g8 g11 g13 g15 g16 g17 g18"
+S_ORDER = "o0 o1 o2 o3 o4 o5 o6 o7 o8 o9 wW11 o10 o11 o12 o13 o14 o15 wW0224 wX0224 wW0324 wX0324 wW1324 wW1224 k000 k001 k100 k101 k010 k011 k110 k111 k200 k201 k210 k211 k300 k301 k310 k311 g4 g6 g7 g9 g10 g12 g14"
+COV_ORDER = "00 10 01 11 20 30 31 21"
+ALIGN = 256
+G_EARLY = 0
+G_AFTER = 2
+GROUPS = 6
+FLIPS = ()
+UNITS = "s10 w4 w5 s00 m01 m02 m12 w6 w7 r62 r72 r21 m03 m13 m23 r31 s22 r63 r73"
 
 
 def tile_concord_precision_gradient_s12_kernel(tc, a_words, a_scales, b_words, b_scales, xw, x, d, out):
     nc = tc.nc
     with ExitStack() as ctx:
         keep = ctx.enter_context(tc.tile_pool(name="keep", bufs=1))
-        work = ctx.enter_context(tc.tile_pool(name="work", bufs=4))
-        psum = ctx.enter_context(tc.psum_pool(name="psum", bufs=8))
+        psum = ctx.enter_context(tc.psum_pool(name="psum", bufs=1))
         ctx.enter_context(tc.manual_schedule())
 
-        def kt(name, shape, dt):
-            t = keep.tile(shape, dt, name=name, tag=name, align_bytes=64)
+        def kt(name, shape, dt, tag=None):
+            t = keep.tile(shape, dt, name=name, tag=tag or name, align_bytes=ALIGN)
             return t
 
-        def bank():
-            t = psum.tile([P, 512], F32, name="bank", tag="bank")
+        def bank(k):
+            t = psum.tile([P, 512], F32, name="bank%d" % k, tag="bank%d" % k)
             return t
 
         def copy(eng, dst, src):
@@ -49,26 +60,24 @@ def tile_concord_precision_gradient_s12_kernel(tc, a_words, a_scales, b_words, b
         b_raw = [kt("b_raw%d" % h, [P, 2, 1024], U8) for h in range(HALVES)]
         b_codes = [kt("b_codes%d" % h, [P, 2, 1024], U8) for h in range(HALVES)]
         b_sc_raw = kt("b_sc_raw", [P, 2, 1024], U8)
-        b_sc = [kt("b_sc%d" % h, [P, 2, 512], U8) for h in range(HALVES)]
-        w_raw = {(h, c): kt("w_raw%d%d" % (h, c), [P, SLOTS, 512], BF16) for h in range(HALVES) for c in range(CHUNKS)}
-        x_first = [kt("x_first%d" % c, [P, SLOTS, 2 * W], BF16) for c in range(CHUNKS)]
-        x_raw = {(s, c): kt("x_raw%d%d" % (s, c), [P, SLOTS, W], BF16) for s in range(2, STAGES) for c in range(CHUNKS)}
-        w_codes = {(h, c): kt("w_codes%d%d" % (h, c), [P, 512], U32) for h in range(HALVES) for c in range(CHUNKS)}
-        w_sc = {(h, c): kt("w_sc%d%d" % (h, c), [P, 512], U8) for h in range(HALVES) for c in range(CHUNKS)}
-        x_codes = {(s, c): kt("x_codes%d%d" % (s, c), [P, W], U32) for s in range(STAGES) for c in range(CHUNKS)}
-        x_sc = {(s, c): kt("x_sc%d%d" % (s, c), [P, W], U8) for s in range(STAGES) for c in range(CHUNKS)}
+        b_sc_all = kt("b_sc", [P, HALVES * 1024], U8)
+        b_sc = [b_sc_all[:, h * 1024 : (h + 1) * 1024].rearrange("p (g n) -> p g n", g=2) for h in range(HALVES)]
+        names = [("W", h, c) for h in range(HALVES) for c in range(CHUNKS)] + [("X", 0, c) for c in range(CHUNKS)] + [("Y", s, k) for s in range(2, STAGES) for k in range(2)]
+        codes = {it: kt("codes%s%d%d" % it, [P, 512], U32) for it in names}
+        scales = {it: kt("scales%s%d%d" % it, [P, 512], U8) for it in names}
         o_codes = [kt("o_codes%d" % h, [P, 1024], U32) for h in range(HALVES)]
         o_sc = [kt("o_sc%d" % h, [P, 1024], U8) for h in range(HALVES)]
         c_codes = [kt("c_codes%d" % h, [P, 1024], U32) for h in range(HALVES)]
         c_sc = [kt("c_sc%d" % h, [P, 1024], U8) for h in range(HALVES)]
-        o_grp = {(h, s): kt("o_grp%d%d" % (h, s), [P, W, SLOTS], BF16) for h in range(HALVES) for s in range(STAGES)}
-        c_grp = {(h, s): kt("c_grp%d%d" % (h, s), [P, W, SLOTS], BF16) for h in range(HALVES) for s in range(STAGES)}
+        o_grp = {(h, z): kt("o_grp%d%d" % (h, z), [P, 2 * W, SLOTS], BF16) for h in range(HALVES) for z in range(2)}
+        c_grp = {(h, z): kt("c_grp%d%d" % (h, z), [P, 2 * W, SLOTS], BF16) for h in range(HALVES) for z in range(2)}
         ident_wide = kt("ident_wide", [P, 3 * P], F32)
         ident = ident_wide[:, P : 2 * P]
         d_rows = kt("d_rows", [P, 256], BF16)
         d_turned = kt("d_turned", [P, 256], BF16)
         d_rec = kt("d_rec", [P, 8], F32)
         d_neg = kt("d_neg", [P, 8], F32)
+        raw = {}
         grp = {}
         ps = {}
         g_sb = {}
@@ -76,12 +85,32 @@ def tile_concord_precision_gradient_s12_kernel(tc, a_words, a_scales, b_words, b
         def load_codes(dst, src, h):
             nc.sync.dma_start(out=dst[:].bitcast(I32), in_=src[:, :, h * 1024 : (h + 1) * 1024].bitcast(I32).rearrange("g p n -> p g n"))
 
-        def load_scales(dst, src, rows):
+        def load_scales(dst, src, rows, cols):
             for r in rows:
-                nc.sync.dma_start(out=dst[r:P:32, :, :].bitcast(I32), in_=src[:, r:16:4, :].bitcast(I32).rearrange("g q n -> q g n"))
+                nc.sync.dma_start(out=dst[r:P:32, :, cols].bitcast(I32), in_=src[:, r:16:4, cols].bitcast(I32).rearrange("g q n -> q g n"))
 
-        def load_rows(dst, src, c, lo, n):
-            nc.sync.dma_start(out=dst[:], in_=src[c * 512 : (c + 1) * 512, lo : lo + n].rearrange("(p j) w -> p j w", j=SLOTS))
+        spent = []
+
+        def loaded(name, shape):
+            spent.append(name)
+            return kt(name, shape, BF16)
+
+        def result(name, width):
+            return kt(name, [P, width], F32, spent.pop(0) if spent else name)
+
+        def load_rows(kind, first, c, n):
+            rows = slice(c * 512, (c + 1) * 512)
+            if kind == "Y":
+                if c % 2 == 0:
+                    raw["Y", first, c // 2] = loaded("rawY%d%d" % (first, c), [P, 2, SLOTS, W])
+                dst = raw["Y", first, c // 2][:, c % 2]
+                src = x[rows, first * W : (first + 1) * W]
+            else:
+                dst = loaded("raw%s%d%d" % (kind, first, c), [P, SLOTS, n * 512])[:]
+                for k in range(n):
+                    raw[kind, first + k, c] = dst[:, :, k * 512 : (k + 1) * 512]
+                src = (xw if kind == "W" else x)[rows, first * 512 : (first + n) * 512]
+            nc.sync.dma_start(out=dst, in_=src.rearrange("(p j) w -> p j w", j=SLOTS))
 
         def sort_b_scales(h):
             cols = slice(h * 512, (h + 1) * 512)
@@ -98,8 +127,8 @@ def tile_concord_precision_gradient_s12_kernel(tc, a_words, a_scales, b_words, b
                 in_=b_raw[h][:].bitcast(I32).rearrange("p g (s u w) -> p g u s w", u=4, w=2),
             )
 
-        def omega(h, b):
-            t = bank()
+        def omega(h, b, k):
+            t = bank(k)
             ps["O", h, b] = t
             for u in range(SLOTS):
                 for g in range(2):
@@ -113,53 +142,59 @@ def tile_concord_precision_gradient_s12_kernel(tc, a_words, a_scales, b_words, b
                         stop=(g == 1),
                     )
 
-        def omega_out(h, b):
-            lo = (b % 2) * P
-            copy("S", o_grp[h, b // 2][:, lo : lo + P, :], ps["O", h, b][:].rearrange("p (u n) -> p n u", u=SLOTS))
+        def omega_out(h, b, eng):
+            lo = (b % 4) * P
+            copy(eng, o_grp[h, b // 4][:, lo : lo + P, :], ps["O", h, b][:].rearrange("p (u n) -> p n u", u=SLOTS))
 
-        def omega_quant(h, s):
-            nc.vector.quantize_mx(out=o_codes[h][:, s * W : (s + 1) * W].bitcast(FP8X4), scales=o_sc[h][:, s * W : (s + 1) * W], in_=o_grp[h, s][:].rearrange("p n t -> p (n t)"))
+        def result_quant(kind, h, lo, hi):
+            dst, sc, src = (o_codes, o_sc, o_grp) if kind == "O" else (c_codes, c_sc, c_grp)
+            cols = slice(lo * W, hi * W)
+            nc.vector.quantize_mx(out=dst[h][:, cols].bitcast(FP8X4), scales=sc[h][:, cols], in_=src[h, lo // 2][:, (lo % 2) * W : (lo % 2 + hi - lo) * W, :].rearrange("p n t -> p (n t)"))
 
-        def w_weave(h, c, eng, slots=slice(0, SLOTS)):
-            if ("W", h, c) not in grp:
-                grp["W", h, c] = work.tile([P, 2048], BF16, name="w_grp", tag="w_grp", align_bytes=64)
-            dst = grp["W", h, c][:].rearrange("p (u s w j) -> p u s j w", u=4, s=32, w=4)
-            copy(eng, dst[:, slots], w_raw[h, c][:].rearrange("p j (s u w) -> p u s j w", u=4, w=4)[:, slots])
+        def weave(item, tag, eng, lo, hi):
+            kind = item[0]
+            if item not in grp:
+                grp[item] = kt("grp%s%d%d" % item, [P, 2048], BF16, tag)
+            if kind == "W":
+                dst = grp[item][:].rearrange("p (u s w j) -> p u s j w", u=4, s=32, w=4)[:, lo:hi]
+                src = raw[item].rearrange("p j (s u w) -> p u s j w", u=4, w=4)[:, lo:hi]
+            elif kind == "X":
+                dst = grp[item][:].rearrange("p (a w j) -> p a j w", w=4, j=4)[:, 32 * lo : 32 * hi]
+                src = raw[item].rearrange("p j (a w) -> p a j w", w=4)[:, 32 * lo : 32 * hi]
+            else:
+                dst = grp[item][:].rearrange("p (e a w j) -> p e a j w", e=2, w=4, j=4)
+                src = raw[item][:].rearrange("p e j (a w) -> p e a j w", w=4)
+                if hi - lo < 4:
+                    part = slice(32 * (lo % 2), 32 * (lo % 2 + hi - lo))
+                    dst, src = dst[:, lo // 2, part], src[:, lo // 2, part]
+            copy(eng, dst, src)
 
-        def w_quant(h, c):
-            nc.vector.quantize_mx(out=w_codes[h, c][:].bitcast(FP8X4), scales=w_sc[h, c][:], in_=grp["W", h, c][:])
+        def quant(item, lo, hi):
+            nc.vector.quantize_mx(out=codes[item][:, lo * P : hi * P].bitcast(FP8X4), scales=scales[item][:, lo * P : hi * P], in_=grp[item][:, lo * 512 : hi * 512])
 
-        def x_weave(s, c, eng):
-            t = work.tile([P, SLOTS * W], BF16, name="x_grp", tag="x_grp", align_bytes=64)
-            grp["X", s, c] = t
-            src = x_first[c][:, :, s * W : (s + 1) * W] if s < 2 else x_raw[s, c][:]
-            copy(eng, t[:].rearrange("p (a w j) -> p a j w", w=4, j=4), src.rearrange("p j (a w) -> p a j w", w=4))
+        def moving(s, c):
+            return (("X", 0, c), s) if s < 2 else (("Y", s, c // 2), c % 2)
 
-        def x_quant(s, c):
-            nc.vector.quantize_mx(out=x_codes[s, c][:].bitcast(FP8X4), scales=x_sc[s, c][:], in_=grp["X", s, c][:])
-
-        def cov(s, c, h):
+        def cov(s, c, h, k, n):
+            item, half = moving(s, c)
+            cols = slice(half * W, (half + 1) * W)
             for pair in range(2):
-                if c == 0:
-                    ps["C", s, h, pair] = bank()
+                if n == 0:
+                    ps["C", s, h, pair] = bank(k + pair)
                 for e in range(2):
                     u = 2 * pair + e
                     nc.tensor.matmul_mx(
                         out=ps["C", s, h, pair][:, e * W : (e + 1) * W],
-                        lhsT=w_codes[h, c][:, u * P : (u + 1) * P].bitcast(FP8X4),
-                        lhsT_scale=w_sc[h, c][:, u * P : (u + 1) * P],
-                        rhs=x_codes[s, c][:].bitcast(FP8X4),
-                        rhs_scale=x_sc[s, c][:],
-                        start=(c == 0 and e == 0),
-                        stop=(c == CHUNKS - 1 and e == 1),
+                        lhsT=codes["W", h, c][:, u * P : (u + 1) * P].bitcast(FP8X4),
+                        lhsT_scale=scales["W", h, c][:, u * P : (u + 1) * P],
+                        rhs=codes[item][:, cols].bitcast(FP8X4),
+                        rhs_scale=scales[item][:, cols],
+                        start=(n == 0 and e == 0),
+                        stop=(n == CHUNKS - 1 and e == 1),
                     )
 
-        def cov_out(s, h):
-            for pair in range(2):
-                copy("S", c_grp[h, s][:, :, 2 * pair : 2 * pair + 2], ps["C", s, h, pair][:].rearrange("p (u n) -> p n u", u=2))
-
-        def cov_quant(s, h):
-            nc.vector.quantize_mx(out=c_codes[h][:, s * W : (s + 1) * W].bitcast(FP8X4), scales=c_sc[h][:, s * W : (s + 1) * W], in_=c_grp[h, s][:].rearrange("p n t -> p (n t)"))
+        def cov_out(s, h, pair, eng):
+            copy(eng, c_grp[h, s // 2][:, (s % 2) * W : (s % 2 + 1) * W, 2 * pair : 2 * pair + 2], ps["C", s, h, pair][:].rearrange("p (u n) -> p n u", u=2))
 
         def grad(dst, b, lo, n):
             rows = slice(b * P, (b + 1) * P)
@@ -178,205 +213,215 @@ def tile_concord_precision_gradient_s12_kernel(tc, a_words, a_scales, b_words, b
                     )
                     step += 1
 
-        def wide(b):
-            t = bank()
-            ps["wide", b] = t
-            grad(t[:], b, 0, 512)
-
-        def wide_out(b, eng):
-            g = kt("g_wide%d" % b, [P, 512], F32)
-            g_sb["wide", b] = g
-            copy(eng, g[:], ps["wide", b][:])
-            nc.sync.dma_start(out=out[b * P : (b + 1) * P, 0:512], in_=g[:])
-
-        def square(s, r):
-            t = bank()
-            ps["square", s, r] = t
-            for e in range(2):
-                grad(t[:, e * W : (e + 1) * W], 2 * s + e, r * W, W)
-
-        def store_square(g, s, r):
-            nc.sync.dma_start(out=out[s * W : (s + 1) * W, r * W : (r + 1) * W].rearrange("(e p) c -> p e c", e=2), in_=g[:].rearrange("p (e c) -> p e c", e=2))
-
-        def square_out(s, r, eng):
-            g = kt("g_square%d%d" % (s, r), [P, 512], F32)
-            g_sb["square", s, r] = g
-            copy(eng, g[:], ps["square", s, r][:])
-            store_square(g, s, r)
-
-        def diag_out(s):
-            g = kt("g_diag%d" % s, [P, 512], F32)
-            for e in range(2):
-                z = P - e * P
-                nc.vector.scalar_tensor_tensor(
-                    out=g[:, e * W : (e + 1) * W],
-                    in0=ident_wide[:, z : z + W],
-                    scalar=d_neg[:, 2 * s + e : 2 * s + e + 1],
-                    in1=ps["square", s, s][:, e * W : (e + 1) * W],
-                    op0=ALU.mult,
-                    op1=ALU.add,
-                )
-            store_square(g, s, s)
-
-        def diag_row(b, dst):
-            s, e = divmod(b, 2)
-            t = bank()
-            grad(t[:, 0:W], b, s * W, W)
-            z = P - e * P
-            nc.vector.scalar_tensor_tensor(out=dst, in0=ident_wide[:, z : z + W], scalar=d_neg[:, b : b + 1], in1=t[:, 0:W], op0=ALU.mult, op1=ALU.add)
-
         def lower_tile(b, m):
             s, e = divmod(b, 2)
             if s >= 2 and m < 4:
                 return g_sb["wide", b][:, m * P : (m + 1) * P]
             return g_sb["square", s, m // 2][:, e * W + (m % 2) * P : e * W + (m % 2 + 1) * P]
 
-        def mirror(r, s):
-            t = bank()
-            ps["mirror", r, s] = t
-            for f in range(2):
+        def g_make(unit, k):
+            t = bank(k)
+            ps[unit] = t
+            if unit[0] == "wide":
+                grad(t[:], unit[1], 0, 512)
+            elif unit[0] == "row":
+                grad(t[:, 0:W], unit[1], unit[2] * W, W)
+            elif unit[0] == "square":
                 for e in range(2):
-                    nc.tensor.transpose(t[:, e * W + f * P : e * W + (f + 1) * P], lower_tile(2 * s + f, 2 * r + e), ident)
+                    grad(t[:, e * W : (e + 1) * W], 2 * unit[1] + e, unit[2] * W, W)
+            else:
+                r, s = unit[1:]
+                for f in range(2):
+                    for e in range(2):
+                        nc.tensor.transpose(t[:, e * W + f * P : e * W + (f + 1) * P], lower_tile(2 * s + f, 2 * r + e), ident)
 
-        def mirror_out(r, s, eng):
-            g = kt("g_mirror%d%d" % (r, s), [P, 512], F32)
-            copy(eng, g[:], ps["mirror", r, s][:])
-            store_square(g, r, s)
+        def less_diagonal(dst, src, b):
+            z = P - (b % 2) * P
+            nc.vector.scalar_tensor_tensor(out=dst, in0=ident_wide[:, z : z + W], scalar=d_neg[:, b : b + 1], in1=src, op0=ALU.mult, op1=ALU.add)
+
+        def store_square(g, s, r):
+            nc.sync.dma_start(out=out[s * W : (s + 1) * W, r * W : (r + 1) * W].rearrange("(e p) c -> p e c", e=2), in_=g[:].rearrange("p (e c) -> p e c", e=2))
+
+        def g_out(unit, eng):
+            t = ps[unit]
+            if unit[0] == "row":
+                b, r = unit[1:]
+                s, e = divmod(b, 2)
+                if s == r:
+                    g_sb[unit] = result("g_row%d" % b, W)
+                    less_diagonal(g_sb[unit][:], t[:, 0:W], b)
+                else:
+                    if e == 0:
+                        g_sb["square", s, r] = result("g_square%d%d" % (s, r), 512)
+                    copy(eng, g_sb["square", s, r][:, e * W : (e + 1) * W], t[:, 0:W])
+                return
+            g = result("g_%s%d%d" % (unit[0], unit[1], unit[-1]), 512)
+            g_sb[unit] = g
+            if unit[0] == "square" and unit[1] == unit[2]:
+                for e in range(2):
+                    less_diagonal(g[:, e * W : (e + 1) * W], t[:, e * W : (e + 1) * W], 2 * unit[1] + e)
+            else:
+                copy(eng, g[:], t[:])
+
+        def flip(unit):
+            g_sb["flip", unit] = kt("g_flip%d" % unit[1], [P, 512], F32)
+            nc.vector.transpose(out=g_sb["flip", unit][:], in_=ps[unit][:])
+
+        def flip_store(unit):
+            for a in range(4):
+                lo = unit[1] * P + 32 * a
+                nc.sync.dma_start(out=out[0:512, lo : lo + 32].rearrange("(b i) j -> i b j", i=32), in_=g_sb["flip", unit][32 * a : 32 * a + 32, :].rearrange("i (b j) -> i b j", j=32))
+
+        def g_store(unit):
+            if unit[0] == "wide":
+                nc.sync.dma_start(out=out[unit[1] * P : (unit[1] + 1) * P, 0:512], in_=g_sb[unit][:])
+            elif unit[0] != "row":
+                store_square(g_sb[unit], unit[1], unit[2])
+            elif unit[1] // 2 == unit[2]:
+                nc.sync.dma_start(out=out[unit[1] * P : (unit[1] + 1) * P, unit[2] * W : (unit[2] + 1) * W], in_=g_sb[unit][:])
+            elif unit[1] % 2:
+                store_square(g_sb["square", unit[1] // 2, unit[2]], unit[1] // 2, unit[2])
 
         nc.vector.memset(a_sc[:].bitcast(I32), 0)
-        for h in range(HALVES):
-            nc.vector.memset(b_sc[h][:].bitcast(I32), 0)
+        nc.vector.memset(b_sc_all[:].bitcast(I32), 0)
+        if WARM:
+            idle_codes = kt("idle_codes", [P, W], U32)
+            idle_sc = kt("idle_sc", [P, W], U8)
+            nc.vector.quantize_mx(out=idle_codes[:].bitcast(FP8X4), scales=idle_sc[:], in_=b_sc_all[:].bitcast(BF16))
+            idle = bank(7)
+            for k in range(WARM):
+                nc.tensor.matmul_mx(out=idle[:, 0:W], lhsT=idle_codes[:, 0:P].bitcast(FP8X4), lhsT_scale=idle_sc[:, 0:P], rhs=idle_codes[:].bitcast(FP8X4), rhs_scale=idle_sc[:], start=True, stop=True)
         nc.gpsimd.memset(d_rows[:], 0.0)
         nc.gpsimd.dma_start(out=d_rows[0:P:32, :].rearrange("q (b a) -> q b a", a=32), in_=d.rearrange("(b q a) -> q b a", q=4, a=32))
         nc.gpsimd.memset(ident_wide[:], 0.0)
         make_identity(nc, ident, nomemset=True)
 
-        load_scales(b_sc_raw, b_scales, range(4))
-        load_scales(a_sc, a_scales, range(2))
-        load_codes(b_raw[0], b_words, 0)
-        load_codes(a_codes[0], a_words, 0)
-        load_scales(a_sc, a_scales, range(2, 4))
-        for c in range(CHUNKS + 1):
-            if c < CHUNKS:
-                load_rows(w_raw[0, c], xw, c, 0, 512)
-                load_rows(x_first[c], x, c, 0, 2 * W)
-            if c == 0:
-                load_codes(a_codes[1], a_words, 1)
-                load_codes(b_raw[1], b_words, 1)
-            else:
-                load_rows(w_raw[1, c - 1], xw, c - 1, 512, 512)
-        for s in range(2, STAGES):
-            for c in range(CHUNKS):
-                load_rows(x_raw[s, c], x, c, s * W, W)
-
         last = CHUNKS - 1
+        for tok in LOADS.split():
+            if tok[0] == "s":
+                dst, src = (b_sc_raw, b_scales) if tok[1] == "B" else (a_sc, a_scales)
+                cols = slice(0, 1024) if tok[2] == "w" else slice(512 * int(tok[2]), 512 * int(tok[2]) + 512)
+                load_scales(dst, src, {"": range(4), "a": range(2), "b": range(2, 4)}[tok[3:]], cols)
+            elif tok[0] == "c":
+                dst, src = (b_raw, b_words) if tok[1] == "B" else (a_codes, a_words)
+                load_codes(dst[int(tok[2])], src, int(tok[2]))
+            else:
+                load_rows(tok[0], int(tok[1]), int(tok[2]), 2 if tok[3:] else 1)
 
-        def omega_run(first, n):
-            for k in range(first, first + n):
-                omega(k // 8, k % 8)
-                omega_out(k // 8, k % 8)
+        pe, vec, act, sp = [], [], [], []
+        def item_of(tok):
+            return (tok[1], int(tok[2]), int(tok[3]))
 
-        def supply(s, first):
-            for c in range(first, CHUNKS):
-                x_weave(s, c, "V")
-                if c:
-                    x_quant(s, c - 1)
-            x_quant(s, last)
-
-        sort_b_scales(0)
-        sort_b_codes(0)
-        sort_b_scales(1)
+        def span(tok):
+            return (int(tok[4]), int(tok[5])) if len(tok) > 4 else (0, 4)
 
         need = []
-        for c in range(CHUNKS + 1):
-            if c < CHUNKS:
-                need += [("W", 0, c), ("X", 0, c), ("X", 1, c)]
-            if c:
-                need += [("W", 1, c - 1)]
-        need += [("X", 2, 0)]
-        banks_before = {("X", 1, 0): 1, ("W", 1, 0): 7, ("X", 0, last): 8, ("X", 1, last): 0}
-        shared = [("W", 1, last - 1), ("W", 1, last)]
-        between = {
-            1: lambda: nc.vector.transpose(out=d_turned[:], in_=d_rows[:]),
-            2: lambda: (sort_b_codes(1), nc.vector.reciprocal(out=d_rec[:], in_=d_turned[:, 0:256:32])),
-            4: lambda: nc.vector.tensor_scalar(out=d_neg[:], in0=d_rec[:], scalar1=-1.0, scalar2=None, op0=ALU.mult),
-        }
-        done = 0
-        woven = []
-        for k, item in enumerate(need):
-            weave = w_weave if item[0] == "W" else x_weave
-            if k in between:
-                between[k]()
-            if item in banks_before:
-                omega_run(done, banks_before[item])
-                done += banks_before[item]
-                weave(*item[1:], "S")
-            else:
-                if item in shared:
-                    weave(*item[1:], "S", slice(2, 4))
-                    weave(*item[1:], "V", slice(0, 2))
-                else:
-                    weave(*item[1:], "V")
-                for kind, a, c in woven:
-                    (w_quant if kind == "W" else x_quant)(a, c)
-                woven = []
-            woven.append(item)
+        for tok in V_ORDER.split():
+            if tok[0] == "q" and item_of(tok) not in need:
+                need.append(item_of(tok))
+        tags = {it: "grp%d" % (k % GROUPS) for k, it in enumerate(need)}
+        frees = {it: [("q", need[k - GROUPS], u) for u in range(4)] if k >= GROUPS else [] for k, it in enumerate(need)}
 
-        for c in range(CHUNKS + 1):
-            for h in range(HALVES):
-                if 0 <= c - h < CHUNKS:
-                    for s in range(2):
-                        cov(s, c - h, h)
-        for h in range(HALVES):
+        def weave_step(tok, eng):
+            it, (lo, hi) = item_of(tok), span(tok)
+            return ([("weave", it, u) for u in range(lo, hi)], frees[it], lambda: weave(it, tags[it], eng, lo, hi))
+
+        def quant_step(tok):
+            it, (lo, hi) = item_of(tok), span(tok)
+            return ([("q", it, u) for u in range(lo, hi)], [("weave", it, u) for u in range(lo, hi)], lambda: quant(it, lo, hi))
+
+        held = {}
+
+        def take(k, n, names):
+            waits = []
+            for m in range(n):
+                waits += held.get(k + m, [])
+                held[k + m] = names[m]
+            return waits
+
+        def cov_step(s, c, h, k, n):
+            item, half = moving(s, c)
+            waits = [("q", ("W", h, c), u) for u in range(4)] + [("q", item, 2 * half), ("q", item, 2 * half + 1)]
+            if n == 0:
+                waits += take(k, 2, [[("out", "C", s, h, pair)] for pair in range(2)])
+            pe.append(([("mm", "C", s, n, h)], waits, lambda: cov(s, c, h, k, n)))
+
+        def omega_step(n, k):
+            h, b = divmod(n, 8)
+            pe.append(([("mm", "O", h, b)], [("sort", h), ("sortsc", h)] + take(k, 1, [[("out", "O", h, b)]]), lambda: omega(h, b, k)))
+
+        if EARLY:
             for s in range(2):
-                cov_out(s, h)
-        supply(2, 1)
-        supply(3, 0)
+                cov_step(s, 0, 0, 2 * s, 0)
+        for n in range(16):
+            omega_step(n, 4 + n % 4 if EARLY else n % 8)
+        seen = [EARLY, 0]
+        for tok in COV_ORDER.split()[EARLY:]:
+            c, h = int(tok[0]), int(tok[1])
+            for s in range(2):
+                cov_step(s, c, h, 4 * h + 2 * s, seen[h])
+            seen[h] += 1
         for s in range(2, STAGES):
             for c in range(CHUNKS):
                 for h in range(HALVES):
-                    cov(s, c, h)
-            for h in range(HALVES):
-                cov_out(s, h)
-        for s in range(STAGES):
-            for h in range(HALVES):
-                omega_quant(h, s)
-            if s < 3:
-                for h in range(HALVES):
-                    cov_quant(s, h)
+                    cov_step(s, c, h, 4 * (s - 2) + 2 * h, c)
+        units = [({"s": "square", "w": "wide", "m": "mirror", "r": "row"}[tok[0]],) + tuple(int(x) for x in tok[1:]) for tok in UNITS.split()]
+        for n, unit in enumerate(units):
+            if unit[0] == "mirror":
+                r, s = unit[1:]
+                waits = [("out", "wide", 2 * s), ("out", "wide", 2 * s + 1)] if s >= 2 and r < 2 else ([("out", "square", 1, 0)] if s == 1 else [("out", "row", 6, 2), ("out", "row", 7, 2)])
+            else:
+                top = unit[1] if unit[0] == "square" else unit[1] // 2
+                waits = [("q", kind, h, s) for kind in "OC" for h in range(HALVES) for s in range(top + 1)]
+            pe.append(([("mm",) + unit], waits + take(n % 8, 1, [[("out",) + unit] + ([("flip",) + unit] if unit in FLIPS else [])]), lambda unit=unit, n=n: g_make(unit, n % 8)))
 
-        square(1, 0)
-        square_out(1, 0, "V")
-        for b in range(4, 6):
-            wide(b)
-            wide_out(b, "V")
-        for h in range(HALVES):
-            cov_quant(3, h)
-        square(0, 0)
-        diag_out(0)
-        for r, s, eng in ((0, 1, "S"), (0, 2, "V"), (1, 2, "S")):
-            mirror(r, s)
-            mirror_out(r, s, eng)
-        for b in range(6, 8):
-            wide(b)
-            wide_out(b, "SV"[b % 2])
-        g = kt("g_square32", [P, 512], F32)
-        g_sb["square", 3, 2] = g
-        for e in range(2):
-            t = bank()
-            grad(t[:, 0:W], 6 + e, 2 * W, W)
-            copy("S", g[:, e * W : (e + 1) * W], t[:, 0:W])
-        store_square(g, 3, 2)
-        g = kt("g_diag1", [P, 512], F32)
-        diag_row(2, g[:, 0:W])
-        for r in range(3):
-            mirror(r, 3)
-            mirror_out(r, 3, "SVS"[r])
-        diag_row(3, g[:, W : 2 * W])
-        store_square(g, 1, 1)
-        square(2, 2)
-        diag_out(2)
-        for b in range(6, 8):
-            g = kt("g_last%d" % b, [P, W], F32)
-            diag_row(b, g[:])
-            nc.sync.dma_start(out=out[b * P : (b + 1) * P, 3 * W : 4 * W], in_=g[:])
+        extras = {
+            "s0": ([("sortsc", 0)], [], lambda: sort_b_scales(0)),
+            "s1": ([("sortsc", 1)], [], lambda: sort_b_scales(1)),
+            "c0": ([("sort", 0)], [], lambda: sort_b_codes(0)),
+            "c1": ([("sort", 1)], [], lambda: sort_b_codes(1)),
+            "d0": ([("d", 0)], [], lambda: nc.vector.transpose(out=d_turned[:], in_=d_rows[:])),
+            "d1": ([("d", 1)], [], lambda: nc.vector.reciprocal(out=d_rec[:], in_=d_turned[:, 0:256:32])),
+            "d2": ([("d", 2)], [], lambda: nc.vector.tensor_scalar(out=d_neg[:], in0=d_rec[:], scalar1=-1.0, scalar2=None, op0=ALU.mult)),
+        }
+        for eng, queue, order in (("V", vec, V_ORDER), ("S", act, S_ORDER)):
+            for tok in order.split():
+                if tok in extras:
+                    queue.append(extras[tok])
+                elif tok[0] == "o":
+                    h, b = divmod(int(tok[1:]), 8)
+                    queue.append(([("out", "O", h, b)], [("mm", "O", h, b)], lambda h=h, b=b, eng=eng: omega_out(h, b, eng)))
+                elif tok[0] == "k":
+                    s, h, pair = int(tok[1]), int(tok[2]), int(tok[3])
+                    queue.append(([("out", "C", s, h, pair)], [("mm", "C", s, last, h)], lambda s=s, h=h, pair=pair, eng=eng: cov_out(s, h, pair, eng)))
+                elif tok[0] in "OC":
+                    h, lo, hi = int(tok[1]), int(tok[2]), int(tok[3])
+                    waits = [("out", "O", h, b) for b in range(2 * lo, 2 * hi)] if tok[0] == "O" else [("out", "C", s, h, pair) for s in range(lo, hi) for pair in range(2)]
+                    queue.append(([("q", tok[0], h, s) for s in range(lo, hi)], waits, lambda tok=tok, h=h, lo=lo, hi=hi: result_quant(tok[0], h, lo, hi)))
+                elif tok[0] == "f":
+                    unit = units[int(tok[1:])]
+                    queue.append(([("flip",) + unit], [("mm",) + unit], lambda unit=unit: flip(unit)))
+                elif tok[0] == "g":
+                    unit = units[int(tok[1:])]
+                    queue.append(([("out",) + unit], [("mm",) + unit], lambda unit=unit, eng=eng: g_out(unit, eng)))
+                else:
+                    queue.append(quant_step(tok) if tok[0] == "q" else weave_step(tok, eng))
+        cut = len(pe) - len(units)
+        back = HALVES * (CHUNKS - G_AFTER)
+        pe[cut - back : cut + G_EARLY] = pe[cut : cut + G_EARLY] + pe[cut - back : cut]
+        for n, unit in enumerate(units):
+            sp.append(([], [("out",) + unit], lambda unit=unit: g_store(unit)))
+            if unit in FLIPS:
+                sp.append(([], [("flip",) + unit], lambda unit=unit: flip_store(unit)))
+
+        written = []
+        queues = [pe, vec, act, sp]
+        while any(queues):
+            moved = 0
+            for queue in queues:
+                while queue and all(w in written for w in queue[0][1]):
+                    name, waits, call = queue.pop(0)
+                    call()
+                    written.extend(name)
+                    moved += 1
+            assert moved

@@ -22,16 +22,18 @@ STAGES = 4
 W = 256
 EARLY = 0
 WARM = 8
-LOADS = "sBw cB0 sAwa cA0 sAwb W00 cA1 X00 cB1 W01+ X01 W10 W02 X02 W03+ X03 W12 Y20 Y21 Y22 Y23 Y30 Y31 Y32 Y33"
-V_ORDER = "s0 c0 s1 wW00 d0 qW00 d1 wX0002 c1 wX0024 d2 qX00 wW01 wX0102 qW01 wX0124 qX0102 wW10 qX0124 qW11 wW0202 qW10 wX0202 qW02 qX0202 wW0302 qX0224 wX0302 qW03 qX0302 wW1302 qX0324 wW1202 qW13 wY2002 qW12 wY2024 qY2002 wY2102 qY2024 wY2124 qY2102 wY3002 qY2124 wY3024 qY3002 wY31 qY3024 O002 qY31 O102 C002 C102 O024 O124 C023 C123 g0 g1 g2 C034 C134 g3 g5 g8 g11 g13 g15 g16 g17 g18"
-S_ORDER = "o0 o1 o2 o3 o4 o5 o6 o7 o8 o9 wW11 o10 o11 o12 o13 o14 o15 wW0224 wX0224 wW0324 wX0324 wW1324 wW1224 k000 k001 k100 k101 k010 k011 k110 k111 k200 k201 k210 k211 k300 k301 k310 k311 g4 g6 g7 g9 g10 g12 g14"
-COV_ORDER = "00 10 01 11 20 30 31 21"
+LOADS = "sBw cB0 sAwa cA0 sAwb W00 cA1 X00 cB1 W01 X01 W10 W02 X02 W11 W03+ X03 W12 X10a X11a X12a X13a X10b X11b X12b X13b"
+V_ORDER = "s0 c0 s1 wW00 qW00 wX0002 c1 wX0024 qX0002 wW01 qX0024 wX0102 qW01 wW1002 qX01 wW02 qW10 wX02 qW02 qX0202 wW1102 qX0224 wW0302 qW11 wX0302 qW03 qX0302 wW1302 qX0324 wW1202 qW13 wX1002 qW12 wX1102 qX1002 wX1202 qX1102 wX1302 qX1202 wX1024 qX1302 wX1124 qX1024 wX1224 qX1124 wX1324 qX1224 O002 qX1324 O102 C002 C102 O023 O123 C023 C123 k301 O034 O134 k311 C034 C134 d0 g3 d1 d2 g5 g7 g10 g12 g14 g15 g16 g17 g18"
+S_ORDER = "o0 o1 o2 o3 o4 o5 o6 o7 o8 wX0124 o9 o10 wW1024 o11 o12 o13 o14 o15 wW1124 wW0324 wX0324 wW1324 wW1224 k000 k001 k100 k101 k010 k011 k110 k111 k200 k201 k210 k211 k300 k310 g0 g1 g2 g4 g6 g8 g9 g11 g13"
+COV_ORDER = "00 10 01 20 11 30 31 21"
+NARROW = ((0, 0), (1, 0))
+NEI = 4
 ALIGN = 256
 G_EARLY = 0
 G_AFTER = 2
 GROUPS = 6
 FLIPS = ()
-UNITS = "s10 w4 w5 s00 m01 m02 m12 w6 w7 r62 r72 r21 m03 m13 m23 r31 s22 r63 r73"
+UNITS = "s10 w4 w5 w6 m01 m02 m12 w7 r62 r72 r00 m03 m13 m23 r10 s11 s22 r63 r73"
 
 
 def tile_concord_precision_gradient_s12_kernel(tc, a_words, a_scales, b_words, b_scales, xw, x, d, out):
@@ -62,7 +64,7 @@ def tile_concord_precision_gradient_s12_kernel(tc, a_words, a_scales, b_words, b
         b_sc_raw = kt("b_sc_raw", [P, 2, 1024], U8)
         b_sc_all = kt("b_sc", [P, HALVES * 1024], U8)
         b_sc = [b_sc_all[:, h * 1024 : (h + 1) * 1024].rearrange("p (g n) -> p g n", g=2) for h in range(HALVES)]
-        names = [("W", h, c) for h in range(HALVES) for c in range(CHUNKS)] + [("X", 0, c) for c in range(CHUNKS)] + [("Y", s, k) for s in range(2, STAGES) for k in range(2)]
+        names = [(kind, h, c) for kind in "WX" for h in range(HALVES) for c in range(CHUNKS)]
         codes = {it: kt("codes%s%d%d" % it, [P, 512], U32) for it in names}
         scales = {it: kt("scales%s%d%d" % it, [P, 512], U8) for it in names}
         o_codes = [kt("o_codes%d" % h, [P, 1024], U32) for h in range(HALVES)]
@@ -98,19 +100,14 @@ def tile_concord_precision_gradient_s12_kernel(tc, a_words, a_scales, b_words, b
         def result(name, width):
             return kt(name, [P, width], F32, spent.pop(0) if spent else name)
 
-        def load_rows(kind, first, c, n):
-            rows = slice(c * 512, (c + 1) * 512)
-            if kind == "Y":
-                if c % 2 == 0:
-                    raw["Y", first, c // 2] = loaded("rawY%d%d" % (first, c), [P, 2, SLOTS, W])
-                dst = raw["Y", first, c // 2][:, c % 2]
-                src = x[rows, first * W : (first + 1) * W]
-            else:
-                dst = loaded("raw%s%d%d" % (kind, first, c), [P, SLOTS, n * 512])[:]
+        def load_rows(kind, first, c, n, lo, hi):
+            if lo == 0:
+                t = loaded("raw%s%d%d" % (kind, first, c), [P, SLOTS, n * 512])
                 for k in range(n):
-                    raw[kind, first + k, c] = dst[:, :, k * 512 : (k + 1) * 512]
-                src = (xw if kind == "W" else x)[rows, first * 512 : (first + n) * 512]
-            nc.sync.dma_start(out=dst, in_=src.rearrange("(p j) w -> p j w", j=SLOTS))
+                    raw[kind, first + k, c] = t[:, :, k * 512 : (k + 1) * 512]
+                raw["whole", kind, first, c] = t
+            src = (xw if kind == "W" else x)[c * 512 : (c + 1) * 512, first * 512 + lo : first * 512 + hi]
+            nc.sync.dma_start(out=raw["whole", kind, first, c][:, :, lo:hi], in_=src.rearrange("(p j) w -> p j w", j=SLOTS))
 
         def sort_b_scales(h):
             cols = slice(h * 512, (h + 1) * 512)
@@ -158,43 +155,46 @@ def tile_concord_precision_gradient_s12_kernel(tc, a_words, a_scales, b_words, b
             if kind == "W":
                 dst = grp[item][:].rearrange("p (u s w j) -> p u s j w", u=4, s=32, w=4)[:, lo:hi]
                 src = raw[item].rearrange("p j (s u w) -> p u s j w", u=4, w=4)[:, lo:hi]
-            elif kind == "X":
-                dst = grp[item][:].rearrange("p (a w j) -> p a j w", w=4, j=4)[:, 32 * lo : 32 * hi]
-                src = raw[item].rearrange("p j (a w) -> p a j w", w=4)[:, 32 * lo : 32 * hi]
+                if NEI == 1:
+                    dst = grp[item][:].rearrange("p (u s w j) -> p u s w j", u=4, s=32, w=4)[:, lo:hi]
+                    src = raw[item].rearrange("p j (s u w) -> p u s w j", u=4, w=4)[:, lo:hi]
             else:
-                dst = grp[item][:].rearrange("p (e a w j) -> p e a j w", e=2, w=4, j=4)
-                src = raw[item][:].rearrange("p e j (a w) -> p e a j w", w=4)
-                if hi - lo < 4:
-                    part = slice(32 * (lo % 2), 32 * (lo % 2 + hi - lo))
-                    dst, src = dst[:, lo // 2, part], src[:, lo // 2, part]
+                dst = grp[item][:].rearrange("p (a w j) -> p a j w", w=NEI, j=4)[:, 128 // NEI * lo : 128 // NEI * hi]
+                src = raw[item].rearrange("p j (a w) -> p a j w", w=NEI)[:, 128 // NEI * lo : 128 // NEI * hi]
             copy(eng, dst, src)
 
         def quant(item, lo, hi):
             nc.vector.quantize_mx(out=codes[item][:, lo * P : hi * P].bitcast(FP8X4), scales=scales[item][:, lo * P : hi * P], in_=grp[item][:, lo * 512 : hi * 512])
 
         def moving(s, c):
-            return (("X", 0, c), s) if s < 2 else (("Y", s, c // 2), c % 2)
+            return ("X", s // 2, c), s % 2
 
         def cov(s, c, h, k, n):
             item, half = moving(s, c)
-            cols = slice(half * W, (half + 1) * W)
-            for pair in range(2):
+            narrow = (s, h) in NARROW
+            for z in range(2):
                 if n == 0:
-                    ps["C", s, h, pair] = bank(k + pair)
-                for e in range(2):
-                    u = 2 * pair + e
+                    ps["C", s, h, z] = bank(k + z)
+                slots = range(SLOTS) if narrow else range(2 * z, 2 * z + 2)
+                width = P if narrow else W
+                lo = half * W + (z * P if narrow else 0)
+                for e, u in enumerate(slots):
                     nc.tensor.matmul_mx(
-                        out=ps["C", s, h, pair][:, e * W : (e + 1) * W],
+                        out=ps["C", s, h, z][:, e * width : (e + 1) * width],
                         lhsT=codes["W", h, c][:, u * P : (u + 1) * P].bitcast(FP8X4),
                         lhsT_scale=scales["W", h, c][:, u * P : (u + 1) * P],
-                        rhs=codes[item][:, cols].bitcast(FP8X4),
-                        rhs_scale=scales[item][:, cols],
+                        rhs=codes[item][:, lo : lo + width].bitcast(FP8X4),
+                        rhs_scale=scales[item][:, lo : lo + width],
                         start=(n == 0 and e == 0),
-                        stop=(n == CHUNKS - 1 and e == 1),
+                        stop=(n == CHUNKS - 1 and e == len(slots) - 1),
                     )
 
-        def cov_out(s, h, pair, eng):
-            copy(eng, c_grp[h, s // 2][:, (s % 2) * W : (s % 2 + 1) * W, 2 * pair : 2 * pair + 2], ps["C", s, h, pair][:].rearrange("p (u n) -> p n u", u=2))
+        def cov_out(s, h, z, eng):
+            lo = (s % 2) * W
+            if (s, h) in NARROW:
+                copy(eng, c_grp[h, s // 2][:, lo + z * P : lo + (z + 1) * P, :], ps["C", s, h, z][:].rearrange("p (u n) -> p n u", u=SLOTS))
+            else:
+                copy(eng, c_grp[h, s // 2][:, lo : lo + W, 2 * z : 2 * z + 2], ps["C", s, h, z][:].rearrange("p (u n) -> p n u", u=2))
 
         def grad(dst, b, lo, n):
             rows = slice(b * P, (b + 1) * P)
@@ -306,7 +306,7 @@ def tile_concord_precision_gradient_s12_kernel(tc, a_words, a_scales, b_words, b
                 dst, src = (b_raw, b_words) if tok[1] == "B" else (a_codes, a_words)
                 load_codes(dst[int(tok[2])], src, int(tok[2]))
             else:
-                load_rows(tok[0], int(tok[1]), int(tok[2]), 2 if tok[3:] else 1)
+                load_rows(tok[0], int(tok[1]), int(tok[2]), 2 if tok[3:] == "+" else 1, *{"": (0, 512), "+": (0, 1024), "a": (0, W), "b": (W, 512)}[tok[3:]])
 
         pe, vec, act, sp = [], [], [], []
         def item_of(tok):

@@ -26,7 +26,7 @@ LOADS = "sBw cB0 sAwa cA0 sAwb W00 cA1 X00 cB1 W01 X01 W10 W02 X02 W11 W03+ X03 
 V_ORDER = "s0 c0 s1 wW00 qW00 wX0002 c1 wX0024 qX0002 wW01 qX0024 wX0102 qW01 wW1002 qX01 wW02 qW10 wX02 qW02 qX0202 wW1102 qX0224 wW0302 qW11 wX0302 qW03 qX0302 wW1302 qX0324 wW1202 qW13 wX1002 qW12 wX1102 qX1002 wX1202 qX1102 wX1302 qX1202 wX1024 qX1302 wX1124 qX1024 wX1224 qX1124 wX1324 qX1224 O002 qX1324 O102 C002 C102 O023 O123 C023 C123 k301 O034 O134 k311 C034 C134 d0 g3 d1 d2 g5 g7 g10 g12 g14 g15 g16 g17 g18"
 S_ORDER = "o0 o1 o2 o3 o4 o5 o6 o7 o8 wX0124 o9 o10 wW1024 o11 o12 o13 o14 o15 wW1124 wW0324 wX0324 wW1324 wW1224 k000 k001 k100 k101 k010 k011 k110 k111 k200 k201 k210 k211 k300 k310 g0 g1 g2 g4 g6 g8 g9 g11 g13"
 COV_ORDER = "00 10 01 20 11 30 31 21"
-NARROW = ((0, 0), (1, 0))
+NARROW = ()
 NEI = 4
 ALIGN = 256
 G_EARLY = 0

@@ -27,10 +27,10 @@ V_ORDER = "s0 c0 s1 wW00 qW00 wX0002 c1 wX0024 qX0002 wW01 qX0024 wX0102 qW01 wW
 S_ORDER = "o0 o1 o2 o3 o4 o5 o6 o7 o8 wX0124 o9 o10 wW1024 o11 o12 o13 o14 o15 wW1124 wW0324 wX0324 wW1324 wW1224 k000 k001 k100 k101 k010 k011 k110 k111 k200 k201 k210 k211 k300 k310 g0 g1 g2 g4 g6 g8 g9 g11 g13"
 COV_ORDER = "00 10 01 20 11 30 31 21"
 NARROW = ()
-NEI = 4
+NEI = 8
+RUN = 8
 ALIGN = 256
-G_EARLY = 0
-G_AFTER = 2
+PE_TAIL = "c20 c21 c22 c23 c30 c31 c32 c33 0 1 2 3 4 5 6 7 0 1 2 3 4 5 6 7 0 1 2"
 GROUPS = 6
 FLIPS = ()
 UNITS = "s10 w4 w5 w6 m01 m02 m12 w7 r62 r72 r00 m03 m13 m23 r10 s11 s22 r63 r73"
@@ -114,14 +114,14 @@ def tile_concord_precision_gradient_s12_kernel(tc, a_words, a_scales, b_words, b
             for q in range(4):
                 rows = slice(32 * q, 32 * q + 4)
                 nc.vector.tensor_copy(
-                    out=b_sc[h][rows].bitcast(I32).rearrange("p g (u s) -> p g u s", u=4),
-                    in_=b_sc_raw[rows, :, cols].bitcast(I32).rearrange("p g (s u) -> p g u s", u=4),
+                    out=b_sc[h][rows].bitcast(I32).rearrange("p g (u s w) -> p g u s w", u=4, w=RUN // 4),
+                    in_=b_sc_raw[rows, :, cols].bitcast(I32).rearrange("p g (s u w) -> p g u s w", u=4, w=RUN // 4),
                 )
 
         def sort_b_codes(h):
             nc.vector.tensor_copy(
-                out=b_codes[h][:].bitcast(I32).rearrange("p g (u s w) -> p g u s w", u=4, w=2),
-                in_=b_raw[h][:].bitcast(I32).rearrange("p g (s u w) -> p g u s w", u=4, w=2),
+                out=b_codes[h][:].bitcast(I32).rearrange("p g (u s w) -> p g u s w", u=4, w=RUN // 2),
+                in_=b_raw[h][:].bitcast(I32).rearrange("p g (s u w) -> p g u s w", u=4, w=RUN // 2),
             )
 
         def omega(h, b, k):
@@ -153,11 +153,8 @@ def tile_concord_precision_gradient_s12_kernel(tc, a_words, a_scales, b_words, b
             if item not in grp:
                 grp[item] = kt("grp%s%d%d" % item, [P, 2048], BF16, tag)
             if kind == "W":
-                dst = grp[item][:].rearrange("p (u s w j) -> p u s j w", u=4, s=32, w=4)[:, lo:hi]
-                src = raw[item].rearrange("p j (s u w) -> p u s j w", u=4, w=4)[:, lo:hi]
-                if NEI == 1:
-                    dst = grp[item][:].rearrange("p (u s w j) -> p u s w j", u=4, s=32, w=4)[:, lo:hi]
-                    src = raw[item].rearrange("p j (s u w) -> p u s w j", u=4, w=4)[:, lo:hi]
+                dst = grp[item][:].rearrange("p (u s w j) -> p u s j w", u=4, w=RUN, j=4)[:, lo:hi]
+                src = raw[item].rearrange("p j (s u w) -> p u s j w", u=4, w=RUN)[:, lo:hi]
             else:
                 dst = grp[item][:].rearrange("p (a w j) -> p a j w", w=NEI, j=4)[:, 128 // NEI * lo : 128 // NEI * hi]
                 src = raw[item].rearrange("p j (a w) -> p a j w", w=NEI)[:, 128 // NEI * lo : 128 // NEI * hi]
@@ -361,19 +358,25 @@ def tile_concord_precision_gradient_s12_kernel(tc, a_words, a_scales, b_words, b
             for s in range(2):
                 cov_step(s, c, h, 4 * h + 2 * s, seen[h])
             seen[h] += 1
-        for s in range(2, STAGES):
-            for c in range(CHUNKS):
-                for h in range(HALVES):
-                    cov_step(s, c, h, 4 * (s - 2) + 2 * h, c)
         units = [({"s": "square", "w": "wide", "m": "mirror", "r": "row"}[tok[0]],) + tuple(int(x) for x in tok[1:]) for tok in UNITS.split()]
-        for n, unit in enumerate(units):
+        def unit_step(n, k):
+            unit = units[n]
             if unit[0] == "mirror":
                 r, s = unit[1:]
                 waits = [("out", "wide", 2 * s), ("out", "wide", 2 * s + 1)] if s >= 2 and r < 2 else ([("out", "square", 1, 0)] if s == 1 else [("out", "row", 6, 2), ("out", "row", 7, 2)])
             else:
                 top = unit[1] if unit[0] == "square" else unit[1] // 2
                 waits = [("q", kind, h, s) for kind in "OC" for h in range(HALVES) for s in range(top + 1)]
-            pe.append(([("mm",) + unit], waits + take(n % 8, 1, [[("out",) + unit] + ([("flip",) + unit] if unit in FLIPS else [])]), lambda unit=unit, n=n: g_make(unit, n % 8)))
+            pe.append(([("mm",) + unit], waits + take(k, 1, [[("out",) + unit] + ([("flip",) + unit] if unit in FLIPS else [])]), lambda: g_make(unit, k)))
+
+        n = 0
+        for tok in PE_TAIL.split():
+            if tok[0] == "c":
+                for h in range(HALVES):
+                    cov_step(int(tok[1]), int(tok[2]), h, 4 * (int(tok[1]) - 2) + 2 * h, int(tok[2]))
+            else:
+                unit_step(n, int(tok))
+                n += 1
 
         extras = {
             "s0": ([("sortsc", 0)], [], lambda: sort_b_scales(0)),
@@ -406,9 +409,6 @@ def tile_concord_precision_gradient_s12_kernel(tc, a_words, a_scales, b_words, b
                     queue.append(([("out",) + unit], [("mm",) + unit], lambda unit=unit, eng=eng: g_out(unit, eng)))
                 else:
                     queue.append(quant_step(tok) if tok[0] == "q" else weave_step(tok, eng))
-        cut = len(pe) - len(units)
-        back = HALVES * (CHUNKS - G_AFTER)
-        pe[cut - back : cut + G_EARLY] = pe[cut : cut + G_EARLY] + pe[cut - back : cut]
         for n, unit in enumerate(units):
             sp.append(([], [("out",) + unit], lambda unit=unit: g_store(unit)))
             if unit in FLIPS:

@@ -22,11 +22,12 @@ STAGES = 4
 W = 256
 EARLY = 0
 WARM = 8
-LOADS = "sBw cB0 sAwa cA0 sAwb W00 cA1 X00 cB1 W01 X01 W10 W02 X02 W11 W03+ X03 W12 X10a X11a X12a X13a X10b X11b X12b X13b"
-V_ORDER = "s0 c0 s1 wW00 qW00 wX0002 c1 wX0024 qX0002 wW01 qX0024 wX0102 qW01 wW1002 qX01 wW02 qW10 wX02 qW02 qX0202 wW1102 qX0224 wW0302 qW11 wX0302 qW03 qX0302 wW1302 qX0324 wW1202 qW13 wX1002 qW12 wX1102 qX1002 wX1202 qX1102 wX1302 qX1202 wX1024 qX1302 wX1124 qX1024 wX1224 qX1124 wX1324 qX1224 O002 qX1324 O102 C002 C102 O023 O123 C023 C123 k301 O034 O134 k311 C034 C134 d0 g3 d1 d2 g5 g7 g10 g12 g14 g15 g16 g17 g18"
-S_ORDER = "o0 o1 o2 o3 o4 o5 o6 o7 o8 wX0124 o9 o10 wW1024 o11 o12 o13 o14 o15 wW1124 wW0324 wX0324 wW1324 wW1224 k000 k001 k100 k101 k010 k011 k110 k111 k200 k201 k210 k211 k300 k310 g0 g1 g2 g4 g6 g8 g9 g11 g13"
-COV_ORDER = "00 10 01 20 11 30 31 21"
+LOADS = "sBw cB0 sAwa cA0 sAwb W00 cA1 X00 cB1 W01+ X01 W02+ X02 W03+ X03 W10 X10a X11a X12a X13a X10b X11b X12b X13b"
+V_ORDER = "s0 c0 s1 wW00 qW00 wX0002 c1 wX0024 qX0002 qX0024 wW01 wW1102 qW01 wX0102 qW11 qX0102 wW02 qX0124 wW12 qW02 wX0202 qW12 qX0202 wW0302 qX0224 wW1302 wX0302 qW03 qX0302 qX0324 wW1002 qW13 wX1002 qW10 wX1102 qX1002 wX1202 qX1102 wX1302 qX1202 wX1024 qX1302 wX1124 qX1024 wX1224 qX1124 wX1324 qX1224 O002 qX1324 O102 C002 C102 O023 O123 C023 C123 k301 O034 O134 k311 C034 C134 d0 g3 d1 d2 g5 g7 g10 g12 g14 g15 g16 g17 g18"
+S_ORDER = "o0 o1 o2 o3 o4 o5 o6 o7 wW1124 o8 o9 wX0124 o10 o11 o12 o13 o14 o15 wX0224 wW0324 wX0324 wW1324 wW1024 k000 k001 k100 k101 k010 k011 k110 k111 k200 k201 k210 k211 k300 k310 g0 g1 g2 g4 g6 g8 g9 g11 g13"
+COV_ORDER = "00 10 11 20 21 30 31 01"
 NARROW = ()
+PAIR = 2
 NEI = 8
 RUN = 8
 ALIGN = 256
@@ -141,7 +142,7 @@ def tile_concord_precision_gradient_s12_kernel(tc, a_words, a_scales, b_words, b
 
         def omega_out(h, b, eng):
             lo = (b % 4) * P
-            copy(eng, o_grp[h, b // 4][:, lo : lo + P, :], ps["O", h, b][:].rearrange("p (u n) -> p n u", u=SLOTS))
+            copy(eng, o_grp[h, b // 4][:, lo : lo + P, :].rearrange("p (n e) u -> p n u e", e=PAIR), ps["O", h, b][:].rearrange("p (u n e) -> p n u e", u=SLOTS, e=PAIR))
 
         def result_quant(kind, h, lo, hi):
             dst, sc, src = (o_codes, o_sc, o_grp) if kind == "O" else (c_codes, c_sc, c_grp)
@@ -189,9 +190,9 @@ def tile_concord_precision_gradient_s12_kernel(tc, a_words, a_scales, b_words, b
         def cov_out(s, h, z, eng):
             lo = (s % 2) * W
             if (s, h) in NARROW:
-                copy(eng, c_grp[h, s // 2][:, lo + z * P : lo + (z + 1) * P, :], ps["C", s, h, z][:].rearrange("p (u n) -> p n u", u=SLOTS))
+                copy(eng, c_grp[h, s // 2][:, lo + z * P : lo + (z + 1) * P, :].rearrange("p (n e) u -> p n u e", e=PAIR), ps["C", s, h, z][:].rearrange("p (u n e) -> p n u e", u=SLOTS, e=PAIR))
             else:
-                copy(eng, c_grp[h, s // 2][:, lo : lo + W, 2 * z : 2 * z + 2], ps["C", s, h, z][:].rearrange("p (u n) -> p n u", u=2))
+                copy(eng, c_grp[h, s // 2][:, lo : lo + W, 2 * z : 2 * z + 2].rearrange("p (n e) u -> p n u e", e=PAIR), ps["C", s, h, z][:].rearrange("p (u n e) -> p n u e", u=2, e=PAIR))
 
         def grad(dst, b, lo, n):
             rows = slice(b * P, (b + 1) * P)

@@ -18,23 +18,15 @@ P = 128
 HALVES = 2
 SLOTS = 4
 CHUNKS = 4
-STAGES = 4
-W = 256
-EARLY = 0
-WARM = 8
-LOADS = "sBw cB0 sAwa cA0 sAwb W00 cA1 X00 cB1 W01+ X01 W02+ X02 W03+ X03 W10 X10a X11a X12a X13a X10b X11b X12b X13b"
-V_ORDER = "s0 c0 s1 wW00 qW00 wX0002 c1 wX0024 qX0002 qX0024 wW01 wW1102 qW01 wX0102 qW11 qX0102 wW02 qX0124 wW12 qW02 wX0202 qW12 qX0202 wW0302 qX0224 wW1302 wX0302 qW03 qX0302 qX0324 wW1002 qW13 wX1002 qW10 wX1102 qX1002 wX1202 qX1102 wX1302 qX1202 wX1024 qX1302 wX1124 qX1024 wX1224 qX1124 wX1324 qX1224 O002 qX1324 O102 C002 C102 O023 O123 C023 C123 k301 O034 O134 k311 C034 C134 d0 g3 d1 d2 g5 g7 g10 g12 g14 g15 g16 g17 g18"
-S_ORDER = "o0 o1 o2 o3 o4 o5 o6 o7 wW1124 o8 o9 wX0124 o10 o11 o12 o13 o14 o15 wX0224 wW0324 wX0324 wW1324 wW1024 k000 k001 k100 k101 k010 k011 k110 k111 k200 k201 k210 k211 k300 k310 g0 g1 g2 g4 g6 g8 g9 g11 g13"
-COV_ORDER = "00 10 11 20 21 30 31 01"
-NARROW = ()
-PAIR = 2
-NEI = 8
+LAST = CHUNKS - 1
+BLOCKS = 4
+WIDTH = 256
 RUN = 8
-ALIGN = 256
-PE_TAIL = "c20 c21 c22 c23 c30 c31 c32 c33 0 1 2 3 4 5 6 7 0 1 2 3 4 5 6 7 0 1 2"
-GROUPS = 6
-FLIPS = ()
-UNITS = "s10 w4 w5 w6 m01 m02 m12 w7 r62 r72 r00 m03 m13 m23 r10 s11 s22 r63 r73"
+BANKS = 8
+WARM_UPS = 8
+WOVEN_TILES = 6
+BANKS_BEFORE_XW, BANKS_BEFORE_X = 8, 10
+WHOLE, FIRST, SECOND = (0, 4), (0, 2), (2, 4)
 
 
 def tile_concord_precision_gradient_s12_kernel(tc, a_words, a_scales, b_words, b_scales, xw, x, d, out):
@@ -44,8 +36,8 @@ def tile_concord_precision_gradient_s12_kernel(tc, a_words, a_scales, b_words, b
         psum = ctx.enter_context(tc.psum_pool(name="psum", bufs=1))
         ctx.enter_context(tc.manual_schedule())
 
-        def kt(name, shape, dt, tag=None):
-            t = keep.tile(shape, dt, name=name, tag=tag or name, align_bytes=ALIGN)
+        def sbuf(name, shape, dt, tag=None):
+            t = keep.tile(shape, dt, name=name, tag=tag or name, align_bytes=256)
             return t
 
         def bank(k):
@@ -58,75 +50,85 @@ def tile_concord_precision_gradient_s12_kernel(tc, a_words, a_scales, b_words, b
             else:
                 nc.vector.tensor_copy(out=dst, in_=src)
 
-        a_codes = [kt("a_codes%d" % q, [P, 2, 1024], U8) for q in range(2)]
-        a_sc = kt("a_sc", [P, 2, 1024], U8)
-        b_raw = [kt("b_raw%d" % h, [P, 2, 1024], U8) for h in range(HALVES)]
-        b_codes = [kt("b_codes%d" % h, [P, 2, 1024], U8) for h in range(HALVES)]
-        b_sc_raw = kt("b_sc_raw", [P, 2, 1024], U8)
-        b_sc_all = kt("b_sc", [P, HALVES * 1024], U8)
+        a_codes = [sbuf("a_codes%d" % q, [P, 2, 1024], U8) for q in range(2)]
+        a_sc = sbuf("a_sc", [P, 2, 1024], U8)
+        b_raw = [sbuf("b_raw%d" % h, [P, 2, 1024], U8) for h in range(HALVES)]
+        b_codes = [sbuf("b_codes%d" % h, [P, 2, 1024], U8) for h in range(HALVES)]
+        b_sc_raw = sbuf("b_sc_raw", [P, 2, 1024], U8)
+        b_sc_all = sbuf("b_sc", [P, HALVES * 1024], U8)
         b_sc = [b_sc_all[:, h * 1024 : (h + 1) * 1024].rearrange("p (g n) -> p g n", g=2) for h in range(HALVES)]
-        names = [(kind, h, c) for kind in "WX" for h in range(HALVES) for c in range(CHUNKS)]
-        codes = {it: kt("codes%s%d%d" % it, [P, 512], U32) for it in names}
-        scales = {it: kt("scales%s%d%d" % it, [P, 512], U8) for it in names}
-        o_codes = [kt("o_codes%d" % h, [P, 1024], U32) for h in range(HALVES)]
-        o_sc = [kt("o_sc%d" % h, [P, 1024], U8) for h in range(HALVES)]
-        c_codes = [kt("c_codes%d" % h, [P, 1024], U32) for h in range(HALVES)]
-        c_sc = [kt("c_sc%d" % h, [P, 1024], U8) for h in range(HALVES)]
-        o_grp = {(h, z): kt("o_grp%d%d" % (h, z), [P, 2 * W, SLOTS], BF16) for h in range(HALVES) for z in range(2)}
-        c_grp = {(h, z): kt("c_grp%d%d" % (h, z), [P, 2 * W, SLOTS], BF16) for h in range(HALVES) for z in range(2)}
-        ident_wide = kt("ident_wide", [P, 3 * P], F32)
+        tiles = [(kind, z, c) for kind in "WX" for z in range(2) for c in range(CHUNKS)]
+        codes = {it: sbuf("codes%s%d%d" % it, [P, 512], U32) for it in tiles}
+        scales = {it: sbuf("scales%s%d%d" % it, [P, 512], U8) for it in tiles}
+        o_codes = [sbuf("o_codes%d" % h, [P, 1024], U32) for h in range(HALVES)]
+        o_sc = [sbuf("o_sc%d" % h, [P, 1024], U8) for h in range(HALVES)]
+        c_codes = [sbuf("c_codes%d" % h, [P, 1024], U32) for h in range(HALVES)]
+        c_sc = [sbuf("c_sc%d" % h, [P, 1024], U8) for h in range(HALVES)]
+        o_words = {(h, z): sbuf("o_words%d%d" % (h, z), [P, 512, SLOTS], BF16) for h in range(HALVES) for z in range(2)}
+        c_words = {(h, z): sbuf("c_words%d%d" % (h, z), [P, 512, SLOTS], BF16) for h in range(HALVES) for z in range(2)}
+        ident_wide = sbuf("ident_wide", [P, 3 * P], F32)
         ident = ident_wide[:, P : 2 * P]
-        d_rows = kt("d_rows", [P, 256], BF16)
-        d_turned = kt("d_turned", [P, 256], BF16)
-        d_rec = kt("d_rec", [P, 8], F32)
-        d_neg = kt("d_neg", [P, 8], F32)
-        raw = {}
-        grp = {}
-        ps = {}
-        g_sb = {}
+        d_rows = sbuf("d_rows", [P, 256], BF16)
+        d_turned = sbuf("d_turned", [P, 256], BF16)
+        d_rec = sbuf("d_rec", [P, 8], F32)
+        d_neg = sbuf("d_neg", [P, 8], F32)
+        raw, woven, ps, g_sb, spent = {}, {}, {}, {}, []
 
-        def load_codes(dst, src, h):
-            nc.sync.dma_start(out=dst[:].bitcast(I32), in_=src[:, :, h * 1024 : (h + 1) * 1024].bitcast(I32).rearrange("g p n -> p g n"))
+        def load_codes(dst, src, z):
+            nc.sync.dma_start(out=dst[:].bitcast(I32), in_=src[:, :, z * 1024 : (z + 1) * 1024].bitcast(I32).rearrange("g p n -> p g n"))
 
-        def load_scales(dst, src, rows, cols):
+        def load_scales(dst, src, rows):
             for r in rows:
-                nc.sync.dma_start(out=dst[r:P:32, :, cols].bitcast(I32), in_=src[:, r:16:4, cols].bitcast(I32).rearrange("g q n -> q g n"))
+                nc.sync.dma_start(out=dst[r:P:32, :, :].bitcast(I32), in_=src[:, r:16:4, :].bitcast(I32).rearrange("g q n -> q g n"))
 
-        spent = []
-
-        def loaded(name, shape):
-            spent.append(name)
-            return kt(name, shape, BF16)
-
-        def result(name, width):
-            return kt(name, [P, width], F32, spent.pop(0) if spent else name)
-
-        def load_rows(kind, first, c, n, lo, hi):
-            if lo == 0:
-                t = loaded("raw%s%d%d" % (kind, first, c), [P, SLOTS, n * 512])
-                for k in range(n):
-                    raw[kind, first + k, c] = t[:, :, k * 512 : (k + 1) * 512]
-                raw["whole", kind, first, c] = t
-            src = (xw if kind == "W" else x)[c * 512 : (c + 1) * 512, first * 512 + lo : first * 512 + hi]
-            nc.sync.dma_start(out=raw["whole", kind, first, c][:, :, lo:hi], in_=src.rearrange("(p j) w -> p j w", j=SLOTS))
+        def load_rows(kind, c, lo, hi):
+            first = lo // 512
+            if lo % 512 == 0:
+                count = max(1, (hi - lo) // 512)
+                name = "raw%s%d%d" % (kind, first, c)
+                spent.append(name)
+                raw["load", kind, first, c] = sbuf(name, [P, SLOTS, count * 512], BF16)
+                for k in range(count):
+                    raw[kind, first + k, c] = raw["load", kind, first, c][:, :, k * 512 : (k + 1) * 512]
+            src = (xw if kind == "W" else x)[c * 512 : (c + 1) * 512, lo:hi]
+            nc.sync.dma_start(out=raw["load", kind, first, c][:, :, lo - first * 512 : hi - first * 512], in_=src.rearrange("(p t) w -> p t w", t=SLOTS))
 
         def sort_b_scales(h):
             cols = slice(h * 512, (h + 1) * 512)
-            for q in range(4):
-                rows = slice(32 * q, 32 * q + 4)
+            for quadrant in range(4):
+                rows = slice(32 * quadrant, 32 * quadrant + 4)
                 nc.vector.tensor_copy(
-                    out=b_sc[h][rows].bitcast(I32).rearrange("p g (u s w) -> p g u s w", u=4, w=RUN // 4),
-                    in_=b_sc_raw[rows, :, cols].bitcast(I32).rearrange("p g (s u w) -> p g u s w", u=4, w=RUN // 4),
+                    out=b_sc[h][rows].bitcast(I32).rearrange("p g (u q w) -> p g u q w", u=SLOTS, w=RUN // 4),
+                    in_=b_sc_raw[rows, :, cols].bitcast(I32).rearrange("p g (q u w) -> p g u q w", u=SLOTS, w=RUN // 4),
                 )
 
         def sort_b_codes(h):
             nc.vector.tensor_copy(
-                out=b_codes[h][:].bitcast(I32).rearrange("p g (u s w) -> p g u s w", u=4, w=RUN // 2),
-                in_=b_raw[h][:].bitcast(I32).rearrange("p g (s u w) -> p g u s w", u=4, w=RUN // 2),
+                out=b_codes[h][:].bitcast(I32).rearrange("p g (u q w) -> p g u q w", u=SLOTS, w=RUN // 2),
+                in_=b_raw[h][:].bitcast(I32).rearrange("p g (q u w) -> p g u q w", u=SLOTS, w=RUN // 2),
             )
 
-        def omega(h, b, k):
-            t = bank(k)
+        def weave(it, tag, eng, part):
+            lo, hi = part
+            if it not in woven:
+                woven[it] = sbuf("woven%s%d%d" % it, [P, 2048], BF16, tag)
+            if it[0] == "W":
+                dst = woven[it][:].rearrange("p (u q w t) -> p u q t w", u=SLOTS, w=RUN, t=SLOTS)[:, lo:hi]
+                src = raw[it].rearrange("p t (q u w) -> p u q t w", u=SLOTS, w=RUN)[:, lo:hi]
+            else:
+                dst = woven[it][:].rearrange("p (a w t) -> p a t w", w=RUN, t=SLOTS)[:, P // RUN * lo : P // RUN * hi]
+                src = raw[it].rearrange("p t (a w) -> p a t w", w=RUN)[:, P // RUN * lo : P // RUN * hi]
+            copy(eng, dst, src)
+
+        def quantise(it, part):
+            lo, hi = part
+            nc.vector.quantize_mx(out=codes[it][:, lo * P : hi * P].bitcast(FP8X4), scales=scales[it][:, lo * P : hi * P], in_=woven[it][:, lo * 512 : hi * 512])
+
+        def slots_out(eng, dst, src, count):
+            copy(eng, dst.rearrange("p (n e) u -> p n u e", e=2), src[:].rearrange("p (u n e) -> p n u e", u=count, e=2))
+
+        def omega(h, b):
+            t = bank(b)
             ps["O", h, b] = t
             for u in range(SLOTS):
                 for g in range(2):
@@ -140,65 +142,49 @@ def tile_concord_precision_gradient_s12_kernel(tc, a_words, a_scales, b_words, b
                         stop=(g == 1),
                     )
 
-        def omega_out(h, b, eng):
+        def omega_out(h, b):
             lo = (b % 4) * P
-            copy(eng, o_grp[h, b // 4][:, lo : lo + P, :].rearrange("p (n e) u -> p n u e", e=PAIR), ps["O", h, b][:].rearrange("p (u n e) -> p n u e", u=SLOTS, e=PAIR))
+            slots_out("S", o_words[h, b // 4][:, lo : lo + P, :], ps["O", h, b], SLOTS)
 
-        def result_quant(kind, h, lo, hi):
-            dst, sc, src = (o_codes, o_sc, o_grp) if kind == "O" else (c_codes, c_sc, c_grp)
-            cols = slice(lo * W, hi * W)
-            nc.vector.quantize_mx(out=dst[h][:, cols].bitcast(FP8X4), scales=sc[h][:, cols], in_=src[h, lo // 2][:, (lo % 2) * W : (lo % 2 + hi - lo) * W, :].rearrange("p n t -> p (n t)"))
+        def four_slots(s, h):
+            return s < 2 and h == 0
 
-        def weave(item, tag, eng, lo, hi):
-            kind = item[0]
-            if item not in grp:
-                grp[item] = kt("grp%s%d%d" % item, [P, 2048], BF16, tag)
-            if kind == "W":
-                dst = grp[item][:].rearrange("p (u s w j) -> p u s j w", u=4, w=RUN, j=4)[:, lo:hi]
-                src = raw[item].rearrange("p j (s u w) -> p u s j w", u=4, w=RUN)[:, lo:hi]
-            else:
-                dst = grp[item][:].rearrange("p (a w j) -> p a j w", w=NEI, j=4)[:, 128 // NEI * lo : 128 // NEI * hi]
-                src = raw[item].rearrange("p j (a w) -> p a j w", w=NEI)[:, 128 // NEI * lo : 128 // NEI * hi]
-            copy(eng, dst, src)
-
-        def quant(item, lo, hi):
-            nc.vector.quantize_mx(out=codes[item][:, lo * P : hi * P].bitcast(FP8X4), scales=scales[item][:, lo * P : hi * P], in_=grp[item][:, lo * 512 : hi * 512])
-
-        def moving(s, c):
-            return ("X", s // 2, c), s % 2
-
-        def cov(s, c, h, k, n):
-            item, half = moving(s, c)
-            narrow = (s, h) in NARROW
+        def cov(s, c, h, first_bank, n):
+            it = ("X", s // 2, c)
             for z in range(2):
                 if n == 0:
-                    ps["C", s, h, z] = bank(k + z)
-                slots = range(SLOTS) if narrow else range(2 * z, 2 * z + 2)
-                width = P if narrow else W
-                lo = half * W + (z * P if narrow else 0)
+                    ps["C", s, h, z] = bank(first_bank + z)
+                slots = range(SLOTS) if four_slots(s, h) else range(2 * z, 2 * z + 2)
+                width = 512 // len(slots)
+                lo = (s % 2) * WIDTH + (z * P if four_slots(s, h) else 0)
                 for e, u in enumerate(slots):
                     nc.tensor.matmul_mx(
                         out=ps["C", s, h, z][:, e * width : (e + 1) * width],
                         lhsT=codes["W", h, c][:, u * P : (u + 1) * P].bitcast(FP8X4),
                         lhsT_scale=scales["W", h, c][:, u * P : (u + 1) * P],
-                        rhs=codes[item][:, lo : lo + width].bitcast(FP8X4),
-                        rhs_scale=scales[item][:, lo : lo + width],
+                        rhs=codes[it][:, lo : lo + width].bitcast(FP8X4),
+                        rhs_scale=scales[it][:, lo : lo + width],
                         start=(n == 0 and e == 0),
-                        stop=(n == CHUNKS - 1 and e == len(slots) - 1),
+                        stop=(n == LAST and e == len(slots) - 1),
                     )
 
         def cov_out(s, h, z, eng):
-            lo = (s % 2) * W
-            if (s, h) in NARROW:
-                copy(eng, c_grp[h, s // 2][:, lo + z * P : lo + (z + 1) * P, :].rearrange("p (n e) u -> p n u e", e=PAIR), ps["C", s, h, z][:].rearrange("p (u n e) -> p n u e", u=SLOTS, e=PAIR))
+            lo = (s % 2) * WIDTH
+            if four_slots(s, h):
+                slots_out(eng, c_words[h, s // 2][:, lo + z * P : lo + (z + 1) * P, :], ps["C", s, h, z], SLOTS)
             else:
-                copy(eng, c_grp[h, s // 2][:, lo : lo + W, 2 * z : 2 * z + 2].rearrange("p (n e) u -> p n u e", e=PAIR), ps["C", s, h, z][:].rearrange("p (u n e) -> p n u e", u=2, e=PAIR))
+                slots_out(eng, c_words[h, s // 2][:, lo : lo + WIDTH, 2 * z : 2 * z + 2], ps["C", s, h, z], 2)
+
+        def quantise_result(kind, h, lo, hi):
+            dst, sc, src = (o_codes, o_sc, o_words) if kind == "O" else (c_codes, c_sc, c_words)
+            cols = slice(lo * WIDTH, hi * WIDTH)
+            words = src[h, lo // 2][:, (lo % 2) * WIDTH : (lo % 2 + hi - lo) * WIDTH, :]
+            nc.vector.quantize_mx(out=dst[h][:, cols].bitcast(FP8X4), scales=sc[h][:, cols], in_=words.rearrange("p n u -> p (n u)"))
 
         def grad(dst, b, lo, n):
             rows = slice(b * P, (b + 1) * P)
             cols = slice(lo, lo + n)
-            step = 0
-            for lc, ls, rc, rs in ((o_codes, o_sc, c_codes, c_sc), (c_codes, c_sc, o_codes, o_sc)):
+            for side, (lc, ls, rc, rs) in enumerate(((o_codes, o_sc, c_codes, c_sc), (c_codes, c_sc, o_codes, o_sc))):
                 for h in range(HALVES):
                     nc.tensor.matmul_mx(
                         out=dst,
@@ -206,223 +192,225 @@ def tile_concord_precision_gradient_s12_kernel(tc, a_words, a_scales, b_words, b
                         lhsT_scale=ls[h][:, rows],
                         rhs=rc[h][:, cols].bitcast(FP8X4),
                         rhs_scale=rs[h][:, cols],
-                        start=(step == 0),
-                        stop=(step == 3),
+                        start=(side == 0 and h == 0),
+                        stop=(side == 1 and h == 1),
                     )
-                    step += 1
+
+        def on_diagonal(piece):
+            return piece[0] in ("square", "row") and piece[2] == (piece[1] if piece[0] == "square" else piece[1] // 2)
 
         def lower_tile(b, m):
             s, e = divmod(b, 2)
             if s >= 2 and m < 4:
                 return g_sb["wide", b][:, m * P : (m + 1) * P]
-            return g_sb["square", s, m // 2][:, e * W + (m % 2) * P : e * W + (m % 2 + 1) * P]
+            return g_sb["square", s, m // 2][:, e * WIDTH + (m % 2) * P : e * WIDTH + (m % 2 + 1) * P]
 
-        def g_make(unit, k):
+        def make_piece(piece, k):
             t = bank(k)
-            ps[unit] = t
-            if unit[0] == "wide":
-                grad(t[:], unit[1], 0, 512)
-            elif unit[0] == "row":
-                grad(t[:, 0:W], unit[1], unit[2] * W, W)
-            elif unit[0] == "square":
+            ps[piece] = t
+            if piece[0] == "wide":
+                grad(t[:], piece[1], 0, 512)
+            elif piece[0] == "row":
+                grad(t[:, 0:WIDTH], piece[1], piece[2] * WIDTH, WIDTH)
+            elif piece[0] == "square":
                 for e in range(2):
-                    grad(t[:, e * W : (e + 1) * W], 2 * unit[1] + e, unit[2] * W, W)
+                    grad(t[:, e * WIDTH : (e + 1) * WIDTH], 2 * piece[1] + e, piece[2] * WIDTH, WIDTH)
             else:
-                r, s = unit[1:]
+                r, s = piece[1:]
                 for f in range(2):
                     for e in range(2):
-                        nc.tensor.transpose(t[:, e * W + f * P : e * W + (f + 1) * P], lower_tile(2 * s + f, 2 * r + e), ident)
+                        nc.tensor.transpose(t[:, e * WIDTH + f * P : e * WIDTH + (f + 1) * P], lower_tile(2 * s + f, 2 * r + e), ident)
 
         def less_diagonal(dst, src, b):
-            z = P - (b % 2) * P
-            nc.vector.scalar_tensor_tensor(out=dst, in0=ident_wide[:, z : z + W], scalar=d_neg[:, b : b + 1], in1=src, op0=ALU.mult, op1=ALU.add)
+            lo = P - (b % 2) * P
+            nc.vector.scalar_tensor_tensor(out=dst, in0=ident_wide[:, lo : lo + WIDTH], scalar=d_neg[:, b : b + 1], in1=src, op0=ALU.mult, op1=ALU.add)
+
+        def result(name, width):
+            return sbuf(name, [P, width], F32, spent.pop(0) if spent else name)
+
+        def piece_out(piece, eng):
+            t = ps[piece]
+            if piece[0] == "row" and on_diagonal(piece):
+                g_sb[piece] = result("g_row%d" % piece[1], WIDTH)
+                less_diagonal(g_sb[piece][:], t[:, 0:WIDTH], piece[1])
+            elif piece[0] == "row":
+                s, e = divmod(piece[1], 2)
+                if e == 0:
+                    g_sb["square", s, piece[2]] = result("g_square%d%d" % (s, piece[2]), 512)
+                copy(eng, g_sb["square", s, piece[2]][:, e * WIDTH : (e + 1) * WIDTH], t[:, 0:WIDTH])
+            else:
+                g_sb[piece] = result("g_%s%d%d" % (piece[0], piece[1], piece[-1]), 512)
+                if on_diagonal(piece):
+                    for e in range(2):
+                        less_diagonal(g_sb[piece][:, e * WIDTH : (e + 1) * WIDTH], t[:, e * WIDTH : (e + 1) * WIDTH], 2 * piece[1] + e)
+                else:
+                    copy(eng, g_sb[piece][:], t[:])
 
         def store_square(g, s, r):
-            nc.sync.dma_start(out=out[s * W : (s + 1) * W, r * W : (r + 1) * W].rearrange("(e p) c -> p e c", e=2), in_=g[:].rearrange("p (e c) -> p e c", e=2))
+            nc.sync.dma_start(out=out[s * WIDTH : (s + 1) * WIDTH, r * WIDTH : (r + 1) * WIDTH].rearrange("(e p) c -> p e c", e=2), in_=g[:].rearrange("p (e c) -> p e c", e=2))
 
-        def g_out(unit, eng):
-            t = ps[unit]
-            if unit[0] == "row":
-                b, r = unit[1:]
-                s, e = divmod(b, 2)
-                if s == r:
-                    g_sb[unit] = result("g_row%d" % b, W)
-                    less_diagonal(g_sb[unit][:], t[:, 0:W], b)
-                else:
-                    if e == 0:
-                        g_sb["square", s, r] = result("g_square%d%d" % (s, r), 512)
-                    copy(eng, g_sb["square", s, r][:, e * W : (e + 1) * W], t[:, 0:W])
-                return
-            g = result("g_%s%d%d" % (unit[0], unit[1], unit[-1]), 512)
-            g_sb[unit] = g
-            if unit[0] == "square" and unit[1] == unit[2]:
-                for e in range(2):
-                    less_diagonal(g[:, e * W : (e + 1) * W], t[:, e * W : (e + 1) * W], 2 * unit[1] + e)
-            else:
-                copy(eng, g[:], t[:])
-
-        def flip(unit):
-            g_sb["flip", unit] = kt("g_flip%d" % unit[1], [P, 512], F32)
-            nc.vector.transpose(out=g_sb["flip", unit][:], in_=ps[unit][:])
-
-        def flip_store(unit):
-            for a in range(4):
-                lo = unit[1] * P + 32 * a
-                nc.sync.dma_start(out=out[0:512, lo : lo + 32].rearrange("(b i) j -> i b j", i=32), in_=g_sb["flip", unit][32 * a : 32 * a + 32, :].rearrange("i (b j) -> i b j", j=32))
-
-        def g_store(unit):
-            if unit[0] == "wide":
-                nc.sync.dma_start(out=out[unit[1] * P : (unit[1] + 1) * P, 0:512], in_=g_sb[unit][:])
-            elif unit[0] != "row":
-                store_square(g_sb[unit], unit[1], unit[2])
-            elif unit[1] // 2 == unit[2]:
-                nc.sync.dma_start(out=out[unit[1] * P : (unit[1] + 1) * P, unit[2] * W : (unit[2] + 1) * W], in_=g_sb[unit][:])
-            elif unit[1] % 2:
-                store_square(g_sb["square", unit[1] // 2, unit[2]], unit[1] // 2, unit[2])
+        def store_piece(piece):
+            if piece[0] == "wide":
+                nc.sync.dma_start(out=out[piece[1] * P : (piece[1] + 1) * P, 0:512], in_=g_sb[piece][:])
+            elif piece[0] != "row":
+                store_square(g_sb[piece], piece[1], piece[2])
+            elif on_diagonal(piece):
+                nc.sync.dma_start(out=out[piece[1] * P : (piece[1] + 1) * P, piece[2] * WIDTH : (piece[2] + 1) * WIDTH], in_=g_sb[piece][:])
+            elif piece[1] % 2:
+                store_square(g_sb["square", piece[1] // 2, piece[2]], piece[1] // 2, piece[2])
 
         nc.vector.memset(a_sc[:].bitcast(I32), 0)
         nc.vector.memset(b_sc_all[:].bitcast(I32), 0)
-        if WARM:
-            idle_codes = kt("idle_codes", [P, W], U32)
-            idle_sc = kt("idle_sc", [P, W], U8)
-            nc.vector.quantize_mx(out=idle_codes[:].bitcast(FP8X4), scales=idle_sc[:], in_=b_sc_all[:].bitcast(BF16))
-            idle = bank(7)
-            for k in range(WARM):
-                nc.tensor.matmul_mx(out=idle[:, 0:W], lhsT=idle_codes[:, 0:P].bitcast(FP8X4), lhsT_scale=idle_sc[:, 0:P], rhs=idle_codes[:].bitcast(FP8X4), rhs_scale=idle_sc[:], start=True, stop=True)
+        idle_codes = sbuf("idle_codes", [P, WIDTH], U32)
+        idle_sc = sbuf("idle_sc", [P, WIDTH], U8)
+        nc.vector.quantize_mx(out=idle_codes[:].bitcast(FP8X4), scales=idle_sc[:], in_=b_sc_all[:].bitcast(BF16))
+        idle = bank(BANKS - 1)
+        for k in range(WARM_UPS):
+            nc.tensor.matmul_mx(out=idle[:, 0:WIDTH], lhsT=idle_codes[:, 0:P].bitcast(FP8X4), lhsT_scale=idle_sc[:, 0:P], rhs=idle_codes[:].bitcast(FP8X4), rhs_scale=idle_sc[:], start=True, stop=True)
         nc.gpsimd.memset(d_rows[:], 0.0)
         nc.gpsimd.dma_start(out=d_rows[0:P:32, :].rearrange("q (b a) -> q b a", a=32), in_=d.rearrange("(b q a) -> q b a", q=4, a=32))
         nc.gpsimd.memset(ident_wide[:], 0.0)
         make_identity(nc, ident, nomemset=True)
 
-        last = CHUNKS - 1
-        for tok in LOADS.split():
-            if tok[0] == "s":
-                dst, src = (b_sc_raw, b_scales) if tok[1] == "B" else (a_sc, a_scales)
-                cols = slice(0, 1024) if tok[2] == "w" else slice(512 * int(tok[2]), 512 * int(tok[2]) + 512)
-                load_scales(dst, src, {"": range(4), "a": range(2), "b": range(2, 4)}[tok[3:]], cols)
-            elif tok[0] == "c":
-                dst, src = (b_raw, b_words) if tok[1] == "B" else (a_codes, a_words)
-                load_codes(dst[int(tok[2])], src, int(tok[2]))
+        load_scales(b_sc_raw, b_scales, range(4))
+        load_codes(b_raw[0], b_words, 0)
+        load_scales(a_sc, a_scales, range(2))
+        load_codes(a_codes[0], a_words, 0)
+        load_scales(a_sc, a_scales, range(2, 4))
+        load_rows("W", 0, 0, 512)
+        load_codes(a_codes[1], a_words, 1)
+        load_rows("X", 0, 0, 512)
+        load_codes(b_raw[1], b_words, 1)
+        for c in range(1, CHUNKS):
+            load_rows("W", c, 0, 1024)
+            load_rows("X", c, 0, 512)
+        load_rows("W", 0, 512, 1024)
+        for s in range(2, BLOCKS):
+            for c in range(CHUNKS):
+                load_rows("X", c, s * WIDTH, (s + 1) * WIDTH)
+
+        tensor, vector, scalar, stores = [], [], [], []
+        need = [("W", 0, 0), ("X", 0, 0)] + [it for c in range(1, LAST) for it in (("W", 0, c), ("W", 1, c), ("X", 0, c))]
+        need += [("W", 0, LAST), ("X", 0, LAST), ("W", 1, LAST), ("W", 1, 0)] + [("X", 1, c) for c in range(CHUNKS)]
+        holders = {}
+
+        def weave_step(it, part, eng):
+            k = need.index(it)
+            frees = [("quantised", need[k - WOVEN_TILES], n) for n in range(4)] if k >= WOVEN_TILES else []
+            return ([("woven", it, n) for n in range(*part)], frees, lambda: weave(it, "woven%d" % (k % WOVEN_TILES), eng, part))
+
+        def quantise_step(it, part):
+            return ([("quantised", it, n) for n in range(*part)], [("woven", it, n) for n in range(*part)], lambda: quantise(it, part))
+
+        def result_step(kind, h, lo, hi):
+            if kind == "O":
+                waits = [("out", "O", h, b) for b in range(2 * lo, 2 * hi)]
             else:
-                load_rows(tok[0], int(tok[1]), int(tok[2]), 2 if tok[3:] == "+" else 1, *{"": (0, 512), "+": (0, 1024), "a": (0, W), "b": (W, 512)}[tok[3:]])
+                waits = [("out", "C", s, h, z) for s in range(lo, hi) for z in range(2)]
+            return ([("quantised", kind, h, s) for s in range(lo, hi)], waits, lambda: quantise_result(kind, h, lo, hi))
 
-        pe, vec, act, sp = [], [], [], []
-        def item_of(tok):
-            return (tok[1], int(tok[2]), int(tok[3]))
+        def cov_out_step(s, h, z, eng):
+            return ([("out", "C", s, h, z)], [("made", "C", s, LAST, h)], lambda: cov_out(s, h, z, eng))
 
-        def span(tok):
-            return (int(tok[4]), int(tok[5])) if len(tok) > 4 else (0, 4)
+        def piece_out_step(piece, eng):
+            return ([("out",) + piece], [("made",) + piece], lambda: piece_out(piece, eng))
 
-        need = []
-        for tok in V_ORDER.split():
-            if tok[0] == "q" and item_of(tok) not in need:
-                need.append(item_of(tok))
-        tags = {it: "grp%d" % (k % GROUPS) for k, it in enumerate(need)}
-        frees = {it: [("q", need[k - GROUPS], u) for u in range(4)] if k >= GROUPS else [] for k, it in enumerate(need)}
+        def free_step(call):
+            return ([], [], call)
 
-        def weave_step(tok, eng):
-            it, (lo, hi) = item_of(tok), span(tok)
-            return ([("weave", it, u) for u in range(lo, hi)], frees[it], lambda: weave(it, tags[it], eng, lo, hi))
-
-        def quant_step(tok):
-            it, (lo, hi) = item_of(tok), span(tok)
-            return ([("q", it, u) for u in range(lo, hi)], [("weave", it, u) for u in range(lo, hi)], lambda: quant(it, lo, hi))
-
-        held = {}
-
-        def take(k, n, names):
-            waits = []
-            for m in range(n):
-                waits += held.get(k + m, [])
-                held[k + m] = names[m]
+        def take_bank(k, emptied_by):
+            waits = holders.get(k, [])
+            holders[k] = [emptied_by]
             return waits
 
-        def cov_step(s, c, h, k, n):
-            item, half = moving(s, c)
-            waits = [("q", ("W", h, c), u) for u in range(4)] + [("q", item, 2 * half), ("q", item, 2 * half + 1)]
+        def cov_step(s, c, h, first_bank, n):
+            waits = [("quantised", ("W", h, c), u) for u in range(4)] + [("quantised", ("X", s // 2, c), 2 * (s % 2) + e) for e in range(2)]
             if n == 0:
-                waits += take(k, 2, [[("out", "C", s, h, pair)] for pair in range(2)])
-            pe.append(([("mm", "C", s, n, h)], waits, lambda: cov(s, c, h, k, n)))
+                waits += [w for z in range(2) for w in take_bank(first_bank + z, ("out", "C", s, h, z))]
+            return ([("made", "C", s, n, h)], waits, lambda: cov(s, c, h, first_bank, n))
 
-        def omega_step(n, k):
-            h, b = divmod(n, 8)
-            pe.append(([("mm", "O", h, b)], [("sort", h), ("sortsc", h)] + take(k, 1, [[("out", "O", h, b)]]), lambda: omega(h, b, k)))
-
-        if EARLY:
-            for s in range(2):
-                cov_step(s, 0, 0, 2 * s, 0)
-        for n in range(16):
-            omega_step(n, 4 + n % 4 if EARLY else n % 8)
-        seen = [EARLY, 0]
-        for tok in COV_ORDER.split()[EARLY:]:
-            c, h = int(tok[0]), int(tok[1])
-            for s in range(2):
-                cov_step(s, c, h, 4 * h + 2 * s, seen[h])
-            seen[h] += 1
-        units = [({"s": "square", "w": "wide", "m": "mirror", "r": "row"}[tok[0]],) + tuple(int(x) for x in tok[1:]) for tok in UNITS.split()]
-        def unit_step(n, k):
-            unit = units[n]
-            if unit[0] == "mirror":
-                r, s = unit[1:]
-                waits = [("out", "wide", 2 * s), ("out", "wide", 2 * s + 1)] if s >= 2 and r < 2 else ([("out", "square", 1, 0)] if s == 1 else [("out", "row", 6, 2), ("out", "row", 7, 2)])
+        def piece_step(piece, k):
+            if piece[0] != "mirror":
+                top = piece[1] if piece[0] == "square" else piece[1] // 2
+                waits = [("quantised", kind, h, s) for kind in "OC" for h in range(HALVES) for s in range(top + 1)]
+            elif piece[2] == 1:
+                waits = [("out", "square", 1, 0)]
             else:
-                top = unit[1] if unit[0] == "square" else unit[1] // 2
-                waits = [("q", kind, h, s) for kind in "OC" for h in range(HALVES) for s in range(top + 1)]
-            pe.append(([("mm",) + unit], waits + take(k, 1, [[("out",) + unit] + ([("flip",) + unit] if unit in FLIPS else [])]), lambda: g_make(unit, k)))
+                waits = [("out", "wide", 2 * piece[2] + e) if piece[1] < 2 else ("out", "row", 6 + e, 2) for e in range(2)]
+            return ([("made",) + piece], waits + take_bank(k, ("out",) + piece), lambda: make_piece(piece, k))
 
-        n = 0
-        for tok in PE_TAIL.split():
-            if tok[0] == "c":
-                for h in range(HALVES):
-                    cov_step(int(tok[1]), int(tok[2]), h, 4 * (int(tok[1]) - 2) + 2 * h, int(tok[2]))
+        for h in range(HALVES):
+            for b in range(BANKS):
+                tensor.append(([("made", "O", h, b)], [("sorted", h)] + take_bank(b, ("out", "O", h, b)), lambda h=h, b=b: omega(h, b)))
+        passes = [(0, 0)] + [(c, h) for c in range(1, CHUNKS) for h in range(HALVES)] + [(0, 1)]
+        for k, (c, h) in enumerate(passes):
+            done = len([1 for other in passes[:k] if other[1] == h])
+            tensor.extend(cov_step(s, c, h, 4 * h + 2 * s, done) for s in range(2))
+        for s in range(2, BLOCKS):
+            tensor.extend(cov_step(s, c, h, 4 * (s - 2) + 2 * h, c) for c in range(CHUNKS) for h in range(HALVES))
+        pieces = [("square", 1, 0), ("wide", 4), ("wide", 5), ("wide", 6), ("mirror", 0, 1), ("mirror", 0, 2), ("mirror", 1, 2)]
+        pieces += [("wide", 7), ("row", 6, 2), ("row", 7, 2), ("square", 0, 0)] + [("mirror", r, 3) for r in range(3)]
+        pieces += [("square", 1, 1), ("square", 2, 2), ("row", 6, 3), ("row", 7, 3)]
+        tensor.extend(piece_step(piece, k % BANKS) for k, piece in enumerate(pieces))
+        stores.extend(([], [("out",) + piece], lambda piece=piece: store_piece(piece)) for piece in pieces)
+
+        early = {BANKS_BEFORE_XW: ("W", 1, 1), BANKS_BEFORE_X: ("X", 0, 1)}
+        late = [("X", 0, LAST - 1), ("W", 0, LAST), ("X", 0, LAST), ("W", 1, LAST), ("W", 1, 0)]
+        for n in range(HALVES * BANKS):
+            h, b = divmod(n, BANKS)
+            if n in early:
+                scalar.append(weave_step(early[n], SECOND, "S"))
+            scalar.append(([("out", "O", h, b)], [("made", "O", h, b)], lambda h=h, b=b: omega_out(h, b)))
+        scalar.extend(weave_step(it, SECOND, "S") for it in late)
+        finished = [(s, h) for h in range(HALVES) for s in range(2)] + [(s, h) for s in range(2, BLOCKS) for h in range(HALVES)]
+        scalar.extend(cov_out_step(s, h, z, "S") for s, h in finished for z in range(2) if s < BLOCKS - 1 or z == 0)
+        on_vector = [piece for piece in pieces if on_diagonal(piece) or piece in (("wide", 6), ("wide", 7), ("mirror", 0, 2), ("mirror", 1, 3))]
+        scalar.extend(piece_out_step(piece, "S") for piece in pieces if piece not in on_vector)
+
+        def mine(it):
+            return weave_step(it, FIRST if it in late or it in early.values() else WHOLE, "V")
+
+        vector.append(free_step(lambda: sort_b_scales(0)))
+        vector.append(([("sorted", 0)], [], lambda: sort_b_codes(0)))
+        vector.append(free_step(lambda: sort_b_scales(1)))
+        vector += [mine(("W", 0, 0)), quantise_step(("W", 0, 0), WHOLE), weave_step(("X", 0, 0), FIRST, "V")]
+        vector.append(([("sorted", 1)], [], lambda: sort_b_codes(1)))
+        vector += [weave_step(("X", 0, 0), SECOND, "V"), quantise_step(("X", 0, 0), FIRST), quantise_step(("X", 0, 0), SECOND)]
+        for c in range(1, CHUNKS):
+            w0, w1, xc = ("W", 0, c), ("W", 1, c), ("X", 0, c)
+            vector.append(mine(w0))
+            if c > 1:
+                vector.append(quantise_step(("X", 0, c - 1), SECOND))
+            vector.append(mine(w1))
+            if c < LAST:
+                vector += [quantise_step(w0, WHOLE), mine(xc), quantise_step(w1, WHOLE), quantise_step(xc, FIRST)]
             else:
-                unit_step(n, int(tok))
-                n += 1
-
-        extras = {
-            "s0": ([("sortsc", 0)], [], lambda: sort_b_scales(0)),
-            "s1": ([("sortsc", 1)], [], lambda: sort_b_scales(1)),
-            "c0": ([("sort", 0)], [], lambda: sort_b_codes(0)),
-            "c1": ([("sort", 1)], [], lambda: sort_b_codes(1)),
-            "d0": ([("d", 0)], [], lambda: nc.vector.transpose(out=d_turned[:], in_=d_rows[:])),
-            "d1": ([("d", 1)], [], lambda: nc.vector.reciprocal(out=d_rec[:], in_=d_turned[:, 0:256:32])),
-            "d2": ([("d", 2)], [], lambda: nc.vector.tensor_scalar(out=d_neg[:], in0=d_rec[:], scalar1=-1.0, scalar2=None, op0=ALU.mult)),
-        }
-        for eng, queue, order in (("V", vec, V_ORDER), ("S", act, S_ORDER)):
-            for tok in order.split():
-                if tok in extras:
-                    queue.append(extras[tok])
-                elif tok[0] == "o":
-                    h, b = divmod(int(tok[1:]), 8)
-                    queue.append(([("out", "O", h, b)], [("mm", "O", h, b)], lambda h=h, b=b, eng=eng: omega_out(h, b, eng)))
-                elif tok[0] == "k":
-                    s, h, pair = int(tok[1]), int(tok[2]), int(tok[3])
-                    queue.append(([("out", "C", s, h, pair)], [("mm", "C", s, last, h)], lambda s=s, h=h, pair=pair, eng=eng: cov_out(s, h, pair, eng)))
-                elif tok[0] in "OC":
-                    h, lo, hi = int(tok[1]), int(tok[2]), int(tok[3])
-                    waits = [("out", "O", h, b) for b in range(2 * lo, 2 * hi)] if tok[0] == "O" else [("out", "C", s, h, pair) for s in range(lo, hi) for pair in range(2)]
-                    queue.append(([("q", tok[0], h, s) for s in range(lo, hi)], waits, lambda tok=tok, h=h, lo=lo, hi=hi: result_quant(tok[0], h, lo, hi)))
-                elif tok[0] == "f":
-                    unit = units[int(tok[1:])]
-                    queue.append(([("flip",) + unit], [("mm",) + unit], lambda unit=unit: flip(unit)))
-                elif tok[0] == "g":
-                    unit = units[int(tok[1:])]
-                    queue.append(([("out",) + unit], [("mm",) + unit], lambda unit=unit, eng=eng: g_out(unit, eng)))
-                else:
-                    queue.append(quant_step(tok) if tok[0] == "q" else weave_step(tok, eng))
-        for n, unit in enumerate(units):
-            sp.append(([], [("out",) + unit], lambda unit=unit: g_store(unit)))
-            if unit in FLIPS:
-                sp.append(([], [("flip",) + unit], lambda unit=unit: flip_store(unit)))
+                vector += [mine(xc), quantise_step(w0, WHOLE), quantise_step(xc, FIRST), quantise_step(xc, SECOND)]
+        behind = quantise_step(("W", 1, LAST), WHOLE)
+        for it, part in [(("W", 1, 0), WHOLE)] + [(("X", 1, c), part) for part in (FIRST, SECOND) for c in range(CHUNKS)]:
+            vector += [weave_step(it, FIRST if it in late else part, "V"), behind]
+            behind = quantise_step(it, part)
+        vector += [result_step("O", 0, 0, 2), behind, result_step("O", 1, 0, 2)]
+        vector += [result_step("C", h, 0, 2) for h in range(HALVES)]
+        vector += [result_step(kind, h, 2, 3) for kind in "OC" for h in range(HALVES)]
+        vector.append(cov_out_step(3, 0, 1, "V"))
+        vector += [result_step("O", h, 3, 4) for h in range(HALVES)]
+        vector.append(cov_out_step(3, 1, 1, "V"))
+        vector += [result_step("C", h, 3, 4) for h in range(HALVES)]
+        vector.append(free_step(lambda: nc.vector.transpose(out=d_turned[:], in_=d_rows[:])))
+        vector.append(piece_out_step(on_vector[0], "V"))
+        vector.append(free_step(lambda: nc.vector.reciprocal(out=d_rec[:], in_=d_turned[:, 0:256:32])))
+        vector.append(free_step(lambda: nc.vector.tensor_scalar(out=d_neg[:], in0=d_rec[:], scalar1=-1.0, scalar2=None, op0=ALU.mult)))
+        vector.extend(piece_out_step(piece, "V") for piece in on_vector[1:])
 
         written = []
-        queues = [pe, vec, act, sp]
+        queues = [tensor, vector, scalar, stores]
         while any(queues):
             moved = 0
             for queue in queues:
                 while queue and all(w in written for w in queue[0][1]):
-                    name, waits, call = queue.pop(0)
+                    makes, waits, call = queue.pop(0)
                     call()
-                    written.extend(name)
+                    written.extend(makes)
                     moved += 1
             assert moved

@@ -24,6 +24,7 @@ WIDTH = 256
 RUN = 8
 BANKS = 8
 WARM_UPS = 8
+WIDE_OMEGA_BANKS = 4
 WOVEN_TILES = 6
 BANKS_BEFORE_XW, BANKS_BEFORE_X = 8, 10
 WHOLE, FIRST, SECOND = (0, 4), (0, 2), (2, 4)
@@ -77,9 +78,9 @@ def tile_concord_precision_gradient_s12_kernel(tc, a_words, a_scales, b_words, b
         def load_codes(dst, src, z):
             nc.sync.dma_start(out=dst[:].bitcast(I32), in_=src[:, :, z * 1024 : (z + 1) * 1024].bitcast(I32).rearrange("g p n -> p g n"))
 
-        def load_scales(dst, src, rows):
+        def load_scales(dst, src, rows, cols):
             for r in rows:
-                nc.sync.dma_start(out=dst[r:P:32, :, :].bitcast(I32), in_=src[:, r:16:4, :].bitcast(I32).rearrange("g q n -> q g n"))
+                nc.sync.dma_start(out=dst[r:P:32, :, cols].bitcast(I32), in_=src[:, r:16:4, cols].bitcast(I32).rearrange("g q n -> q g n"))
 
         def load_rows(kind, c, lo, hi):
             first = lo // 512
@@ -127,27 +128,37 @@ def tile_concord_precision_gradient_s12_kernel(tc, a_words, a_scales, b_words, b
         def slots_out(eng, dst, src, count):
             copy(eng, dst.rearrange("p (n e) u -> p n u e", e=2), src[:].rearrange("p (u n e) -> p n u e", u=count, e=2))
 
+        def two_slots(h, b):
+            return h * BANKS + b < WIDE_OMEGA_BANKS
+
         def omega(h, b):
             t = bank(b)
             ps["O", h, b] = t
-            for u in range(SLOTS):
+            slots = range(2 * (b % 2), 2 * (b % 2) + 2) if two_slots(h, b) else range(SLOTS)
+            width = 512 // len(slots)
+            lo = b // 2 * WIDTH if two_slots(h, b) else b * P
+            for e, u in enumerate(slots):
                 for g in range(2):
                     nc.tensor.matmul_mx(
-                        out=t[:, u * P : (u + 1) * P],
+                        out=t[:, e * width : (e + 1) * width],
                         lhsT=b_codes[h][:, g, u * 256 : (u + 1) * 256].bitcast(FP4X4),
                         lhsT_scale=b_sc[h][:, g, u * P : (u + 1) * P],
-                        rhs=a_codes[b // 4][:, g, (b % 4) * 256 : (b % 4 + 1) * 256].bitcast(FP4X4),
-                        rhs_scale=a_sc[:, g, b * P : (b + 1) * P],
+                        rhs=a_codes[b // 4][:, g, 2 * (lo % 512) : 2 * (lo % 512 + width)].bitcast(FP4X4),
+                        rhs_scale=a_sc[:, g, lo : lo + width],
                         start=(g == 0),
                         stop=(g == 1),
                     )
 
         def omega_out(h, b):
-            lo = (b % 4) * P
-            slots_out("S", o_words[h, b // 4][:, lo : lo + P, :], ps["O", h, b], SLOTS)
+            if two_slots(h, b):
+                lo = (b // 2 % 2) * WIDTH
+                slots_out("S", o_words[h, b // 4][:, lo : lo + WIDTH, 2 * (b % 2) : 2 * (b % 2) + 2], ps["O", h, b], 2)
+            else:
+                lo = (b % 4) * P
+                slots_out("S", o_words[h, b // 4][:, lo : lo + P, :], ps["O", h, b], SLOTS)
 
         def four_slots(s, h):
-            return s < 2 and h == 0
+            return s == 0 and h == 0
 
         def cov(s, c, h, first_bank, n):
             it = ("X", s // 2, c)
@@ -272,12 +283,13 @@ def tile_concord_precision_gradient_s12_kernel(tc, a_words, a_scales, b_words, b
         nc.gpsimd.memset(ident_wide[:], 0.0)
         make_identity(nc, ident, nomemset=True)
 
-        load_scales(b_sc_raw, b_scales, range(4))
+        load_scales(b_sc_raw, b_scales, range(4), slice(0, 1024))
         load_codes(b_raw[0], b_words, 0)
-        load_scales(a_sc, a_scales, range(2))
+        load_scales(a_sc, a_scales, range(2), slice(0, 512))
         load_codes(a_codes[0], a_words, 0)
-        load_scales(a_sc, a_scales, range(2, 4))
+        load_scales(a_sc, a_scales, range(2, 4), slice(0, 512))
         load_rows("W", 0, 0, 512)
+        load_scales(a_sc, a_scales, range(4), slice(512, 1024))
         load_codes(a_codes[1], a_words, 1)
         load_rows("X", 0, 0, 512)
         load_codes(b_raw[1], b_words, 1)

@@ -24,7 +24,6 @@ WIDTH = 256
 RUN = 8
 BANKS = 8
 WARM_UPS = 8
-WIDE_OMEGA_BANKS = 4
 WOVEN_TILES = 6
 BANKS_BEFORE_XW, BANKS_BEFORE_X = 8, 10
 WHOLE, FIRST, SECOND = (0, 4), (0, 2), (2, 4)
@@ -78,9 +77,9 @@ def tile_concord_precision_gradient_s12_kernel(tc, a_words, a_scales, b_words, b
         def load_codes(dst, src, z):
             nc.sync.dma_start(out=dst[:].bitcast(I32), in_=src[:, :, z * 1024 : (z + 1) * 1024].bitcast(I32).rearrange("g p n -> p g n"))
 
-        def load_scales(dst, src, rows, cols):
+        def load_scales(dst, src, rows):
             for r in rows:
-                nc.sync.dma_start(out=dst[r:P:32, :, cols].bitcast(I32), in_=src[:, r:16:4, cols].bitcast(I32).rearrange("g q n -> q g n"))
+                nc.sync.dma_start(out=dst[r:P:32, :, :].bitcast(I32), in_=src[:, r:16:4, :].bitcast(I32).rearrange("g q n -> q g n"))
 
         def load_rows(kind, c, lo, hi):
             first = lo // 512
@@ -128,34 +127,24 @@ def tile_concord_precision_gradient_s12_kernel(tc, a_words, a_scales, b_words, b
         def slots_out(eng, dst, src, count):
             copy(eng, dst.rearrange("p (n e) u -> p n u e", e=2), src[:].rearrange("p (u n e) -> p n u e", u=count, e=2))
 
-        def two_slots(h, b):
-            return h * BANKS + b < WIDE_OMEGA_BANKS
-
         def omega(h, b):
             t = bank(b)
             ps["O", h, b] = t
-            slots = range(2 * (b % 2), 2 * (b % 2) + 2) if two_slots(h, b) else range(SLOTS)
-            width = 512 // len(slots)
-            lo = b // 2 * WIDTH if two_slots(h, b) else b * P
-            for e, u in enumerate(slots):
+            for u in range(SLOTS):
                 for g in range(2):
                     nc.tensor.matmul_mx(
-                        out=t[:, e * width : (e + 1) * width],
+                        out=t[:, u * P : (u + 1) * P],
                         lhsT=b_codes[h][:, g, u * 256 : (u + 1) * 256].bitcast(FP4X4),
                         lhsT_scale=b_sc[h][:, g, u * P : (u + 1) * P],
-                        rhs=a_codes[b // 4][:, g, 2 * (lo % 512) : 2 * (lo % 512 + width)].bitcast(FP4X4),
-                        rhs_scale=a_sc[:, g, lo : lo + width],
+                        rhs=a_codes[b // 4][:, g, (b % 4) * 256 : (b % 4 + 1) * 256].bitcast(FP4X4),
+                        rhs_scale=a_sc[:, g, b * P : (b + 1) * P],
                         start=(g == 0),
                         stop=(g == 1),
                     )
 
         def omega_out(h, b):
-            if two_slots(h, b):
-                lo = (b // 2 % 2) * WIDTH
-                slots_out("S", o_words[h, b // 4][:, lo : lo + WIDTH, 2 * (b % 2) : 2 * (b % 2) + 2], ps["O", h, b], 2)
-            else:
-                lo = (b % 4) * P
-                slots_out("S", o_words[h, b // 4][:, lo : lo + P, :], ps["O", h, b], SLOTS)
+            lo = (b % 4) * P
+            slots_out("S", o_words[h, b // 4][:, lo : lo + P, :], ps["O", h, b], SLOTS)
 
         def four_slots(s, h):
             return s == 0 and h == 0
@@ -283,13 +272,12 @@ def tile_concord_precision_gradient_s12_kernel(tc, a_words, a_scales, b_words, b
         nc.gpsimd.memset(ident_wide[:], 0.0)
         make_identity(nc, ident, nomemset=True)
 
-        load_scales(b_sc_raw, b_scales, range(4), slice(0, 1024))
+        load_scales(b_sc_raw, b_scales, range(4))
         load_codes(b_raw[0], b_words, 0)
-        load_scales(a_sc, a_scales, range(2), slice(0, 512))
+        load_scales(a_sc, a_scales, range(2))
         load_codes(a_codes[0], a_words, 0)
-        load_scales(a_sc, a_scales, range(2, 4), slice(0, 512))
+        load_scales(a_sc, a_scales, range(2, 4))
         load_rows("W", 0, 0, 512)
-        load_scales(a_sc, a_scales, range(4), slice(512, 1024))
         load_codes(a_codes[1], a_words, 1)
         load_rows("X", 0, 0, 512)
         load_codes(b_raw[1], b_words, 1)
@@ -374,8 +362,10 @@ def tile_concord_precision_gradient_s12_kernel(tc, a_words, a_scales, b_words, b
                 scalar.append(weave_step(early[n], SECOND, "S"))
             scalar.append(([("out", "O", h, b)], [("made", "O", h, b)], lambda h=h, b=b: omega_out(h, b)))
         scalar.extend(weave_step(it, SECOND, "S") for it in late)
-        finished = [(s, h) for h in range(HALVES) for s in range(2)] + [(s, h) for s in range(2, BLOCKS) for h in range(HALVES)]
-        scalar.extend(cov_out_step(s, h, z, "S") for s, h in finished for z in range(2) if s < BLOCKS - 1 or z == 0)
+        scalar.extend(cov_out_step(s, h, z, "S") for h in range(HALVES) for s in range(2) for z in range(2))
+        scalar.extend(weave_step(("X", 1, c), SECOND, "S") for c in range(2, CHUNKS))
+        scalar.extend(cov_out_step(2, h, z, "S") for h in range(HALVES) for z in range(2))
+        scalar.extend(cov_out_step(3, h, 0, "S") for h in range(HALVES))
         on_vector = [piece for piece in pieces if on_diagonal(piece) or piece in (("wide", 6), ("wide", 7), ("mirror", 0, 2), ("mirror", 1, 3))]
         scalar.extend(piece_out_step(piece, "S") for piece in pieces if piece not in on_vector)
 
@@ -399,16 +389,13 @@ def tile_concord_precision_gradient_s12_kernel(tc, a_words, a_scales, b_words, b
             else:
                 vector += [mine(xc), quantise_step(w0, WHOLE), quantise_step(xc, FIRST), quantise_step(xc, SECOND)]
         behind = quantise_step(("W", 1, LAST), WHOLE)
-        for it, part in [(("W", 1, 0), WHOLE)] + [(("X", 1, c), part) for part in (FIRST, SECOND) for c in range(CHUNKS)]:
+        for it, part in [(("W", 1, 0), WHOLE)] + [(("X", 1, c), FIRST) for c in range(CHUNKS)] + [(("X", 1, c), SECOND) for c in range(2)]:
             vector += [weave_step(it, FIRST if it in late else part, "V"), behind]
             behind = quantise_step(it, part)
-        vector += [result_step("O", 0, 0, 2), behind, result_step("O", 1, 0, 2)]
-        vector += [result_step("C", h, 0, 2) for h in range(HALVES)]
-        vector += [result_step(kind, h, 2, 3) for kind in "OC" for h in range(HALVES)]
-        vector.append(cov_out_step(3, 0, 1, "V"))
-        vector += [result_step("O", h, 3, 4) for h in range(HALVES)]
-        vector.append(cov_out_step(3, 1, 1, "V"))
-        vector += [result_step("C", h, 3, 4) for h in range(HALVES)]
+        vector += [result_step("O", 0, 0, 2), behind, result_step("O", 1, 0, 2), quantise_step(("X", 1, 2), SECOND)]
+        vector += [result_step("C", 0, 0, 2), quantise_step(("X", 1, 3), SECOND), result_step("C", 1, 0, 2)]
+        vector += [result_step("O", h, 2, 4) for h in range(HALVES)] + [result_step("C", h, 2, 3) for h in range(HALVES)]
+        vector += [cov_out_step(3, h, 1, "V") for h in range(HALVES)] + [result_step("C", h, 3, 4) for h in range(HALVES)]
         vector.append(free_step(lambda: nc.vector.transpose(out=d_turned[:], in_=d_rows[:])))
         vector.append(piece_out_step(on_vector[0], "V"))
         vector.append(free_step(lambda: nc.vector.reciprocal(out=d_rec[:], in_=d_turned[:, 0:256:32])))

@@ -113,8 +113,8 @@ def tile_concord_precision_gradient_s12_kernel(tc, a_words, a_scales, b_words, b
             if it not in woven:
                 woven[it] = sbuf("woven%s%d%d" % it, [P, 2048], BF16, tag)
             if it[0] == "W":
-                dst = woven[it][:].rearrange("p (u q w t) -> p u q t w", u=SLOTS, w=RUN, t=SLOTS)[:, lo:hi]
-                src = raw[it].rearrange("p t (q u w) -> p u q t w", u=SLOTS, w=RUN)[:, lo:hi]
+                dst = woven[it][:].rearrange("p (u q w t) -> p q u t w", u=SLOTS, w=RUN, t=SLOTS)[:, :, lo:hi]
+                src = raw[it].rearrange("p t (q u w) -> p q u t w", u=SLOTS, w=RUN)[:, :, lo:hi]
             else:
                 dst = woven[it][:].rearrange("p (a w t) -> p a t w", w=RUN, t=SLOTS)[:, P // RUN * lo : P // RUN * hi]
                 src = raw[it].rearrange("p t (a w) -> p a t w", w=RUN)[:, P // RUN * lo : P // RUN * hi]

@@ -23,7 +23,6 @@ BLOCKS = 4
 WIDTH = 256
 RUN = 8
 BANKS = 8
-WARM_UPS = 8
 WOVEN_TILES = 6
 BANKS_BEFORE_XW, BANKS_BEFORE_X = 8, 10
 WHOLE, FIRST, SECOND = (0, 4), (0, 2), (2, 4)
@@ -261,12 +260,6 @@ def tile_concord_precision_gradient_s12_kernel(tc, a_words, a_scales, b_words, b
 
         nc.vector.memset(a_sc[:].bitcast(I32), 0)
         nc.vector.memset(b_sc_all[:].bitcast(I32), 0)
-        idle_codes = sbuf("idle_codes", [P, WIDTH], U32)
-        idle_sc = sbuf("idle_sc", [P, WIDTH], U8)
-        nc.vector.quantize_mx(out=idle_codes[:].bitcast(FP8X4), scales=idle_sc[:], in_=b_sc_all[:].bitcast(BF16))
-        idle = bank(BANKS - 1)
-        for k in range(WARM_UPS):
-            nc.tensor.matmul_mx(out=idle[:, 0:WIDTH], lhsT=idle_codes[:, 0:P].bitcast(FP8X4), lhsT_scale=idle_sc[:, 0:P], rhs=idle_codes[:].bitcast(FP8X4), rhs_scale=idle_sc[:], start=True, stop=True)
         nc.gpsimd.memset(d_rows[:], 0.0)
         nc.gpsimd.dma_start(out=d_rows[0:P:32, :].rearrange("q (b a) -> q b a", a=32), in_=d.rearrange("(b q a) -> q b a", q=4, a=32))
         nc.gpsimd.memset(ident_wide[:], 0.0)

@@ -23,9 +23,8 @@ BLOCKS = 4
 WIDTH = 256
 RUN = 8
 BANKS = 8
-WOVEN_TILES = 6
-BANKS_BEFORE_XW, BANKS_BEFORE_X = 8, 10
-WHOLE, FIRST, SECOND = (0, 4), (0, 2), (2, 4)
+WOVEN_PAIRS = 4
+WOVEN_UNITS = 8
 
 
 def tile_concord_precision_gradient_s12_kernel(tc, a_words, a_scales, b_words, b_scales, xw, x, d, out):
@@ -49,16 +48,16 @@ def tile_concord_precision_gradient_s12_kernel(tc, a_words, a_scales, b_words, b
             else:
                 nc.vector.tensor_copy(out=dst, in_=src)
 
-        a_codes = [sbuf("a_codes%d" % q, [P, 2, 1024], U8) for q in range(2)]
+        a_ranges = [(0, 256), (256, 512), (512, 1024)]
+        a_codes = [sbuf("a_codes%d" % lo, [P, 2, 2 * (hi - lo)], U8) for lo, hi in a_ranges]
         a_sc = sbuf("a_sc", [P, 2, 1024], U8)
         b_raw = [sbuf("b_raw%d" % h, [P, 2, 1024], U8) for h in range(HALVES)]
         b_codes = [sbuf("b_codes%d" % h, [P, 2, 1024], U8) for h in range(HALVES)]
-        b_sc_raw = sbuf("b_sc_raw", [P, 2, 1024], U8)
-        b_sc_all = sbuf("b_sc", [P, HALVES * 1024], U8)
-        b_sc = [b_sc_all[:, h * 1024 : (h + 1) * 1024].rearrange("p (g n) -> p g n", g=2) for h in range(HALVES)]
-        tiles = [(kind, z, c) for kind in "WX" for z in range(2) for c in range(CHUNKS)]
-        codes = {it: sbuf("codes%s%d%d" % it, [P, 512], U32) for it in tiles}
-        scales = {it: sbuf("scales%s%d%d" % it, [P, 512], U8) for it in tiles}
+        b_sc_raw = [sbuf("b_sc_raw%d" % h, [P, 2, 512], U8) for h in range(HALVES)]
+        b_sc = [sbuf("b_sc%d" % h, [P, 2, 512], U8) for h in range(HALVES)]
+        pairs = [(kind, k, c) for kind in "WX" for k in range(2) for c in range(CHUNKS)]
+        codes = {it: sbuf("codes%s%d%d" % it, [P, 512], U32) for it in pairs}
+        scales = {it: sbuf("scales%s%d%d" % it, [P, 512], U8) for it in pairs}
         o_codes = [sbuf("o_codes%d" % h, [P, 1024], U32) for h in range(HALVES)]
         o_sc = [sbuf("o_sc%d" % h, [P, 1024], U8) for h in range(HALVES)]
         c_codes = [sbuf("c_codes%d" % h, [P, 1024], U32) for h in range(HALVES)]
@@ -73,69 +72,60 @@ def tile_concord_precision_gradient_s12_kernel(tc, a_words, a_scales, b_words, b
         d_neg = sbuf("d_neg", [P, 8], F32)
         raw, woven, ps, g_sb, spent = {}, {}, {}, {}, []
 
-        def load_codes(dst, src, z):
-            nc.sync.dma_start(out=dst[:].bitcast(I32), in_=src[:, :, z * 1024 : (z + 1) * 1024].bitcast(I32).rearrange("g p n -> p g n"))
+        def load_codes(dst, src, lo, hi):
+            nc.sync.dma_start(out=dst[:].bitcast(I32), in_=src[:, :, 2 * lo : 2 * hi].bitcast(I32).rearrange("g p n -> p g n"))
 
-        def load_scales(dst, src, rows):
+        def load_scales(dst, src, lo, hi, rows=range(4)):
             for r in rows:
-                nc.sync.dma_start(out=dst[r:P:32, :, :].bitcast(I32), in_=src[:, r:16:4, :].bitcast(I32).rearrange("g q n -> q g n"))
+                nc.sync.dma_start(out=dst[r:P:32, :, :].bitcast(I32), in_=src[:, r:16:4, lo:hi].bitcast(I32).rearrange("g q n -> q g n"))
 
         def load_rows(kind, c, lo, hi):
-            first = lo // 512
-            if lo % 512 == 0:
-                count = max(1, (hi - lo) // 512)
-                name = "raw%s%d%d" % (kind, first, c)
-                spent.append(name)
-                raw["load", kind, first, c] = sbuf(name, [P, SLOTS, count * 512], BF16)
-                for k in range(count):
-                    raw[kind, first + k, c] = raw["load", kind, first, c][:, :, k * 512 : (k + 1) * 512]
-            src = (xw if kind == "W" else x)[c * 512 : (c + 1) * 512, lo:hi]
-            nc.sync.dma_start(out=raw["load", kind, first, c][:, :, lo - first * 512 : hi - first * 512], in_=src.rearrange("(p t) w -> p t w", t=SLOTS))
+            name = "raw%s%d%d" % (kind, lo, c)
+            spent.append(name)
+            t = sbuf(name, [P, SLOTS, (hi - lo) * WIDTH], BF16)
+            for n in range(lo, hi):
+                raw[kind, n, c] = t[:] if kind == "W" else t[:, :, (n - lo) * WIDTH : (n - lo + 1) * WIDTH]
+            if hi - lo == 2:
+                raw[kind, lo, c, "pair"] = t[:]
+            src = (xw if kind == "W" else x)[c * 512 : (c + 1) * 512, lo * WIDTH : hi * WIDTH]
+            nc.sync.dma_start(out=t[:], in_=src.rearrange("(p t) w -> p t w", t=SLOTS))
 
-        def sort_b_scales(h):
-            cols = slice(h * 512, (h + 1) * 512)
-            for quadrant in range(4):
-                rows = slice(32 * quadrant, 32 * quadrant + 4)
-                nc.vector.tensor_copy(
-                    out=b_sc[h][rows].bitcast(I32).rearrange("p g (u q w) -> p g u q w", u=SLOTS, w=RUN // 4),
-                    in_=b_sc_raw[rows, :, cols].bitcast(I32).rearrange("p g (q u w) -> p g u q w", u=SLOTS, w=RUN // 4),
-                )
-
-        def sort_b_codes(h):
+        def sort_b(dst, src, words, rows=slice(0, P)):
             nc.vector.tensor_copy(
-                out=b_codes[h][:].bitcast(I32).rearrange("p g (u q w) -> p g u q w", u=SLOTS, w=RUN // 2),
-                in_=b_raw[h][:].bitcast(I32).rearrange("p g (q u w) -> p g u q w", u=SLOTS, w=RUN // 2),
+                out=dst[rows].bitcast(I32).rearrange("p g (u q w) -> p g u q w", u=SLOTS, w=words),
+                in_=src[rows].bitcast(I32).rearrange("p g (q u w) -> p g u q w", u=SLOTS, w=words),
             )
 
-        def weave(it, tag, eng, part):
-            lo, hi = part
-            if it not in woven:
-                woven[it] = sbuf("woven%s%d%d" % it, [P, 2048], BF16, tag)
-            if it[0] == "W":
-                dst = woven[it][:].rearrange("p (u q w t) -> p q u t w", u=SLOTS, w=RUN, t=SLOTS)[:, :, lo:hi]
-                src = raw[it].rearrange("p t (q u w) -> p q u t w", u=SLOTS, w=RUN)[:, :, lo:hi]
+        def weave(kind, n, c, count, eng):
+            dst = woven[kind, n, c, count]
+            if kind == "W":
+                lo = 2 * (n % 2)
+                dst = dst.rearrange("p (u q w t) -> p q u t w", u=2 * count, w=RUN, t=SLOTS)
+                src = raw[kind, n, c].rearrange("p t (q u w) -> p q u t w", u=SLOTS, w=RUN)[:, :, lo : lo + 2 * count]
             else:
-                dst = woven[it][:].rearrange("p (a w t) -> p a t w", w=RUN, t=SLOTS)[:, P // RUN * lo : P // RUN * hi]
-                src = raw[it].rearrange("p t (a w) -> p a t w", w=RUN)[:, P // RUN * lo : P // RUN * hi]
+                dst = dst.rearrange("p (a w t) -> p a t w", w=RUN, t=SLOTS)
+                src = (raw[kind, n, c, "pair"] if count == 2 else raw[kind, n, c]).rearrange("p t (a w) -> p a t w", w=RUN)
             copy(eng, dst, src)
 
-        def quantise(it, part):
-            lo, hi = part
-            nc.vector.quantize_mx(out=codes[it][:, lo * P : hi * P].bitcast(FP8X4), scales=scales[it][:, lo * P : hi * P], in_=woven[it][:, lo * 512 : hi * 512])
+        def quantise(kind, n, c, count):
+            cols = slice((n % 2) * WIDTH, (n % 2 + count) * WIDTH)
+            nc.vector.quantize_mx(out=codes[kind, n // 2, c][:, cols].bitcast(FP8X4), scales=scales[kind, n // 2, c][:, cols], in_=woven[kind, n, c, count])
 
         def slots_out(eng, dst, src, count):
             copy(eng, dst.rearrange("p (n e) u -> p n u e", e=2), src[:].rearrange("p (u n e) -> p n u e", u=count, e=2))
 
-        def omega(h, b):
-            t = bank(b)
+        def omega(h, b, k):
+            t = bank(k)
             ps["O", h, b] = t
+            q = min(b // 2, 2)
+            lo = b * P - a_ranges[q][0]
             for u in range(SLOTS):
                 for g in range(2):
                     nc.tensor.matmul_mx(
                         out=t[:, u * P : (u + 1) * P],
                         lhsT=b_codes[h][:, g, u * 256 : (u + 1) * 256].bitcast(FP4X4),
                         lhsT_scale=b_sc[h][:, g, u * P : (u + 1) * P],
-                        rhs=a_codes[b // 4][:, g, (b % 4) * 256 : (b % 4 + 1) * 256].bitcast(FP4X4),
+                        rhs=a_codes[q][:, g, 2 * lo : 2 * (lo + P)].bitcast(FP4X4),
                         rhs_scale=a_sc[:, g, b * P : (b + 1) * P],
                         start=(g == 0),
                         stop=(g == 1),
@@ -145,34 +135,29 @@ def tile_concord_precision_gradient_s12_kernel(tc, a_words, a_scales, b_words, b
             lo = (b % 4) * P
             slots_out("S", o_words[h, b // 4][:, lo : lo + P, :], ps["O", h, b], SLOTS)
 
-        def four_slots(s, h):
-            return s == 0 and h == 0
+        def shape_of(it):
+            h, z, n = it
+            return (range(SLOTS), n * P, P) if z == "four" else (range(2 * z, 2 * z + 2), n * WIDTH, WIDTH)
 
-        def cov(s, c, h, first_bank, n):
-            it = ("X", s // 2, c)
-            for z in range(2):
-                if n == 0:
-                    ps["C", s, h, z] = bank(first_bank + z)
-                slots = range(SLOTS) if four_slots(s, h) else range(2 * z, 2 * z + 2)
-                width = 512 // len(slots)
-                lo = (s % 2) * WIDTH + (z * P if four_slots(s, h) else 0)
-                for e, u in enumerate(slots):
-                    nc.tensor.matmul_mx(
-                        out=ps["C", s, h, z][:, e * width : (e + 1) * width],
-                        lhsT=codes["W", h, c][:, u * P : (u + 1) * P].bitcast(FP8X4),
-                        lhsT_scale=scales["W", h, c][:, u * P : (u + 1) * P],
-                        rhs=codes[it][:, lo : lo + width].bitcast(FP8X4),
-                        rhs_scale=scales[it][:, lo : lo + width],
-                        start=(n == 0 and e == 0),
-                        stop=(n == LAST and e == len(slots) - 1),
-                    )
+        def cov(it, c, k):
+            if c == 0:
+                ps["C", it] = bank(k)
+            slots, lo, width = shape_of(it)
+            cols = slice(lo % 512, lo % 512 + width)
+            for e, u in enumerate(slots):
+                nc.tensor.matmul_mx(
+                    out=ps["C", it][:, e * width : (e + 1) * width],
+                    lhsT=codes["W", it[0], c][:, u * P : (u + 1) * P].bitcast(FP8X4),
+                    lhsT_scale=scales["W", it[0], c][:, u * P : (u + 1) * P],
+                    rhs=codes["X", lo // 512, c][:, cols].bitcast(FP8X4),
+                    rhs_scale=scales["X", lo // 512, c][:, cols],
+                    start=(c == 0 and e == 0),
+                    stop=(c == LAST and e == len(slots) - 1),
+                )
 
-        def cov_out(s, h, z, eng):
-            lo = (s % 2) * WIDTH
-            if four_slots(s, h):
-                slots_out(eng, c_words[h, s // 2][:, lo + z * P : lo + (z + 1) * P, :], ps["C", s, h, z], SLOTS)
-            else:
-                slots_out(eng, c_words[h, s // 2][:, lo : lo + WIDTH, 2 * z : 2 * z + 2], ps["C", s, h, z], 2)
+        def cov_out(it, eng):
+            slots, lo, width = shape_of(it)
+            slots_out(eng, c_words[it[0], lo // 512][:, lo % 512 : lo % 512 + width, slots[0] : slots[-1] + 1], ps["C", it], len(slots))
 
         def quantise_result(kind, h, lo, hi):
             dst, sc, src = (o_codes, o_sc, o_words) if kind == "O" else (c_codes, c_sc, c_words)
@@ -258,52 +243,68 @@ def tile_concord_precision_gradient_s12_kernel(tc, a_words, a_scales, b_words, b
             elif piece[1] % 2:
                 store_square(g_sb["square", piece[1] // 2, piece[2]], piece[1] // 2, piece[2])
 
-        nc.vector.memset(a_sc[:].bitcast(I32), 0)
-        nc.vector.memset(b_sc_all[:].bitcast(I32), 0)
-        nc.gpsimd.memset(d_rows[:], 0.0)
-        nc.gpsimd.dma_start(out=d_rows[0:P:32, :].rearrange("q (b a) -> q b a", a=32), in_=d.rearrange("(b q a) -> q b a", q=4, a=32))
+
+        for t in (a_sc, b_sc[0], b_sc_raw[1]):
+            nc.vector.memset(t[:].bitcast(I32), 0)
         nc.gpsimd.memset(ident_wide[:], 0.0)
         make_identity(nc, ident, nomemset=True)
+        nc.gpsimd.memset(d_rows[:], 0.0)
+        nc.gpsimd.dma_start(out=d_rows[0:P:32, :].rearrange("q (b a) -> q b a", a=32), in_=d.rearrange("(b q a) -> q b a", q=4, a=32))
 
-        load_scales(b_sc_raw, b_scales, range(4))
-        load_codes(b_raw[0], b_words, 0)
-        load_scales(a_sc, a_scales, range(2))
-        load_codes(a_codes[0], a_words, 0)
-        load_scales(a_sc, a_scales, range(2, 4))
-        load_rows("W", 0, 0, 512)
-        load_codes(a_codes[1], a_words, 1)
-        load_rows("X", 0, 0, 512)
-        load_codes(b_raw[1], b_words, 1)
+        load_scales(b_sc_raw[0], b_scales, 0, 512)
+        load_codes(b_raw[0], b_words, 0, 512)
+        load_scales(a_sc, a_scales, 0, 1024, range(2))
+        load_codes(a_codes[0], a_words, 0, 256)
+        load_scales(a_sc, a_scales, 0, 1024, range(2, 4))
+        load_rows("W", 0, 0, 2)
+        load_codes(a_codes[1], a_words, 256, 512)
+        load_rows("X", 0, 0, 2)
+        load_codes(a_codes[2], a_words, 512, 1024)
+        load_scales(b_sc_raw[1], b_scales, 512, 1024)
+        load_codes(b_raw[1], b_words, 512, 1024)
         for c in range(1, CHUNKS):
-            load_rows("W", c, 0, 1024)
-            load_rows("X", c, 0, 512)
-        load_rows("W", 0, 512, 1024)
-        for s in range(2, BLOCKS):
+            load_rows("W", c, 0, 2)
+            load_rows("X", c, 0, 2)
+        for kind, lo, hi in (("X", 2, 3), ("W", 2, 4), ("X", 3, 4)):
             for c in range(CHUNKS):
-                load_rows("X", c, s * WIDTH, (s + 1) * WIDTH)
+                load_rows(kind, c, lo, hi)
 
         tensor, vector, scalar, stores = [], [], [], []
-        need = [("W", 0, 0), ("X", 0, 0)] + [it for c in range(1, LAST) for it in (("W", 0, c), ("W", 1, c), ("X", 0, c))]
-        need += [("W", 0, LAST), ("X", 0, LAST), ("W", 1, LAST), ("W", 1, 0)] + [("X", 1, c) for c in range(CHUNKS)]
         holders = {}
+        first_pairs = [(kind, 0, c) for c in range(CHUNKS) for kind in "WX"]
+        late_units = [(kind, n, c) for kind, n in (("X", 2), ("W", 2), ("W", 3), ("X", 3)) for c in range(CHUNKS)]
 
-        def weave_step(it, part, eng):
-            k = need.index(it)
-            frees = [("quantised", need[k - WOVEN_TILES], n) for n in range(4)] if k >= WOVEN_TILES else []
-            return ([("woven", it, n) for n in range(*part)], frees, lambda: weave(it, "woven%d" % (k % WOVEN_TILES), eng, part))
+        def open_woven(kind, n, c):
+            if n < 2 and (kind, 0, c, 2) not in woven:
+                k = first_pairs.index((kind, 0, c))
+                t = sbuf("woven%s%d" % (kind, c), [P, 2048], BF16, "woven_pair%d" % (k % WOVEN_PAIRS))
+                woven[kind, 0, c, 2], woven[kind, 0, c, 1], woven[kind, 1, c, 1] = t[:], t[:, 0:1024], t[:, 1024:2048]
+            elif n >= 2:
+                k = late_units.index((kind, n, c))
+                t = sbuf("woven%s%d%d" % (kind, n, c), [P, 1024], BF16, "woven_unit%d" % (k % WOVEN_UNITS))
+                woven[kind, n, c, 1] = t[:]
 
-        def quantise_step(it, part):
-            return ([("quantised", it, n) for n in range(*part)], [("woven", it, n) for n in range(*part)], lambda: quantise(it, part))
+        def weave_step(kind, n, c, count, eng):
+            if n < 2:
+                k = first_pairs.index((kind, 0, c)) - WOVEN_PAIRS
+                frees = [("quantised", first_pairs[k][0], e, first_pairs[k][2]) for e in range(2)] if k >= 0 else []
+            else:
+                k = late_units.index((kind, n, c)) - WOVEN_UNITS
+                frees = [("quantised",) + late_units[k]] if k >= 0 else []
+            return ([("woven", kind, n + e, c) for e in range(count)], frees, lambda: (open_woven(kind, n, c), weave(kind, n, c, count, eng)))
+
+        def quantise_step(kind, n, c, count):
+            return ([("quantised", kind, n + e, c) for e in range(count)], [("woven", kind, n + e, c) for e in range(count)], lambda: quantise(kind, n, c, count))
 
         def result_step(kind, h, lo, hi):
             if kind == "O":
                 waits = [("out", "O", h, b) for b in range(2 * lo, 2 * hi)]
             else:
-                waits = [("out", "C", s, h, z) for s in range(lo, hi) for z in range(2)]
+                waits = [("out", "C", it) for region in regions for it in region if it[0] == h and lo <= shape_of(it)[1] // WIDTH < hi]
             return ([("quantised", kind, h, s) for s in range(lo, hi)], waits, lambda: quantise_result(kind, h, lo, hi))
 
-        def cov_out_step(s, h, z, eng):
-            return ([("out", "C", s, h, z)], [("made", "C", s, LAST, h)], lambda: cov_out(s, h, z, eng))
+        def cov_out_step(it, eng):
+            return ([("out", "C", it)], [("made", "C", it, LAST)], lambda: cov_out(it, eng))
 
         def piece_out_step(piece, eng):
             return ([("out",) + piece], [("made",) + piece], lambda: piece_out(piece, eng))
@@ -311,18 +312,24 @@ def tile_concord_precision_gradient_s12_kernel(tc, a_words, a_scales, b_words, b
         def free_step(call):
             return ([], [], call)
 
-        def take_bank(k, emptied_by):
-            waits = holders.get(k, [])
-            holders[k] = [emptied_by]
-            return waits
+        def take_bank(emptied_by):
+            k = len(holders) % BANKS
+            waits = [holders[len(holders) - BANKS]] if len(holders) >= BANKS else []
+            holders[len(holders)] = emptied_by
+            return k, waits
 
-        def cov_step(s, c, h, first_bank, n):
-            waits = [("quantised", ("W", h, c), u) for u in range(4)] + [("quantised", ("X", s // 2, c), 2 * (s % 2) + e) for e in range(2)]
-            if n == 0:
-                waits += [w for z in range(2) for w in take_bank(first_bank + z, ("out", "C", s, h, z))]
-            return ([("made", "C", s, n, h)], waits, lambda: cov(s, c, h, first_bank, n))
+        def omega_step(h, b):
+            k, waits = take_bank(("out", "O", h, b))
+            return ([("made", "O", h, b)], [("sorted", h)] + waits, lambda: omega(h, b, k))
 
-        def piece_step(piece, k):
+        def cov_step(it, c):
+            k, waits = take_bank(("out", "C", it)) if c == 0 else (None, [])
+            slots, lo, width = shape_of(it)
+            waits += [("quantised", "W", 2 * it[0] + u // 2, c) for u in slots] + [("quantised", "X", lo // WIDTH, c)]
+            return ([("made", "C", it, c)], waits, lambda: cov(it, c, k))
+
+        def piece_step(piece):
+            k, free = take_bank(("out",) + piece)
             if piece[0] != "mirror":
                 top = piece[1] if piece[0] == "square" else piece[1] // 2
                 waits = [("quantised", kind, h, s) for kind in "OC" for h in range(HALVES) for s in range(top + 1)]
@@ -330,65 +337,59 @@ def tile_concord_precision_gradient_s12_kernel(tc, a_words, a_scales, b_words, b
                 waits = [("out", "square", 1, 0)]
             else:
                 waits = [("out", "wide", 2 * piece[2] + e) if piece[1] < 2 else ("out", "row", 6 + e, 2) for e in range(2)]
-            return ([("made",) + piece], waits + take_bank(k, ("out",) + piece), lambda: make_piece(piece, k))
+            return ([("made",) + piece], waits + free, lambda: make_piece(piece, k))
 
-        for h in range(HALVES):
-            for b in range(BANKS):
-                tensor.append(([("made", "O", h, b)], [("sorted", h)] + take_bank(b, ("out", "O", h, b)), lambda h=h, b=b: omega(h, b)))
-        passes = [(0, 0)] + [(c, h) for c in range(1, CHUNKS) for h in range(HALVES)] + [(0, 1)]
-        for k, (c, h) in enumerate(passes):
-            done = len([1 for other in passes[:k] if other[1] == h])
-            tensor.extend(cov_step(s, c, h, 4 * h + 2 * s, done) for s in range(2))
-        for s in range(2, BLOCKS):
-            tensor.extend(cov_step(s, c, h, 4 * (s - 2) + 2 * h, c) for c in range(CHUNKS) for h in range(HALVES))
+        tensor.extend(omega_step(h, b) for h in range(HALVES) for b in range(BANKS))
+        regions = [[(0, "four", b) for b in range(4)], [(0, "four", b) for b in (4, 5)], [(1, 0, s) for s in range(3)], [(1, 1, s) for s in range(3)]]
+        regions.append([(h, z, 3) for h in range(HALVES) for z in range(2)])
+        for region in regions:
+            tensor.extend(cov_step(it, c) for c in range(CHUNKS) for it in region)
         pieces = [("square", 1, 0), ("wide", 4), ("wide", 5), ("wide", 6), ("mirror", 0, 1), ("mirror", 0, 2), ("mirror", 1, 2)]
         pieces += [("wide", 7), ("row", 6, 2), ("row", 7, 2), ("square", 0, 0)] + [("mirror", r, 3) for r in range(3)]
         pieces += [("square", 1, 1), ("square", 2, 2), ("row", 6, 3), ("row", 7, 3)]
-        tensor.extend(piece_step(piece, k % BANKS) for k, piece in enumerate(pieces))
+        tensor.extend(piece_step(piece) for piece in pieces)
         stores.extend(([], [("out",) + piece], lambda piece=piece: store_piece(piece)) for piece in pieces)
 
-        early = {BANKS_BEFORE_XW: ("W", 1, 1), BANKS_BEFORE_X: ("X", 0, 1)}
-        late = [("X", 0, LAST - 1), ("W", 0, LAST), ("X", 0, LAST), ("W", 1, LAST), ("W", 1, 0)]
-        for n in range(HALVES * BANKS):
+        def omega_out_step(n):
             h, b = divmod(n, BANKS)
-            if n in early:
-                scalar.append(weave_step(early[n], SECOND, "S"))
-            scalar.append(([("out", "O", h, b)], [("made", "O", h, b)], lambda h=h, b=b: omega_out(h, b)))
-        scalar.extend(weave_step(it, SECOND, "S") for it in late)
-        scalar.extend(cov_out_step(s, h, z, "S") for h in range(HALVES) for s in range(2) for z in range(2))
-        scalar.extend(weave_step(("X", 1, c), SECOND, "S") for c in range(2, CHUNKS))
-        scalar.extend(cov_out_step(2, h, z, "S") for h in range(HALVES) for z in range(2))
-        scalar.extend(cov_out_step(3, h, 0, "S") for h in range(HALVES))
+            return ([("out", "O", h, b)], [("made", "O", h, b)], lambda: omega_out(h, b))
+
+        cov_banks = [it for region in regions for it in region]
+        theirs = []
+        for what, it in [("O", (0, 8)), ("w", ("X", 1, 1)), ("O", (8, 12)), ("w", ("X", 1, 2)), ("w", ("W", 1, 3)), ("w", ("X", 1, 3)), ("O", (12, 14)), ("w", ("X", 2, 3)), ("O", (14, 16)), ("C", (0, 1)), ("w", ("W", 2, 2)), ("C", (1, 4)), ("w", ("W", 3, 1)), ("C", (4, 6)), ("w", ("W", 3, 3)), ("C", (6, 8)), ("w", ("X", 3, 2)), ("C", (8, 12))]:
+            if what == "O":
+                scalar.extend(omega_out_step(n) for n in range(*it))
+            elif what == "C":
+                scalar.extend(cov_out_step(b, "S") for b in cov_banks[it[0] : it[1]])
+            else:
+                theirs.append(it)
+                scalar.append(weave_step(*it, 1, "S"))
+        scalar.extend(cov_out_step(it, "S") for it in regions[-1][0::2])
         on_vector = [piece for piece in pieces if on_diagonal(piece) or piece in (("wide", 6), ("wide", 7), ("mirror", 0, 2), ("mirror", 1, 3))]
         scalar.extend(piece_out_step(piece, "S") for piece in pieces if piece not in on_vector)
 
-        def mine(it):
-            return weave_step(it, FIRST if it in late or it in early.values() else WHOLE, "V")
-
-        vector.append(free_step(lambda: sort_b_scales(0)))
-        vector.append(([("sorted", 0)], [], lambda: sort_b_codes(0)))
-        vector.append(free_step(lambda: sort_b_scales(1)))
-        vector += [mine(("W", 0, 0)), quantise_step(("W", 0, 0), WHOLE), weave_step(("X", 0, 0), FIRST, "V")]
-        vector.append(([("sorted", 1)], [], lambda: sort_b_codes(1)))
-        vector += [weave_step(("X", 0, 0), SECOND, "V"), quantise_step(("X", 0, 0), FIRST), quantise_step(("X", 0, 0), SECOND)]
-        for c in range(1, CHUNKS):
-            w0, w1, xc = ("W", 0, c), ("W", 1, c), ("X", 0, c)
-            vector.append(mine(w0))
-            if c > 1:
-                vector.append(quantise_step(("X", 0, c - 1), SECOND))
-            vector.append(mine(w1))
-            if c < LAST:
-                vector += [quantise_step(w0, WHOLE), mine(xc), quantise_step(w1, WHOLE), quantise_step(xc, FIRST)]
-            else:
-                vector += [mine(xc), quantise_step(w0, WHOLE), quantise_step(xc, FIRST), quantise_step(xc, SECOND)]
-        behind = quantise_step(("W", 1, LAST), WHOLE)
-        for it, part in [(("W", 1, 0), WHOLE)] + [(("X", 1, c), FIRST) for c in range(CHUNKS)] + [(("X", 1, c), SECOND) for c in range(2)]:
-            vector += [weave_step(it, FIRST if it in late else part, "V"), behind]
-            behind = quantise_step(it, part)
-        vector += [result_step("O", 0, 0, 2), behind, result_step("O", 1, 0, 2), quantise_step(("X", 1, 2), SECOND)]
-        vector += [result_step("C", 0, 0, 2), quantise_step(("X", 1, 3), SECOND), result_step("C", 1, 0, 2)]
+        vector.extend(free_step(lambda q=q: sort_b(b_sc[0], b_sc_raw[0], RUN // 4, slice(32 * q, 32 * q + 4))) for q in range(4))
+        vector.append(([("sorted", 0)], [], lambda: sort_b(b_codes[0], b_raw[0], RUN // 2)))
+        behind = []
+        for kind, n, c in first_pairs:
+            vector.append(weave_step(kind, 0, c, 1 if (kind, 1, c) in theirs else 2, "V"))
+            vector.extend(behind)
+            behind = [quantise_step(kind, 0, c, 2)]
+            if (kind, c) == ("X", 0):
+                vector.extend(behind)
+                behind = []
+                vector.append(free_step(lambda: sort_b(b_sc[1], b_sc_raw[1], RUN // 4)))
+                vector.append(([("sorted", 1)], [], lambda: sort_b(b_codes[1], b_raw[1], RUN // 2)))
+        vector += [quantise_step("X", e, LAST, 1) for e in range(2)]
+        behind = []
+        for it in late_units:
+            if it not in theirs:
+                vector.append(weave_step(*it, 1, "V"))
+            vector.extend(behind)
+            behind = [quantise_step(*it, 1)]
+        vector += [result_step("O", 0, 0, 2)] + behind + [result_step("O", 1, 0, 2)] + [result_step("C", h, 0, 2) for h in range(HALVES)]
         vector += [result_step("O", h, 2, 4) for h in range(HALVES)] + [result_step("C", h, 2, 3) for h in range(HALVES)]
-        vector += [cov_out_step(3, h, 1, "V") for h in range(HALVES)] + [result_step("C", h, 3, 4) for h in range(HALVES)]
+        vector += [cov_out_step(it, "V") for it in regions[-1][1::2]] + [result_step("C", h, 3, 4) for h in range(HALVES)]
         vector.append(free_step(lambda: nc.vector.transpose(out=d_turned[:], in_=d_rows[:])))
         vector.append(piece_out_step(on_vector[0], "V"))
         vector.append(free_step(lambda: nc.vector.reciprocal(out=d_rec[:], in_=d_turned[:, 0:256:32])))

@@ -23,8 +23,9 @@ BLOCKS = 4
 WIDTH = 256
 RUN = 8
 BANKS = 8
+WARM_UPS = 8
 WOVEN_PAIRS = 4
-WOVEN_UNITS = 8
+WOVEN_UNITS = 10
 
 
 def tile_concord_precision_gradient_s12_kernel(tc, a_words, a_scales, b_words, b_scales, xw, x, d, out):
@@ -48,13 +49,15 @@ def tile_concord_precision_gradient_s12_kernel(tc, a_words, a_scales, b_words, b
             else:
                 nc.vector.tensor_copy(out=dst, in_=src)
 
-        a_ranges = [(0, 256), (256, 512), (512, 1024)]
+        a_ranges = [(0, 512), (512, 1024)]
         a_codes = [sbuf("a_codes%d" % lo, [P, 2, 2 * (hi - lo)], U8) for lo, hi in a_ranges]
         a_sc = sbuf("a_sc", [P, 2, 1024], U8)
         b_raw = [sbuf("b_raw%d" % h, [P, 2, 1024], U8) for h in range(HALVES)]
         b_codes = [sbuf("b_codes%d" % h, [P, 2, 1024], U8) for h in range(HALVES)]
-        b_sc_raw = [sbuf("b_sc_raw%d" % h, [P, 2, 512], U8) for h in range(HALVES)]
-        b_sc = [sbuf("b_sc%d" % h, [P, 2, 512], U8) for h in range(HALVES)]
+        b_sc_rows = sbuf("b_sc_rows", [P, 2, 1024], U8)
+        b_sc_raw = [b_sc_rows[:, :, h * 512 : (h + 1) * 512] for h in range(HALVES)]
+        b_sc_all = sbuf("b_sc", [P, 2048], U8)
+        b_sc = [b_sc_all[:, h * 1024 : (h + 1) * 1024].rearrange("p (g n) -> p g n", g=2) for h in range(HALVES)]
         pairs = [(kind, k, c) for kind in "WX" for k in range(2) for c in range(CHUNKS)]
         codes = {it: sbuf("codes%s%d%d" % it, [P, 512], U32) for it in pairs}
         scales = {it: sbuf("scales%s%d%d" % it, [P, 512], U8) for it in pairs}
@@ -84,7 +87,7 @@ def tile_concord_precision_gradient_s12_kernel(tc, a_words, a_scales, b_words, b
             spent.append(name)
             t = sbuf(name, [P, SLOTS, (hi - lo) * WIDTH], BF16)
             for n in range(lo, hi):
-                raw[kind, n, c] = t[:] if kind == "W" else t[:, :, (n - lo) * WIDTH : (n - lo + 1) * WIDTH]
+                raw[kind, n, c] = t[:, :, (n - lo) // 2 * 512 : (n - lo) // 2 * 512 + 512] if kind == "W" else t[:, :, (n - lo) * WIDTH : (n - lo + 1) * WIDTH]
             if hi - lo == 2:
                 raw[kind, lo, c, "pair"] = t[:]
             src = (xw if kind == "W" else x)[c * 512 : (c + 1) * 512, lo * WIDTH : hi * WIDTH]
@@ -117,7 +120,7 @@ def tile_concord_precision_gradient_s12_kernel(tc, a_words, a_scales, b_words, b
         def omega(h, b, k):
             t = bank(k)
             ps["O", h, b] = t
-            q = min(b // 2, 2)
+            q = b // 4
             lo = b * P - a_ranges[q][0]
             for u in range(SLOTS):
                 for g in range(2):
@@ -139,8 +142,8 @@ def tile_concord_precision_gradient_s12_kernel(tc, a_words, a_scales, b_words, b
             h, z, n = it
             return (range(SLOTS), n * P, P) if z == "four" else (range(2 * z, 2 * z + 2), n * WIDTH, WIDTH)
 
-        def cov(it, c, k):
-            if c == 0:
+        def cov(it, c, n, k):
+            if n == 0:
                 ps["C", it] = bank(k)
             slots, lo, width = shape_of(it)
             cols = slice(lo % 512, lo % 512 + width)
@@ -151,8 +154,8 @@ def tile_concord_precision_gradient_s12_kernel(tc, a_words, a_scales, b_words, b
                     lhsT_scale=scales["W", it[0], c][:, u * P : (u + 1) * P],
                     rhs=codes["X", lo // 512, c][:, cols].bitcast(FP8X4),
                     rhs_scale=scales["X", lo // 512, c][:, cols],
-                    start=(c == 0 and e == 0),
-                    stop=(c == LAST and e == len(slots) - 1),
+                    start=(n == 0 and e == 0),
+                    stop=(n == LAST and e == len(slots) - 1),
                 )
 
         def cov_out(it, eng):
@@ -244,35 +247,40 @@ def tile_concord_precision_gradient_s12_kernel(tc, a_words, a_scales, b_words, b
                 store_square(g_sb["square", piece[1] // 2, piece[2]], piece[1] // 2, piece[2])
 
 
-        for t in (a_sc, b_sc[0], b_sc_raw[1]):
+        for t in (a_sc, b_sc_all):
             nc.vector.memset(t[:].bitcast(I32), 0)
+        idle_codes = sbuf("idle_codes", [P, WIDTH], U32)
+        idle_sc = sbuf("idle_sc", [P, WIDTH], U8)
+        nc.vector.quantize_mx(out=idle_codes[:].bitcast(FP8X4), scales=idle_sc[:], in_=b_sc_all[:].bitcast(BF16))
+        idle = bank(BANKS - 1)
+        for k in range(WARM_UPS):
+            nc.tensor.matmul_mx(out=idle[:, 0:WIDTH], lhsT=idle_codes[:, 0:P].bitcast(FP8X4), lhsT_scale=idle_sc[:, 0:P], rhs=idle_codes[:].bitcast(FP8X4), rhs_scale=idle_sc[:], start=True, stop=True)
         nc.gpsimd.memset(ident_wide[:], 0.0)
         make_identity(nc, ident, nomemset=True)
         nc.gpsimd.memset(d_rows[:], 0.0)
         nc.gpsimd.dma_start(out=d_rows[0:P:32, :].rearrange("q (b a) -> q b a", a=32), in_=d.rearrange("(b q a) -> q b a", q=4, a=32))
 
-        load_scales(b_sc_raw[0], b_scales, 0, 512)
+        load_scales(b_sc_rows, b_scales, 0, 1024)
         load_codes(b_raw[0], b_words, 0, 512)
         load_scales(a_sc, a_scales, 0, 1024, range(2))
-        load_codes(a_codes[0], a_words, 0, 256)
+        load_codes(a_codes[0], a_words, 0, 512)
         load_scales(a_sc, a_scales, 0, 1024, range(2, 4))
         load_rows("W", 0, 0, 2)
-        load_codes(a_codes[1], a_words, 256, 512)
+        load_codes(a_codes[1], a_words, 512, 1024)
         load_rows("X", 0, 0, 2)
-        load_codes(a_codes[2], a_words, 512, 1024)
-        load_scales(b_sc_raw[1], b_scales, 512, 1024)
         load_codes(b_raw[1], b_words, 512, 1024)
         for c in range(1, CHUNKS):
-            load_rows("W", c, 0, 2)
+            load_rows("W", c, 0, 4 if c == LAST else 2)
             load_rows("X", c, 0, 2)
-        for kind, lo, hi in (("X", 2, 3), ("W", 2, 4), ("X", 3, 4)):
-            for c in range(CHUNKS):
+        for kind, lo, hi, count in (("X", 2, 3, CHUNKS), ("W", 2, 4, LAST), ("X", 3, 4, CHUNKS)):
+            for c in range(count):
                 load_rows(kind, c, lo, hi)
 
         tensor, vector, scalar, stores = [], [], [], []
         holders = {}
         first_pairs = [(kind, 0, c) for c in range(CHUNKS) for kind in "WX"]
-        late_units = [(kind, n, c) for kind, n in (("X", 2), ("W", 2), ("W", 3), ("X", 3)) for c in range(CHUNKS)]
+        turned = [LAST] + list(range(LAST))
+        late_units = [(kind, n, c) for kind, n in (("X", 2), ("W", 2), ("W", 3), ("X", 3)) for c in (turned if kind == "W" else range(CHUNKS))]
 
         def open_woven(kind, n, c):
             if n < 2 and (kind, 0, c, 2) not in woven:
@@ -322,11 +330,11 @@ def tile_concord_precision_gradient_s12_kernel(tc, a_words, a_scales, b_words, b
             k, waits = take_bank(("out", "O", h, b))
             return ([("made", "O", h, b)], [("sorted", h)] + waits, lambda: omega(h, b, k))
 
-        def cov_step(it, c):
-            k, waits = take_bank(("out", "C", it)) if c == 0 else (None, [])
+        def cov_step(it, c, n):
+            k, waits = take_bank(("out", "C", it)) if n == 0 else (None, [])
             slots, lo, width = shape_of(it)
             waits += [("quantised", "W", 2 * it[0] + u // 2, c) for u in slots] + [("quantised", "X", lo // WIDTH, c)]
-            return ([("made", "C", it, c)], waits, lambda: cov(it, c, k))
+            return ([("made", "C", it, n)], waits, lambda: cov(it, c, n, k))
 
         def piece_step(piece):
             k, free = take_bank(("out",) + piece)
@@ -343,7 +351,8 @@ def tile_concord_precision_gradient_s12_kernel(tc, a_words, a_scales, b_words, b
         regions = [[(0, "four", b) for b in range(4)], [(0, "four", b) for b in (4, 5)], [(1, 0, s) for s in range(3)], [(1, 1, s) for s in range(3)]]
         regions.append([(h, z, 3) for h in range(HALVES) for z in range(2)])
         for region in regions:
-            tensor.extend(cov_step(it, c) for c in range(CHUNKS) for it in region)
+            order = turned if region[0][0] == 1 else range(CHUNKS)
+            tensor.extend(cov_step(it, c, n) for n, c in enumerate(order) for it in region)
         pieces = [("square", 1, 0), ("wide", 4), ("wide", 5), ("wide", 6), ("mirror", 0, 1), ("mirror", 0, 2), ("mirror", 1, 2)]
         pieces += [("wide", 7), ("row", 6, 2), ("row", 7, 2), ("square", 0, 0)] + [("mirror", r, 3) for r in range(3)]
         pieces += [("square", 1, 1), ("square", 2, 2), ("row", 6, 3), ("row", 7, 3)]
@@ -356,7 +365,7 @@ def tile_concord_precision_gradient_s12_kernel(tc, a_words, a_scales, b_words, b
 
         cov_banks = [it for region in regions for it in region]
         theirs = []
-        for what, it in [("O", (0, 8)), ("w", ("X", 1, 1)), ("O", (8, 12)), ("w", ("X", 1, 2)), ("w", ("W", 1, 3)), ("w", ("X", 1, 3)), ("O", (12, 14)), ("w", ("X", 2, 3)), ("O", (14, 16)), ("C", (0, 1)), ("w", ("W", 2, 2)), ("C", (1, 4)), ("w", ("W", 3, 1)), ("C", (4, 6)), ("w", ("W", 3, 3)), ("C", (6, 8)), ("w", ("X", 3, 2)), ("C", (8, 12))]:
+        for what, it in [("O", (0, 8)), ("w", ("X", 1, 1)), ("O", (8, 12)), ("w", ("X", 1, 2)), ("O", (12, 13)), ("w", ("W", 1, 3)), ("w", ("X", 1, 3)), ("O", (13, 14)), ("w", ("X", 2, 1)), ("w", ("W", 2, 3)), ("O", (14, 16)), ("C", (0, 1)), ("w", ("W", 3, 3)), ("C", (1, 6)), ("w", ("X", 3, 1)), ("C", (6, 8)), ("w", ("X", 3, 3)), ("C", (8, 12))]:
             if what == "O":
                 scalar.extend(omega_out_step(n) for n in range(*it))
             elif what == "C":
@@ -364,32 +373,24 @@ def tile_concord_precision_gradient_s12_kernel(tc, a_words, a_scales, b_words, b
             else:
                 theirs.append(it)
                 scalar.append(weave_step(*it, 1, "S"))
-        scalar.extend(cov_out_step(it, "S") for it in regions[-1][0::2])
+        scalar.extend(cov_out_step(it, "S") for it in regions[-1][:3])
         on_vector = [piece for piece in pieces if on_diagonal(piece) or piece in (("wide", 6), ("wide", 7), ("mirror", 0, 2), ("mirror", 1, 3))]
         scalar.extend(piece_out_step(piece, "S") for piece in pieces if piece not in on_vector)
 
         vector.extend(free_step(lambda q=q: sort_b(b_sc[0], b_sc_raw[0], RUN // 4, slice(32 * q, 32 * q + 4))) for q in range(4))
         vector.append(([("sorted", 0)], [], lambda: sort_b(b_codes[0], b_raw[0], RUN // 2)))
-        behind = []
-        for kind, n, c in first_pairs:
-            vector.append(weave_step(kind, 0, c, 1 if (kind, 1, c) in theirs else 2, "V"))
-            vector.extend(behind)
-            behind = [quantise_step(kind, 0, c, 2)]
-            if (kind, c) == ("X", 0):
-                vector.extend(behind)
-                behind = []
-                vector.append(free_step(lambda: sort_b(b_sc[1], b_sc_raw[1], RUN // 4)))
+        vector.extend(free_step(lambda q=q: sort_b(b_sc[1], b_sc_raw[1], RUN // 4, slice(32 * q, 32 * q + 4))) for q in range(4))
+        for what, kind, n, c, count in [("w", "W", 0, 0, 2), ("q", "W", 0, 0, 2), ("w", "X", 0, 0, 2), ("s", "B", 1, 0, 0), ("q", "X", 0, 0, 2), ("w", "W", 0, 1, 2), ("w", "X", 0, 1, 1), ("q", "W", 0, 1, 2), ("w", "W", 0, 2, 2), ("q", "X", 0, 1, 2), ("w", "X", 0, 2, 1), ("q", "W", 0, 2, 2), ("w", "W", 0, 3, 1), ("q", "X", 0, 2, 2), ("w", "X", 0, 3, 1), ("q", "W", 0, 3, 2), ("q", "X", 0, 3, 2), ("w", "X", 2, 0, 1), ("w", "X", 2, 2, 1), ("q", "X", 2, 0, 1), ("q", "X", 2, 1, 1), ("w", "X", 2, 3, 1), ("q", "X", 2, 2, 1), ("w", "W", 2, 0, 1), ("q", "X", 2, 3, 1), ("q", "W", 2, 3, 1), ("w", "W", 2, 1, 1), ("q", "W", 2, 0, 1), ("w", "W", 2, 2, 1), ("q", "W", 2, 1, 1), ("w", "W", 3, 0, 1), ("q", "W", 2, 2, 1), ("q", "W", 3, 3, 1), ("w", "W", 3, 1, 1), ("q", "W", 3, 0, 1), ("w", "W", 3, 2, 1), ("q", "W", 3, 1, 1), ("w", "X", 3, 0, 1), ("q", "W", 3, 2, 1), ("q", "X", 3, 0, 1), ("w", "X", 3, 2, 1), ("q", "X", 3, 1, 1), ("q", "X", 3, 2, 1)]:
+            if what == "w":
+                vector.append(weave_step(kind, n, c, count, "V"))
+            elif what == "q":
+                vector.append(quantise_step(kind, n, c, count))
+            else:
                 vector.append(([("sorted", 1)], [], lambda: sort_b(b_codes[1], b_raw[1], RUN // 2)))
-        vector += [quantise_step("X", e, LAST, 1) for e in range(2)]
-        behind = []
-        for it in late_units:
-            if it not in theirs:
-                vector.append(weave_step(*it, 1, "V"))
-            vector.extend(behind)
-            behind = [quantise_step(*it, 1)]
+        behind = [quantise_step("X", 3, 3, 1)]
         vector += [result_step("O", 0, 0, 2)] + behind + [result_step("O", 1, 0, 2)] + [result_step("C", h, 0, 2) for h in range(HALVES)]
         vector += [result_step("O", h, 2, 4) for h in range(HALVES)] + [result_step("C", h, 2, 3) for h in range(HALVES)]
-        vector += [cov_out_step(it, "V") for it in regions[-1][1::2]] + [result_step("C", h, 3, 4) for h in range(HALVES)]
+        vector += [cov_out_step(it, "V") for it in regions[-1][3:]] + [result_step("C", h, 3, 4) for h in range(HALVES)]
         vector.append(free_step(lambda: nc.vector.transpose(out=d_turned[:], in_=d_rows[:])))
         vector.append(piece_out_step(on_vector[0], "V"))
         vector.append(free_step(lambda: nc.vector.reciprocal(out=d_rec[:], in_=d_turned[:, 0:256:32])))

@@ -117,26 +117,25 @@ def tile_concord_precision_gradient_s12_kernel(tc, a_words, a_scales, b_words, b
         def slots_out(eng, dst, src, count):
             copy(eng, dst.rearrange("p (n e) u -> p n u e", e=2), src[:].rearrange("p (u n e) -> p n u e", u=count, e=2))
 
-        def omega(h, b, k):
+        def omega(it, k):
             t = bank(k)
-            ps["O", h, b] = t
-            q = b // 4
-            lo = b * P - a_ranges[q][0]
-            for u in range(SLOTS):
+            ps["O", it] = t
+            slots, lo, width = shape_of(it)
+            for e, u in enumerate(slots):
                 for g in range(2):
                     nc.tensor.matmul_mx(
-                        out=t[:, u * P : (u + 1) * P],
-                        lhsT=b_codes[h][:, g, u * 256 : (u + 1) * 256].bitcast(FP4X4),
-                        lhsT_scale=b_sc[h][:, g, u * P : (u + 1) * P],
-                        rhs=a_codes[q][:, g, 2 * lo : 2 * (lo + P)].bitcast(FP4X4),
-                        rhs_scale=a_sc[:, g, b * P : (b + 1) * P],
+                        out=t[:, e * width : (e + 1) * width],
+                        lhsT=b_codes[it[0]][:, g, u * 256 : (u + 1) * 256].bitcast(FP4X4),
+                        lhsT_scale=b_sc[it[0]][:, g, u * P : (u + 1) * P],
+                        rhs=a_codes[lo // 512][:, g, 2 * (lo % 512) : 2 * (lo % 512 + width)].bitcast(FP4X4),
+                        rhs_scale=a_sc[:, g, lo : lo + width],
                         start=(g == 0),
                         stop=(g == 1),
                     )
 
-        def omega_out(h, b):
-            lo = (b % 4) * P
-            slots_out("S", o_words[h, b // 4][:, lo : lo + P, :], ps["O", h, b], SLOTS)
+        def omega_out(it):
+            slots, lo, width = shape_of(it)
+            slots_out("S", o_words[it[0], lo // 512][:, lo % 512 : lo % 512 + width, slots[0] : slots[-1] + 1], ps["O", it], len(slots))
 
         def shape_of(it):
             h, z, n = it
@@ -306,7 +305,7 @@ def tile_concord_precision_gradient_s12_kernel(tc, a_words, a_scales, b_words, b
 
         def result_step(kind, h, lo, hi):
             if kind == "O":
-                waits = [("out", "O", h, b) for b in range(2 * lo, 2 * hi)]
+                waits = [("out", "O", it) for it in omega_banks if it[0] == h and lo <= shape_of(it)[1] // WIDTH < hi]
             else:
                 waits = [("out", "C", it) for region in regions for it in region if it[0] == h and lo <= shape_of(it)[1] // WIDTH < hi]
             return ([("quantised", kind, h, s) for s in range(lo, hi)], waits, lambda: quantise_result(kind, h, lo, hi))
@@ -326,9 +325,9 @@ def tile_concord_precision_gradient_s12_kernel(tc, a_words, a_scales, b_words, b
             holders[len(holders)] = emptied_by
             return k, waits
 
-        def omega_step(h, b):
-            k, waits = take_bank(("out", "O", h, b))
-            return ([("made", "O", h, b)], [("sorted", h)] + waits, lambda: omega(h, b, k))
+        def omega_step(it):
+            k, waits = take_bank(("out", "O", it))
+            return ([("made", "O", it)], [("sorted", it[0])] + waits, lambda: omega(it, k))
 
         def cov_step(it, c, n):
             k, waits = take_bank(("out", "C", it)) if n == 0 else (None, [])
@@ -347,8 +346,9 @@ def tile_concord_precision_gradient_s12_kernel(tc, a_words, a_scales, b_words, b
                 waits = [("out", "wide", 2 * piece[2] + e) if piece[1] < 2 else ("out", "row", 6 + e, 2) for e in range(2)]
             return ([("made",) + piece], waits + free, lambda: make_piece(piece, k))
 
-        tensor.extend(omega_step(h, b) for h in range(HALVES) for b in range(BANKS))
-        regions = [[(0, "four", b) for b in range(4)], [(0, "four", b) for b in (4, 5)], [(1, 0, s) for s in range(3)], [(1, 1, s) for s in range(3)]]
+        omega_banks = [(h, "four", b) for h in range(HALVES) for b in range(BANKS)]
+        tensor.extend(omega_step(it) for it in omega_banks)
+        regions = [[(0, "four", b) for b in range(4)], [(0, z, 2) for z in range(2)], [(1, 0, s) for s in range(3)], [(1, 1, s) for s in range(3)]]
         regions.append([(h, z, 3) for h in range(HALVES) for z in range(2)])
         for region in regions:
             order = turned if region[0][0] == 1 else range(CHUNKS)
@@ -360,12 +360,12 @@ def tile_concord_precision_gradient_s12_kernel(tc, a_words, a_scales, b_words, b
         stores.extend(([], [("out",) + piece], lambda piece=piece: store_piece(piece)) for piece in pieces)
 
         def omega_out_step(n):
-            h, b = divmod(n, BANKS)
-            return ([("out", "O", h, b)], [("made", "O", h, b)], lambda: omega_out(h, b))
+            it = omega_banks[n]
+            return ([("out", "O", it)], [("made", "O", it)], lambda: omega_out(it))
 
         cov_banks = [it for region in regions for it in region]
         theirs = []
-        for what, it in [("O", (0, 8)), ("w", ("X", 1, 1)), ("O", (8, 12)), ("w", ("X", 1, 2)), ("O", (12, 13)), ("w", ("W", 1, 3)), ("w", ("X", 1, 3)), ("O", (13, 14)), ("w", ("X", 2, 1)), ("w", ("W", 2, 3)), ("O", (14, 16)), ("C", (0, 1)), ("w", ("W", 3, 3)), ("C", (1, 6)), ("w", ("X", 3, 1)), ("C", (6, 8)), ("w", ("X", 3, 3)), ("C", (8, 12))]:
+        for what, it in [("O", (0, 8)), ("w", ("X", 1, 1)), ("O", (8, 12)), ("w", ("X", 1, 2)), ("O", (12, 13)), ("w", ("W", 1, 3)), ("w", ("X", 1, 3)), ("O", (13, 14)), ("w", ("X", 2, 1)), ("w", ("X", 2, 2)), ("O", (14, 16)), ("C", (0, 1)), ("w", ("W", 2, 1)), ("C", (1, 4)), ("w", ("W", 3, 1)), ("C", (4, 8)), ("w", ("X", 3, 3)), ("C", (8, 12))]:
             if what == "O":
                 scalar.extend(omega_out_step(n) for n in range(*it))
             elif what == "C":
@@ -380,7 +380,7 @@ def tile_concord_precision_gradient_s12_kernel(tc, a_words, a_scales, b_words, b
         vector.extend(free_step(lambda q=q: sort_b(b_sc[0], b_sc_raw[0], RUN // 4, slice(32 * q, 32 * q + 4))) for q in range(4))
         vector.append(([("sorted", 0)], [], lambda: sort_b(b_codes[0], b_raw[0], RUN // 2)))
         vector.extend(free_step(lambda q=q: sort_b(b_sc[1], b_sc_raw[1], RUN // 4, slice(32 * q, 32 * q + 4))) for q in range(4))
-        for what, kind, n, c, count in [("w", "W", 0, 0, 2), ("q", "W", 0, 0, 2), ("w", "X", 0, 0, 2), ("s", "B", 1, 0, 0), ("q", "X", 0, 0, 2), ("w", "W", 0, 1, 2), ("w", "X", 0, 1, 1), ("q", "W", 0, 1, 2), ("w", "W", 0, 2, 2), ("q", "X", 0, 1, 2), ("w", "X", 0, 2, 1), ("q", "W", 0, 2, 2), ("w", "W", 0, 3, 1), ("q", "X", 0, 2, 2), ("w", "X", 0, 3, 1), ("q", "W", 0, 3, 2), ("q", "X", 0, 3, 2), ("w", "X", 2, 0, 1), ("w", "X", 2, 2, 1), ("q", "X", 2, 0, 1), ("q", "X", 2, 1, 1), ("w", "X", 2, 3, 1), ("q", "X", 2, 2, 1), ("w", "W", 2, 0, 1), ("q", "X", 2, 3, 1), ("q", "W", 2, 3, 1), ("w", "W", 2, 1, 1), ("q", "W", 2, 0, 1), ("w", "W", 2, 2, 1), ("q", "W", 2, 1, 1), ("w", "W", 3, 0, 1), ("q", "W", 2, 2, 1), ("q", "W", 3, 3, 1), ("w", "W", 3, 1, 1), ("q", "W", 3, 0, 1), ("w", "W", 3, 2, 1), ("q", "W", 3, 1, 1), ("w", "X", 3, 0, 1), ("q", "W", 3, 2, 1), ("q", "X", 3, 0, 1), ("w", "X", 3, 2, 1), ("q", "X", 3, 1, 1), ("q", "X", 3, 2, 1)]:
+        for what, kind, n, c, count in [("w", "W", 0, 0, 2), ("q", "W", 0, 0, 2), ("w", "X", 0, 0, 2), ("s", "B", 1, 0, 0), ("q", "X", 0, 0, 2), ("w", "W", 0, 1, 2), ("w", "X", 0, 1, 1), ("q", "W", 0, 1, 2), ("w", "W", 0, 2, 2), ("q", "X", 0, 1, 2), ("w", "X", 0, 2, 1), ("q", "W", 0, 2, 2), ("w", "W", 0, 3, 1), ("q", "X", 0, 2, 2), ("w", "X", 0, 3, 1), ("q", "W", 0, 3, 2), ("q", "X", 0, 3, 2), ("w", "X", 2, 0, 1), ("w", "W", 2, 3, 1), ("q", "X", 2, 0, 1), ("q", "X", 2, 1, 1), ("w", "X", 2, 3, 1), ("q", "X", 2, 2, 1), ("q", "W", 2, 3, 1), ("q", "X", 2, 3, 1), ("w", "W", 2, 0, 1), ("w", "W", 3, 3, 1), ("q", "W", 2, 0, 1), ("q", "W", 2, 1, 1), ("w", "W", 2, 2, 1), ("q", "W", 3, 3, 1), ("q", "W", 2, 2, 1), ("w", "W", 3, 0, 1), ("w", "W", 3, 2, 1), ("q", "W", 3, 0, 1), ("q", "W", 3, 1, 1), ("w", "X", 3, 0, 1), ("q", "W", 3, 2, 1), ("w", "X", 3, 1, 1), ("q", "X", 3, 0, 1), ("w", "X", 3, 2, 1), ("q", "X", 3, 1, 1), ("q", "X", 3, 2, 1)]:
             if what == "w":
                 vector.append(weave_step(kind, n, c, count, "V"))
             elif what == "q":

@@ -23,7 +23,7 @@ BLOCKS = 4
 WIDTH = 256
 RUN = 8
 BANKS = 8
-WARM_UPS = 8
+WARM_UPS = 5
 WOVEN_PAIRS = 4
 WOVEN_UNITS = 10
 
@@ -248,12 +248,13 @@ def tile_concord_precision_gradient_s12_kernel(tc, a_words, a_scales, b_words, b
 
         for t in (a_sc, b_sc_all):
             nc.vector.memset(t[:].bitcast(I32), 0)
-        idle_codes = sbuf("idle_codes", [P, WIDTH], U32)
-        idle_sc = sbuf("idle_sc", [P, WIDTH], U8)
-        nc.vector.quantize_mx(out=idle_codes[:].bitcast(FP8X4), scales=idle_sc[:], in_=b_sc_all[:].bitcast(BF16))
+        idle_codes = sbuf("idle_codes", [P, 512], U32)
+        idle_sc = sbuf("idle_sc", [P, 512], U8)
+        for lo in (0, WIDTH):
+            nc.vector.quantize_mx(out=idle_codes[:, lo : lo + WIDTH].bitcast(FP8X4), scales=idle_sc[:, lo : lo + WIDTH], in_=b_sc_all[:].bitcast(BF16))
         idle = bank(BANKS - 1)
         for k in range(WARM_UPS):
-            nc.tensor.matmul_mx(out=idle[:, 0:WIDTH], lhsT=idle_codes[:, 0:P].bitcast(FP8X4), lhsT_scale=idle_sc[:, 0:P], rhs=idle_codes[:].bitcast(FP8X4), rhs_scale=idle_sc[:], start=True, stop=True)
+            nc.tensor.matmul_mx(out=idle[:], lhsT=idle_codes[:, 0:P].bitcast(FP8X4), lhsT_scale=idle_sc[:, 0:P], rhs=idle_codes[:].bitcast(FP8X4), rhs_scale=idle_sc[:], start=True, stop=True)
         nc.gpsimd.memset(ident_wide[:], 0.0)
         make_identity(nc, ident, nomemset=True)
         nc.gpsimd.memset(d_rows[:], 0.0)

@@ -26,6 +26,7 @@ BANKS = 8
 WARM_UPS = 5
 WOVEN_PAIRS = 4
 WOVEN_UNITS = 10
+PAIRED_BANKS = 2
 
 
 def tile_concord_precision_gradient_s12_kernel(tc, a_words, a_scales, b_words, b_scales, xw, x, d, out):
@@ -49,8 +50,7 @@ def tile_concord_precision_gradient_s12_kernel(tc, a_words, a_scales, b_words, b
             else:
                 nc.vector.tensor_copy(out=dst, in_=src)
 
-        a_ranges = [(0, 512), (512, 1024)]
-        a_codes = [sbuf("a_codes%d" % lo, [P, 2, 2 * (hi - lo)], U8) for lo, hi in a_ranges]
+        a_codes = [sbuf("a_codes%d" % q, [P, 2, 1024], U8) for q in range(2)]
         a_sc = sbuf("a_sc", [P, 2, 1024], U8)
         b_raw = [sbuf("b_raw%d" % h, [P, 2, 1024], U8) for h in range(HALVES)]
         b_codes = [sbuf("b_codes%d" % h, [P, 2, 1024], U8) for h in range(HALVES)]
@@ -75,25 +75,23 @@ def tile_concord_precision_gradient_s12_kernel(tc, a_words, a_scales, b_words, b
         d_neg = sbuf("d_neg", [P, 8], F32)
         raw, woven, ps, g_sb, spent = {}, {}, {}, {}, []
 
-        def load_codes(dst, src, lo, hi):
-            nc.sync.dma_start(out=dst[:].bitcast(I32), in_=src[:, :, 2 * lo : 2 * hi].bitcast(I32).rearrange("g p n -> p g n"))
+        def load_codes(dst, src, half):
+            nc.sync.dma_start(out=dst[:].bitcast(I32), in_=src[:, :, half * 1024 : (half + 1) * 1024].bitcast(I32).rearrange("g p n -> p g n"))
 
-        def load_scales(dst, src, lo, hi, rows=range(4)):
+        def load_scales(dst, src, rows):
             for r in rows:
-                nc.sync.dma_start(out=dst[r:P:32, :, :].bitcast(I32), in_=src[:, r:16:4, lo:hi].bitcast(I32).rearrange("g q n -> q g n"))
+                nc.sync.dma_start(out=dst[r:P:32, :, :].bitcast(I32), in_=src[:, r:16:4, :].bitcast(I32).rearrange("g q n -> q g n"))
 
         def load_rows(kind, c, lo, hi):
             name = "raw%s%d%d" % (kind, lo, c)
             spent.append(name)
             t = sbuf(name, [P, SLOTS, (hi - lo) * WIDTH], BF16)
             for n in range(lo, hi):
-                raw[kind, n, c] = t[:, :, (n - lo) // 2 * 512 : (n - lo) // 2 * 512 + 512] if kind == "W" else t[:, :, (n - lo) * WIDTH : (n - lo + 1) * WIDTH]
-            if hi - lo == 2:
-                raw[kind, lo, c, "pair"] = t[:]
+                raw[kind, n, c] = t[:, :, (n - lo - n % 2 * (kind == "W")) * WIDTH :]
             src = (xw if kind == "W" else x)[c * 512 : (c + 1) * 512, lo * WIDTH : hi * WIDTH]
             nc.sync.dma_start(out=t[:], in_=src.rearrange("(p t) w -> p t w", t=SLOTS))
 
-        def sort_b(dst, src, words, rows=slice(0, P)):
+        def sort_b(dst, src, words, rows):
             nc.vector.tensor_copy(
                 out=dst[rows].bitcast(I32).rearrange("p g (u q w) -> p g u q w", u=SLOTS, w=words),
                 in_=src[rows].bitcast(I32).rearrange("p g (q u w) -> p g u q w", u=SLOTS, w=words),
@@ -104,10 +102,10 @@ def tile_concord_precision_gradient_s12_kernel(tc, a_words, a_scales, b_words, b
             if kind == "W":
                 lo = 2 * (n % 2)
                 dst = dst.rearrange("p (u q w t) -> p q u t w", u=2 * count, w=RUN, t=SLOTS)
-                src = raw[kind, n, c].rearrange("p t (q u w) -> p q u t w", u=SLOTS, w=RUN)[:, :, lo : lo + 2 * count]
+                src = raw[kind, n, c][:, :, 0:512].rearrange("p t (q u w) -> p q u t w", u=SLOTS, w=RUN)[:, :, lo : lo + 2 * count]
             else:
                 dst = dst.rearrange("p (a w t) -> p a t w", w=RUN, t=SLOTS)
-                src = (raw[kind, n, c, "pair"] if count == 2 else raw[kind, n, c]).rearrange("p t (a w) -> p a t w", w=RUN)
+                src = raw[kind, n, c][:, :, 0 : count * WIDTH].rearrange("p t (a w) -> p a t w", w=RUN)
             copy(eng, dst, src)
 
         def quantise(kind, n, c, count):
@@ -116,6 +114,10 @@ def tile_concord_precision_gradient_s12_kernel(tc, a_words, a_scales, b_words, b
 
         def slots_out(eng, dst, src, count):
             copy(eng, dst.rearrange("p (n e) u -> p n u e", e=2), src[:].rearrange("p (u n e) -> p n u e", u=count, e=2))
+
+        def shape_of(it):
+            h, z, n = it
+            return (range(SLOTS), n * P, P) if z == "four" else (range(2 * z, 2 * z + 2), n * WIDTH, WIDTH)
 
         def omega(it, k):
             t = bank(k)
@@ -133,14 +135,6 @@ def tile_concord_precision_gradient_s12_kernel(tc, a_words, a_scales, b_words, b
                         stop=(g == 1),
                     )
 
-        def omega_out(it):
-            slots, lo, width = shape_of(it)
-            slots_out("S", o_words[it[0], lo // 512][:, lo % 512 : lo % 512 + width, slots[0] : slots[-1] + 1], ps["O", it], len(slots))
-
-        def shape_of(it):
-            h, z, n = it
-            return (range(SLOTS), n * P, P) if z == "four" else (range(2 * z, 2 * z + 2), n * WIDTH, WIDTH)
-
         def cov(it, c, n, k):
             if n == 0:
                 ps["C", it] = bank(k)
@@ -157,9 +151,10 @@ def tile_concord_precision_gradient_s12_kernel(tc, a_words, a_scales, b_words, b
                     stop=(n == LAST and e == len(slots) - 1),
                 )
 
-        def cov_out(it, eng):
+        def bank_out(kind, it, eng):
             slots, lo, width = shape_of(it)
-            slots_out(eng, c_words[it[0], lo // 512][:, lo % 512 : lo % 512 + width, slots[0] : slots[-1] + 1], ps["C", it], len(slots))
+            words = (o_words if kind == "O" else c_words)[it[0], lo // 512]
+            slots_out(eng, words[:, lo % 512 : lo % 512 + width, slots[0] : slots[-1] + 1], ps[kind, it], len(slots))
 
         def quantise_result(kind, h, lo, hi):
             dst, sc, src = (o_codes, o_sc, o_words) if kind == "O" else (c_codes, c_sc, c_words)
@@ -245,7 +240,6 @@ def tile_concord_precision_gradient_s12_kernel(tc, a_words, a_scales, b_words, b
             elif piece[1] % 2:
                 store_square(g_sb["square", piece[1] // 2, piece[2]], piece[1] // 2, piece[2])
 
-
         for t in (a_sc, b_sc_all):
             nc.vector.memset(t[:].bitcast(I32), 0)
         idle_codes = sbuf("idle_codes", [P, 512], U32)
@@ -260,15 +254,15 @@ def tile_concord_precision_gradient_s12_kernel(tc, a_words, a_scales, b_words, b
         nc.gpsimd.memset(d_rows[:], 0.0)
         nc.gpsimd.dma_start(out=d_rows[0:P:32, :].rearrange("q (b a) -> q b a", a=32), in_=d.rearrange("(b q a) -> q b a", q=4, a=32))
 
-        load_scales(b_sc_rows, b_scales, 0, 1024)
-        load_codes(b_raw[0], b_words, 0, 512)
-        load_scales(a_sc, a_scales, 0, 1024, range(2))
-        load_codes(a_codes[0], a_words, 0, 512)
-        load_scales(a_sc, a_scales, 0, 1024, range(2, 4))
+        load_scales(b_sc_rows, b_scales, range(4))
+        load_codes(b_raw[0], b_words, 0)
+        load_scales(a_sc, a_scales, range(2))
+        load_codes(a_codes[0], a_words, 0)
+        load_scales(a_sc, a_scales, range(2, 4))
         load_rows("W", 0, 0, 2)
-        load_codes(a_codes[1], a_words, 512, 1024)
+        load_codes(a_codes[1], a_words, 1)
         load_rows("X", 0, 0, 2)
-        load_codes(b_raw[1], b_words, 512, 1024)
+        load_codes(b_raw[1], b_words, 1)
         for c in range(1, CHUNKS):
             load_rows("W", c, 0, 4 if c == LAST else 2)
             load_rows("X", c, 0, 2)
@@ -280,7 +274,8 @@ def tile_concord_precision_gradient_s12_kernel(tc, a_words, a_scales, b_words, b
         holders = {}
         first_pairs = [(kind, 0, c) for c in range(CHUNKS) for kind in "WX"]
         turned = [LAST] + list(range(LAST))
-        late_units = [(kind, n, c) for kind, n in (("X", 2), ("W", 2), ("W", 3), ("X", 3)) for c in (turned if kind == "W" else range(CHUNKS))]
+        new_units = [[(kind, n, c) for c in (turned if kind == "W" else range(CHUNKS))] for kind, n in (("X", 2), ("W", 2), ("W", 3), ("X", 3))]
+        late_units = [it for units in new_units for it in units]
 
         def open_woven(kind, n, c):
             if n < 2 and (kind, 0, c, 2) not in woven:
@@ -305,14 +300,11 @@ def tile_concord_precision_gradient_s12_kernel(tc, a_words, a_scales, b_words, b
             return ([("quantised", kind, n + e, c) for e in range(count)], [("woven", kind, n + e, c) for e in range(count)], lambda: quantise(kind, n, c, count))
 
         def result_step(kind, h, lo, hi):
-            if kind == "O":
-                waits = [("out", "O", it) for it in omega_banks if it[0] == h and lo <= shape_of(it)[1] // WIDTH < hi]
-            else:
-                waits = [("out", "C", it) for region in regions for it in region if it[0] == h and lo <= shape_of(it)[1] // WIDTH < hi]
+            waits = [("out", kind, it) for other, it in banks if other == kind and it[0] == h and lo <= shape_of(it)[1] // WIDTH < hi]
             return ([("quantised", kind, h, s) for s in range(lo, hi)], waits, lambda: quantise_result(kind, h, lo, hi))
 
-        def cov_out_step(it, eng):
-            return ([("out", "C", it)], [("made", "C", it, LAST)], lambda: cov_out(it, eng))
+        def bank_out_step(kind, it, eng):
+            return ([("out", kind, it)], [("made", kind, it)], lambda: bank_out(kind, it, eng))
 
         def piece_out_step(piece, eng):
             return ([("out",) + piece], [("made",) + piece], lambda: piece_out(piece, eng))
@@ -334,7 +326,7 @@ def tile_concord_precision_gradient_s12_kernel(tc, a_words, a_scales, b_words, b
             k, waits = take_bank(("out", "C", it)) if n == 0 else (None, [])
             slots, lo, width = shape_of(it)
             waits += [("quantised", "W", 2 * it[0] + u // 2, c) for u in slots] + [("quantised", "X", lo // WIDTH, c)]
-            return ([("made", "C", it, n)], waits, lambda: cov(it, c, n, k))
+            return ([("made", "C", it)] if n == LAST else [], waits, lambda: cov(it, c, n, k))
 
         def piece_step(piece):
             k, free = take_bank(("out",) + piece)
@@ -347,51 +339,66 @@ def tile_concord_precision_gradient_s12_kernel(tc, a_words, a_scales, b_words, b
                 waits = [("out", "wide", 2 * piece[2] + e) if piece[1] < 2 else ("out", "row", 6 + e, 2) for e in range(2)]
             return ([("made",) + piece], waits + free, lambda: make_piece(piece, k))
 
-        omega_banks = [(h, "four", b) for h in range(HALVES) for b in range(BANKS)]
+        omega_banks = [(0, k % 2, k // 2) for k in range(PAIRED_BANKS)] + [(h, "four", b) for h in range(HALVES) for b in range(BANKS)][PAIRED_BANKS:]
         tensor.extend(omega_step(it) for it in omega_banks)
         regions = [[(0, "four", b) for b in range(4)], [(0, z, 2) for z in range(2)], [(1, 0, s) for s in range(3)], [(1, 1, s) for s in range(3)]]
         regions.append([(h, z, 3) for h in range(HALVES) for z in range(2)])
         for region in regions:
             order = turned if region[0][0] == 1 else range(CHUNKS)
             tensor.extend(cov_step(it, c, n) for n, c in enumerate(order) for it in region)
+        banks = [("O", it) for it in omega_banks] + [("C", it) for region in regions for it in region]
         pieces = [("square", 1, 0), ("wide", 4), ("wide", 5), ("wide", 6), ("mirror", 0, 1), ("mirror", 0, 2), ("mirror", 1, 2)]
         pieces += [("wide", 7), ("row", 6, 2), ("row", 7, 2), ("square", 0, 0)] + [("mirror", r, 3) for r in range(3)]
         pieces += [("square", 1, 1), ("square", 2, 2), ("row", 6, 3), ("row", 7, 3)]
         tensor.extend(piece_step(piece) for piece in pieces)
         stores.extend(([], [("out",) + piece], lambda piece=piece: store_piece(piece)) for piece in pieces)
 
-        def omega_out_step(n):
-            it = omega_banks[n]
-            return ([("out", "O", it)], [("made", "O", it)], lambda: omega_out(it))
-
-        cov_banks = [it for region in regions for it in region]
-        theirs = []
-        for what, it in [("O", (0, 8)), ("w", ("X", 1, 1)), ("O", (8, 12)), ("w", ("X", 1, 2)), ("O", (12, 13)), ("w", ("W", 1, 3)), ("w", ("X", 1, 3)), ("O", (13, 14)), ("w", ("X", 2, 1)), ("w", ("X", 2, 2)), ("O", (14, 16)), ("C", (0, 1)), ("w", ("W", 2, 1)), ("C", (1, 4)), ("w", ("W", 3, 1)), ("C", (4, 8)), ("w", ("X", 3, 3)), ("C", (8, 12))]:
-            if what == "O":
-                scalar.extend(omega_out_step(n) for n in range(*it))
-            elif what == "C":
-                scalar.extend(cov_out_step(b, "S") for b in cov_banks[it[0] : it[1]])
-            else:
-                theirs.append(it)
-                scalar.append(weave_step(*it, 1, "S"))
-        scalar.extend(cov_out_step(it, "S") for it in regions[-1][:3])
+        outs = [bank_out_step(kind, it, "S") for kind, it in banks[:-1]]
+        starts = [BANKS]
+        for region in regions:
+            starts.append(starts[-1] + len(region))
+        starts.append(len(outs))
+        frees = [outs[starts[r] : starts[r + 1]] for r in range(len(regions) + 1)]
+        shares = [new_units[0][1:3]] + [units[2:3] for units in new_units[1:]]
+        scalar += outs[:BANKS] + [weave_step("X", 1, 1, 1, "S")] + frees[0] + [weave_step("X", 1, 2, 1, "S")] + frees[1][:1]
+        scalar += [weave_step(kind, 1, LAST, 1, "S") for kind in "WX"] + frees[1][1:]
+        for share, steps in zip(shares, frees[2:]):
+            scalar += [weave_step(*it, 1, "S") for it in share] + steps
         on_vector = [piece for piece in pieces if on_diagonal(piece) or piece in (("wide", 6), ("wide", 7), ("mirror", 0, 2), ("mirror", 1, 3))]
         scalar.extend(piece_out_step(piece, "S") for piece in pieces if piece not in on_vector)
 
-        vector.extend(free_step(lambda q=q: sort_b(b_sc[0], b_sc_raw[0], RUN // 4, slice(32 * q, 32 * q + 4))) for q in range(4))
-        vector.append(([("sorted", 0)], [], lambda: sort_b(b_codes[0], b_raw[0], RUN // 2)))
-        vector.extend(free_step(lambda q=q: sort_b(b_sc[1], b_sc_raw[1], RUN // 4, slice(32 * q, 32 * q + 4))) for q in range(4))
-        for what, kind, n, c, count in [("w", "W", 0, 0, 2), ("q", "W", 0, 0, 2), ("w", "X", 0, 0, 2), ("s", "B", 1, 0, 0), ("q", "X", 0, 0, 2), ("w", "W", 0, 1, 2), ("w", "X", 0, 1, 1), ("q", "W", 0, 1, 2), ("w", "W", 0, 2, 2), ("q", "X", 0, 1, 2), ("w", "X", 0, 2, 1), ("q", "W", 0, 2, 2), ("w", "W", 0, 3, 1), ("q", "X", 0, 2, 2), ("w", "X", 0, 3, 1), ("q", "W", 0, 3, 2), ("q", "X", 0, 3, 2), ("w", "X", 2, 0, 1), ("w", "W", 2, 3, 1), ("q", "X", 2, 0, 1), ("q", "X", 2, 1, 1), ("w", "X", 2, 3, 1), ("q", "X", 2, 2, 1), ("q", "W", 2, 3, 1), ("q", "X", 2, 3, 1), ("w", "W", 2, 0, 1), ("w", "W", 3, 3, 1), ("q", "W", 2, 0, 1), ("q", "W", 2, 1, 1), ("w", "W", 2, 2, 1), ("q", "W", 3, 3, 1), ("q", "W", 2, 2, 1), ("w", "W", 3, 0, 1), ("w", "W", 3, 2, 1), ("q", "W", 3, 0, 1), ("q", "W", 3, 1, 1), ("w", "X", 3, 0, 1), ("q", "W", 3, 2, 1), ("w", "X", 3, 1, 1), ("q", "X", 3, 0, 1), ("w", "X", 3, 2, 1), ("q", "X", 3, 1, 1), ("q", "X", 3, 2, 1)]:
-            if what == "w":
-                vector.append(weave_step(kind, n, c, count, "V"))
-            elif what == "q":
-                vector.append(quantise_step(kind, n, c, count))
+        def sort_scales(h):
+            return [free_step(lambda q=q: sort_b(b_sc[h], b_sc_raw[h], RUN // 4, slice(32 * q, 32 * q + 4))) for q in range(4)]
+
+        def sort_codes(h):
+            return [([("sorted", h)], [], lambda: sort_b(b_codes[h], b_raw[h], RUN // 2, slice(0, P)))]
+
+        def w(it):
+            return weave_step(*it, 1, "V")
+
+        def q(it):
+            return quantise_step(*it, 1)
+
+        vector += sort_scales(0) + sort_codes(0) + sort_scales(1)
+        vector += [weave_step("W", 0, 0, 2, "V"), quantise_step("W", 0, 0, 2), weave_step("X", 0, 0, 2, "V")] + sort_codes(1)
+        for c in range(1, CHUNKS):
+            before = quantise_step("X", 0, c - 1, 2)
+            mine = weave_step("W", 0, c, 1 if c == LAST else 2, "V")
+            vector += [before, mine] if c == 1 else [mine, before]
+            vector += [w(("X", 0, c)), quantise_step("W", 0, c, 2)]
+        vector += [q(("X", 0, LAST)), w(late_units[0]), q(("X", 1, LAST)), q(late_units[0])]
+        for units, share, ahead in zip(new_units, shares, new_units[1:]):
+            second, third, fourth = units[1:]
+            if second in share:
+                vector += [w(ahead[0]), q(second), w(fourth), q(third)]
             else:
-                vector.append(([("sorted", 1)], [], lambda: sort_b(b_codes[1], b_raw[1], RUN // 2)))
-        behind = [quantise_step("X", 3, 3, 1)]
-        vector += [result_step("O", 0, 0, 2)] + behind + [result_step("O", 1, 0, 2)] + [result_step("C", h, 0, 2) for h in range(HALVES)]
+                vector += [w(second), w(ahead[0]), q(second), q(third), w(fourth)]
+            vector += [q(ahead[0]), q(fourth)]
+        second, third, fourth = new_units[-1][1:]
+        vector += [w(second), w(fourth), q(second), q(third), result_step("O", 0, 0, 2), q(fourth), result_step("O", 1, 0, 2)]
+        vector += [result_step("C", h, 0, 2) for h in range(HALVES)]
         vector += [result_step("O", h, 2, 4) for h in range(HALVES)] + [result_step("C", h, 2, 3) for h in range(HALVES)]
-        vector += [cov_out_step(it, "V") for it in regions[-1][3:]] + [result_step("C", h, 3, 4) for h in range(HALVES)]
+        vector += [bank_out_step(*banks[-1], "V")] + [result_step("C", h, 3, 4) for h in range(HALVES)]
         vector.append(free_step(lambda: nc.vector.transpose(out=d_turned[:], in_=d_rows[:])))
         vector.append(piece_out_step(on_vector[0], "V"))
         vector.append(free_step(lambda: nc.vector.reciprocal(out=d_rec[:], in_=d_turned[:, 0:256:32])))

@@ -26,7 +26,6 @@ BANKS = 8
 WARM_UPS = 5
 WOVEN_PAIRS = 4
 WOVEN_UNITS = 10
-PAIRED_BANKS = 2
 
 
 def tile_concord_precision_gradient_s12_kernel(tc, a_words, a_scales, b_words, b_scales, xw, x, d, out):
@@ -339,7 +338,7 @@ def tile_concord_precision_gradient_s12_kernel(tc, a_words, a_scales, b_words, b
                 waits = [("out", "wide", 2 * piece[2] + e) if piece[1] < 2 else ("out", "row", 6 + e, 2) for e in range(2)]
             return ([("made",) + piece], waits + free, lambda: make_piece(piece, k))
 
-        omega_banks = [(0, k % 2, k // 2) for k in range(PAIRED_BANKS)] + [(h, "four", b) for h in range(HALVES) for b in range(BANKS)][PAIRED_BANKS:]
+        omega_banks = [(h, "four", b) for h in range(HALVES) for b in range(BANKS)]
         tensor.extend(omega_step(it) for it in omega_banks)
         regions = [[(0, "four", b) for b in range(4)], [(0, z, 2) for z in range(2)], [(1, 0, s) for s in range(3)], [(1, 1, s) for s in range(3)]]
         regions.append([(h, z, 3) for h in range(HALVES) for z in range(2)])
@@ -359,7 +358,7 @@ def tile_concord_precision_gradient_s12_kernel(tc, a_words, a_scales, b_words, b
             starts.append(starts[-1] + len(region))
         starts.append(len(outs))
         frees = [outs[starts[r] : starts[r + 1]] for r in range(len(regions) + 1)]
-        shares = [new_units[0][1:3]] + [units[2:3] for units in new_units[1:]]
+        shares = [new_units[0][1:3]] + [units[2:3] for units in new_units[1:LAST]] + [[]]
         scalar += outs[:BANKS] + [weave_step("X", 1, 1, 1, "S")] + frees[0] + [weave_step("X", 1, 2, 1, "S")] + frees[1][:1]
         scalar += [weave_step(kind, 1, LAST, 1, "S") for kind in "WX"] + frees[1][1:]
         for share, steps in zip(shares, frees[2:]):
@@ -395,7 +394,7 @@ def tile_concord_precision_gradient_s12_kernel(tc, a_words, a_scales, b_words, b
                 vector += [w(second), w(ahead[0]), q(second), q(third), w(fourth)]
             vector += [q(ahead[0]), q(fourth)]
         second, third, fourth = new_units[-1][1:]
-        vector += [w(second), w(fourth), q(second), q(third), result_step("O", 0, 0, 2), q(fourth), result_step("O", 1, 0, 2)]
+        vector += [w(second), w(third), q(second), w(fourth), q(third), result_step("O", 0, 0, 2), q(fourth), result_step("O", 1, 0, 2)]
         vector += [result_step("C", h, 0, 2) for h in range(HALVES)]
         vector += [result_step("O", h, 2, 4) for h in range(HALVES)] + [result_step("C", h, 2, 3) for h in range(HALVES)]
         vector += [bank_out_step(*banks[-1], "V")] + [result_step("C", h, 3, 4) for h in range(HALVES)]

@@ -23,7 +23,6 @@ BLOCKS = 4
 WIDTH = 256
 RUN = 8
 BANKS = 8
-WARM_UPS = 5
 WOVEN_PAIRS = 4
 WOVEN_UNITS = 10
 
@@ -241,13 +240,6 @@ def tile_concord_precision_gradient_s12_kernel(tc, a_words, a_scales, b_words, b
 
         for t in (a_sc, b_sc_all):
             nc.vector.memset(t[:].bitcast(I32), 0)
-        idle_codes = sbuf("idle_codes", [P, 512], U32)
-        idle_sc = sbuf("idle_sc", [P, 512], U8)
-        for lo in (0, WIDTH):
-            nc.vector.quantize_mx(out=idle_codes[:, lo : lo + WIDTH].bitcast(FP8X4), scales=idle_sc[:, lo : lo + WIDTH], in_=b_sc_all[:].bitcast(BF16))
-        idle = bank(BANKS - 1)
-        for k in range(WARM_UPS):
-            nc.tensor.matmul_mx(out=idle[:], lhsT=idle_codes[:, 0:P].bitcast(FP8X4), lhsT_scale=idle_sc[:, 0:P], rhs=idle_codes[:].bitcast(FP8X4), rhs_scale=idle_sc[:], start=True, stop=True)
         nc.gpsimd.memset(ident_wide[:], 0.0)
         make_identity(nc, ident, nomemset=True)
         nc.gpsimd.memset(d_rows[:], 0.0)

from contextlib import ExitStack

import concourse.mybir as mybir
from concourse.masks import make_identity

FLOPS = 2 * 1024 * 1024 * (1024 + 2048 + 1024)

F32 = mybir.dt.float32
BF16 = mybir.dt.bfloat16
I32 = mybir.dt.int32
U32 = mybir.dt.uint32
U8 = mybir.dt.uint8
FP8X4 = mybir.dt.float8_e4m3fn_x4
FP4X4 = mybir.dt.float4_e2m1fn_x4
ALU = mybir.AluOpType

P = 128
HALVES = 2
SLOTS = 4
CHUNKS = 4
LAST = CHUNKS - 1
BLOCKS = 4
WIDTH = 256
RUN = 8
BANKS = 8
WOVEN_PAIRS = 4
WOVEN_UNITS = 10


def tile_concord_precision_gradient_s12_kernel(tc, a_words, a_scales, b_words, b_scales, xw, x, d, out):
    nc = tc.nc
    with ExitStack() as ctx:
        keep = ctx.enter_context(tc.tile_pool(name="keep", bufs=1))
        psum = ctx.enter_context(tc.psum_pool(name="psum", bufs=1))
        ctx.enter_context(tc.manual_schedule())

        def sbuf(name, shape, dt, tag=None):
            t = keep.tile(shape, dt, name=name, tag=tag or name, align_bytes=256)
            return t

        def bank(k):
            t = psum.tile([P, 512], F32, name="bank%d" % k, tag="bank%d" % k)
            return t

        def copy(eng, dst, src):
            if eng == "S":
                nc.scalar.copy(out=dst, in_=src)
            else:
                nc.vector.tensor_copy(out=dst, in_=src)

        a_codes = [sbuf("a_codes%d" % q, [P, 2, 1024], U8) for q in range(2)]
        a_sc = sbuf("a_sc", [P, 2, 1024], U8)
        b_raw = [sbuf("b_raw%d" % h, [P, 2, 1024], U8) for h in range(HALVES)]
        b_codes = [sbuf("b_codes%d" % h, [P, 2, 1024], U8) for h in range(HALVES)]
        b_sc_rows = sbuf("b_sc_rows", [P, 2, 1024], U8)
        b_sc_raw = [b_sc_rows[:, :, h * 512 : (h + 1) * 512] for h in range(HALVES)]
        b_sc_all = sbuf("b_sc", [P, 2048], U8)
        b_sc = [b_sc_all[:, h * 1024 : (h + 1) * 1024].rearrange("p (g n) -> p g n", g=2) for h in range(HALVES)]
        pairs = [(kind, k, c) for kind in "WX" for k in range(2) for c in range(CHUNKS)]
        codes = {it: sbuf("codes%s%d%d" % it, [P, 512], U32) for it in pairs}
        scales = {it: sbuf("scales%s%d%d" % it, [P, 512], U8) for it in pairs}
        o_codes = [sbuf("o_codes%d" % h, [P, 1024], U32) for h in range(HALVES)]
        o_sc = [sbuf("o_sc%d" % h, [P, 1024], U8) for h in range(HALVES)]
        c_codes = [sbuf("c_codes%d" % h, [P, 1024], U32) for h in range(HALVES)]
        c_sc = [sbuf("c_sc%d" % h, [P, 1024], U8) for h in range(HALVES)]
        o_words = {(h, z): sbuf("o_words%d%d" % (h, z), [P, 512, SLOTS], BF16) for h in range(HALVES) for z in range(2)}
        c_words = {(h, z): sbuf("c_words%d%d" % (h, z), [P, 512, SLOTS], BF16) for h in range(HALVES) for z in range(2)}
        ident_wide = sbuf("ident_wide", [P, 3 * P], F32)
        ident = ident_wide[:, P : 2 * P]
        d_rows = sbuf("d_rows", [P, 256], BF16)
        d_turned = sbuf("d_turned", [P, 256], BF16)
        d_rec = sbuf("d_rec", [P, 8], F32)
        d_neg = sbuf("d_neg", [P, 8], F32)
        raw, woven, ps, g_sb, spent = {}, {}, {}, {}, []

        def load_codes(dst, src, half):
            nc.sync.dma_start(out=dst[:].bitcast(I32), in_=src[:, :, half * 1024 : (half + 1) * 1024].bitcast(I32).rearrange("g p n -> p g n"))

        def load_scales(dst, src, rows):
            for r in rows:
                nc.sync.dma_start(out=dst[r:P:32, :, :].bitcast(I32), in_=src[:, r:16:4, :].bitcast(I32).rearrange("g q n -> q g n"))

        def load_rows(kind, c, lo, hi):
            name = "raw%s%d%d" % (kind, lo, c)
            spent.append(name)
            t = sbuf(name, [P, SLOTS, (hi - lo) * WIDTH], BF16)
            for n in range(lo, hi):
                raw[kind, n, c] = t[:, :, (n - lo - n % 2 * (kind == "W")) * WIDTH :]
            src = (xw if kind == "W" else x)[c * 512 : (c + 1) * 512, lo * WIDTH : hi * WIDTH]
            nc.sync.dma_start(out=t[:], in_=src.rearrange("(p t) w -> p t w", t=SLOTS))

        def sort_b(dst, src, words, rows):
            nc.vector.tensor_copy(
                out=dst[rows].bitcast(I32).rearrange("p g (u q w) -> p g u q w", u=SLOTS, w=words),
                in_=src[rows].bitcast(I32).rearrange("p g (q u w) -> p g u q w", u=SLOTS, w=words),
            )

        def weave(kind, n, c, count, eng):
            dst = woven[kind, n, c, count]
            if kind == "W":
                lo = 2 * (n % 2)
                dst = dst.rearrange("p (u q w t) -> p q u t w", u=2 * count, w=RUN, t=SLOTS)
                src = raw[kind, n, c][:, :, 0:512].rearrange("p t (q u w) -> p q u t w", u=SLOTS, w=RUN)[:, :, lo : lo + 2 * count]
            else:
                dst = dst.rearrange("p (a w t) -> p a t w", w=RUN, t=SLOTS)
                src = raw[kind, n, c][:, :, 0 : count * WIDTH].rearrange("p t (a w) -> p a t w", w=RUN)
            copy(eng, dst, src)

        def quantise(kind, n, c, count):
            cols = slice((n % 2) * WIDTH, (n % 2 + count) * WIDTH)
            nc.vector.quantize_mx(out=codes[kind, n // 2, c][:, cols].bitcast(FP8X4), scales=scales[kind, n // 2, c][:, cols], in_=woven[kind, n, c, count])

        def slots_out(eng, dst, src, count):
            copy(eng, dst.rearrange("p (n e) u -> p n u e", e=2), src[:].rearrange("p (u n e) -> p n u e", u=count, e=2))

        def shape_of(it):
            h, z, n = it
            return (range(SLOTS), n * P, P) if z == "four" else (range(2 * z, 2 * z + 2), n * WIDTH, WIDTH)

        def omega(it, k):
            t = bank(k)
            ps["O", it] = t
            slots, lo, width = shape_of(it)
            for e, u in enumerate(slots):
                for g in range(2):
                    nc.tensor.matmul_mx(
                        out=t[:, e * width : (e + 1) * width],
                        lhsT=b_codes[it[0]][:, g, u * 256 : (u + 1) * 256].bitcast(FP4X4),
                        lhsT_scale=b_sc[it[0]][:, g, u * P : (u + 1) * P],
                        rhs=a_codes[lo // 512][:, g, 2 * (lo % 512) : 2 * (lo % 512 + width)].bitcast(FP4X4),
                        rhs_scale=a_sc[:, g, lo : lo + width],
                        start=(g == 0),
                        stop=(g == 1),
                    )

        def cov(it, c, n, k):
            if n == 0:
                ps["C", it] = bank(k)
            slots, lo, width = shape_of(it)
            cols = slice(lo % 512, lo % 512 + width)
            for e, u in enumerate(slots):
                nc.tensor.matmul_mx(
                    out=ps["C", it][:, e * width : (e + 1) * width],
                    lhsT=codes["W", it[0], c][:, u * P : (u + 1) * P].bitcast(FP8X4),
                    lhsT_scale=scales["W", it[0], c][:, u * P : (u + 1) * P],
                    rhs=codes["X", lo // 512, c][:, cols].bitcast(FP8X4),
                    rhs_scale=scales["X", lo // 512, c][:, cols],
                    start=(n == 0 and e == 0),
                    stop=(n == LAST and e == len(slots) - 1),
                )

        def bank_out(kind, it, eng):
            slots, lo, width = shape_of(it)
            words = (o_words if kind == "O" else c_words)[it[0], lo // 512]
            slots_out(eng, words[:, lo % 512 : lo % 512 + width, slots[0] : slots[-1] + 1], ps[kind, it], len(slots))

        def quantise_result(kind, h, lo, hi):
            dst, sc, src = (o_codes, o_sc, o_words) if kind == "O" else (c_codes, c_sc, c_words)
            cols = slice(lo * WIDTH, hi * WIDTH)
            words = src[h, lo // 2][:, (lo % 2) * WIDTH : (lo % 2 + hi - lo) * WIDTH, :]
            nc.vector.quantize_mx(out=dst[h][:, cols].bitcast(FP8X4), scales=sc[h][:, cols], in_=words.rearrange("p n u -> p (n u)"))

        def grad(dst, b, lo, n):
            rows = slice(b * P, (b + 1) * P)
            cols = slice(lo, lo + n)
            for side, (lc, ls, rc, rs) in enumerate(((o_codes, o_sc, c_codes, c_sc), (c_codes, c_sc, o_codes, o_sc))):
                for h in range(HALVES):
                    nc.tensor.matmul_mx(
                        out=dst,
                        lhsT=lc[h][:, rows].bitcast(FP8X4),
                        lhsT_scale=ls[h][:, rows],
                        rhs=rc[h][:, cols].bitcast(FP8X4),
                        rhs_scale=rs[h][:, cols],
                        start=(side == 0 and h == 0),
                        stop=(side == 1 and h == 1),
                    )

        def on_diagonal(piece):
            return piece[0] in ("square", "row") and piece[2] == (piece[1] if piece[0] == "square" else piece[1] // 2)

        def lower_tile(b, m):
            s, e = divmod(b, 2)
            if s >= 2 and m < 4:
                return g_sb["wide", b][:, m * P : (m + 1) * P]
            return g_sb["square", s, m // 2][:, e * WIDTH + (m % 2) * P : e * WIDTH + (m % 2 + 1) * P]

        def make_piece(piece, k):
            t = bank(k)
            ps[piece] = t
            if piece[0] == "wide":
                grad(t[:], piece[1], 0, 512)
            elif piece[0] == "row":
                grad(t[:, 0:WIDTH], piece[1], piece[2] * WIDTH, WIDTH)
            elif piece[0] == "square":
                for e in range(2):
                    grad(t[:, e * WIDTH : (e + 1) * WIDTH], 2 * piece[1] + e, piece[2] * WIDTH, WIDTH)
            else:
                r, s = piece[1:]
                for f in range(2):
                    for e in range(2):
                        nc.tensor.transpose(t[:, e * WIDTH + f * P : e * WIDTH + (f + 1) * P], lower_tile(2 * s + f, 2 * r + e), ident)

        def less_diagonal(dst, src, b):
            lo = P - (b % 2) * P
            nc.vector.scalar_tensor_tensor(out=dst, in0=ident_wide[:, lo : lo + WIDTH], scalar=d_neg[:, b : b + 1], in1=src, op0=ALU.mult, op1=ALU.add)

        def result(name, width):
            return sbuf(name, [P, width], F32, spent.pop(0) if spent else name)

        def piece_out(piece, eng):
            t = ps[piece]
            if piece[0] == "row" and on_diagonal(piece):
                g_sb[piece] = result("g_row%d" % piece[1], WIDTH)
                less_diagonal(g_sb[piece][:], t[:, 0:WIDTH], piece[1])
            elif piece[0] == "row":
                s, e = divmod(piece[1], 2)
                if e == 0:
                    g_sb["square", s, piece[2]] = result("g_square%d%d" % (s, piece[2]), 512)
                copy(eng, g_sb["square", s, piece[2]][:, e * WIDTH : (e + 1) * WIDTH], t[:, 0:WIDTH])
            else:
                g_sb[piece] = result("g_%s%d%d" % (piece[0], piece[1], piece[-1]), 512)
                if on_diagonal(piece):
                    for e in range(2):
                        less_diagonal(g_sb[piece][:, e * WIDTH : (e + 1) * WIDTH], t[:, e * WIDTH : (e + 1) * WIDTH], 2 * piece[1] + e)
                else:
                    copy(eng, g_sb[piece][:], t[:])

        def store_square(g, s, r):
            nc.sync.dma_start(out=out[s * WIDTH : (s + 1) * WIDTH, r * WIDTH : (r + 1) * WIDTH].rearrange("(e p) c -> p e c", e=2), in_=g[:].rearrange("p (e c) -> p e c", e=2))

        def store_piece(piece):
            if piece[0] == "wide":
                nc.sync.dma_start(out=out[piece[1] * P : (piece[1] + 1) * P, 0:512], in_=g_sb[piece][:])
            elif piece[0] != "row":
                store_square(g_sb[piece], piece[1], piece[2])
            elif on_diagonal(piece):
                nc.sync.dma_start(out=out[piece[1] * P : (piece[1] + 1) * P, piece[2] * WIDTH : (piece[2] + 1) * WIDTH], in_=g_sb[piece][:])
            elif piece[1] % 2:
                store_square(g_sb["square", piece[1] // 2, piece[2]], piece[1] // 2, piece[2])

        for t in (a_sc, b_sc_all):
            nc.vector.memset(t[:].bitcast(I32), 0)
        nc.gpsimd.memset(ident_wide[:], 0.0)
        make_identity(nc, ident, nomemset=True)
        nc.gpsimd.memset(d_rows[:], 0.0)
        nc.gpsimd.dma_start(out=d_rows[0:P:32, :].rearrange("q (b a) -> q b a", a=32), in_=d.rearrange("(b q a) -> q b a", q=4, a=32))

        load_scales(b_sc_rows, b_scales, range(4))
        load_codes(b_raw[0], b_words, 0)
        load_scales(a_sc, a_scales, range(2))
        load_codes(a_codes[0], a_words, 0)
        load_scales(a_sc, a_scales, range(2, 4))
        load_rows("W", 0, 0, 2)
        load_codes(a_codes[1], a_words, 1)
        load_rows("X", 0, 0, 2)
        load_codes(b_raw[1], b_words, 1)
        for c in range(1, CHUNKS):
            load_rows("W", c, 0, 4 if c == LAST else 2)
            load_rows("X", c, 0, 2)
        for kind, lo, hi, count in (("X", 2, 3, CHUNKS), ("W", 2, 4, LAST), ("X", 3, 4, CHUNKS)):
            for c in range(count):
                load_rows(kind, c, lo, hi)

        tensor, vector, scalar, stores = [], [], [], []
        holders = {}
        first_pairs = [(kind, 0, c) for c in range(CHUNKS) for kind in "WX"]
        turned = [LAST] + list(range(LAST))
        new_units = [[(kind, n, c) for c in (turned if kind == "W" else range(CHUNKS))] for kind, n in (("X", 2), ("W", 2), ("W", 3), ("X", 3))]
        late_units = [it for units in new_units for it in units]

        def open_woven(kind, n, c):
            if n < 2 and (kind, 0, c, 2) not in woven:
                k = first_pairs.index((kind, 0, c))
                t = sbuf("woven%s%d" % (kind, c), [P, 2048], BF16, "woven_pair%d" % (k % WOVEN_PAIRS))
                woven[kind, 0, c, 2], woven[kind, 0, c, 1], woven[kind, 1, c, 1] = t[:], t[:, 0:1024], t[:, 1024:2048]
            elif n >= 2:
                k = late_units.index((kind, n, c))
                t = sbuf("woven%s%d%d" % (kind, n, c), [P, 1024], BF16, "woven_unit%d" % (k % WOVEN_UNITS))
                woven[kind, n, c, 1] = t[:]

        def weave_step(kind, n, c, count, eng):
            if n < 2:
                k = first_pairs.index((kind, 0, c)) - WOVEN_PAIRS
                frees = [("quantised", first_pairs[k][0], e, first_pairs[k][2]) for e in range(2)] if k >= 0 else []
            else:
                k = late_units.index((kind, n, c)) - WOVEN_UNITS
                frees = [("quantised",) + late_units[k]] if k >= 0 else []
            return ([("woven", kind, n + e, c) for e in range(count)], frees, lambda: (open_woven(kind, n, c), weave(kind, n, c, count, eng)))

        def quantise_step(kind, n, c, count):
            return ([("quantised", kind, n + e, c) for e in range(count)], [("woven", kind, n + e, c) for e in range(count)], lambda: quantise(kind, n, c, count))

        def result_step(kind, h, lo, hi):
            waits = [("out", kind, it) for other, it in banks if other == kind and it[0] == h and lo <= shape_of(it)[1] // WIDTH < hi]
            return ([("quantised", kind, h, s) for s in range(lo, hi)], waits, lambda: quantise_result(kind, h, lo, hi))

        def bank_out_step(kind, it, eng):
            return ([("out", kind, it)], [("made", kind, it)], lambda: bank_out(kind, it, eng))

        def piece_out_step(piece, eng):
            return ([("out",) + piece], [("made",) + piece], lambda: piece_out(piece, eng))

        def free_step(call):
            return ([], [], call)

        def take_bank(emptied_by):
            k = len(holders) % BANKS
            waits = [holders[len(holders) - BANKS]] if len(holders) >= BANKS else []
            holders[len(holders)] = emptied_by
            return k, waits

        def omega_step(it):
            k, waits = take_bank(("out", "O", it))
            return ([("made", "O", it)], [("sorted", it[0])] + waits, lambda: omega(it, k))

        def cov_step(it, c, n):
            k, waits = take_bank(("out", "C", it)) if n == 0 else (None, [])
            slots, lo, width = shape_of(it)
            waits += [("quantised", "W", 2 * it[0] + u // 2, c) for u in slots] + [("quantised", "X", lo // WIDTH, c)]
            return ([("made", "C", it)] if n == LAST else [], waits, lambda: cov(it, c, n, k))

        def piece_step(piece):
            k, free = take_bank(("out",) + piece)
            if piece[0] != "mirror":
                top = piece[1] if piece[0] == "square" else piece[1] // 2
                waits = [("quantised", kind, h, s) for kind in "OC" for h in range(HALVES) for s in range(top + 1)]
            elif piece[2] == 1:
                waits = [("out", "square", 1, 0)]
            else:
                waits = [("out", "wide", 2 * piece[2] + e) if piece[1] < 2 else ("out", "row", 6 + e, 2) for e in range(2)]
            return ([("made",) + piece], waits + free, lambda: make_piece(piece, k))

        omega_banks = [(h, "four", b) for h in range(HALVES) for b in range(BANKS)]
        tensor.extend(omega_step(it) for it in omega_banks)
        regions = [[(0, "four", b) for b in range(4)], [(0, z, 2) for z in range(2)], [(1, 0, s) for s in range(3)], [(1, 1, s) for s in range(3)]]
        regions.append([(h, z, 3) for h in range(HALVES) for z in range(2)])
        for region in regions:
            order = turned if region[0][0] == 1 else range(CHUNKS)
            tensor.extend(cov_step(it, c, n) for n, c in enumerate(order) for it in region)
        banks = [("O", it) for it in omega_banks] + [("C", it) for region in regions for it in region]
        pieces = [("square", 1, 0), ("wide", 4), ("wide", 5), ("wide", 6), ("mirror", 0, 1), ("mirror", 0, 2), ("mirror", 1, 2)]
        pieces += [("wide", 7), ("row", 6, 2), ("row", 7, 2), ("square", 0, 0)] + [("mirror", r, 3) for r in range(3)]
        pieces += [("square", 1, 1), ("square", 2, 2), ("row", 6, 3), ("row", 7, 3)]
        tensor.extend(piece_step(piece) for piece in pieces)
        stores.extend(([], [("out",) + piece], lambda piece=piece: store_piece(piece)) for piece in pieces)

        outs = [bank_out_step(kind, it, "S") for kind, it in banks[:-1]]
        starts = [BANKS]
        for region in regions:
            starts.append(starts[-1] + len(region))
        starts.append(len(outs))
        frees = [outs[starts[r] : starts[r + 1]] for r in range(len(regions) + 1)]
        shares = [new_units[0][1:3]] + [units[2:3] for units in new_units[1:LAST]] + [[]]
        scalar += outs[:BANKS] + [weave_step("X", 1, 1, 1, "S")] + frees[0] + [weave_step("X", 1, 2, 1, "S")] + frees[1][:1]
        scalar += [weave_step(kind, 1, LAST, 1, "S") for kind in "WX"] + frees[1][1:]
        for share, steps in zip(shares, frees[2:]):
            scalar += [weave_step(*it, 1, "S") for it in share] + steps
        on_vector = [piece for piece in pieces if on_diagonal(piece) or piece in (("wide", 6), ("wide", 7), ("mirror", 0, 2), ("mirror", 1, 3))]
        scalar.extend(piece_out_step(piece, "S") for piece in pieces if piece not in on_vector)

        def sort_scales(h):
            return [free_step(lambda q=q: sort_b(b_sc[h], b_sc_raw[h], RUN // 4, slice(32 * q, 32 * q + 4))) for q in range(4)]

        def sort_codes(h):
            return [([("sorted", h)], [], lambda: sort_b(b_codes[h], b_raw[h], RUN // 2, slice(0, P)))]

        def w(it):
            return weave_step(*it, 1, "V")

        def q(it):
            return quantise_step(*it, 1)

        vector += sort_scales(0) + sort_codes(0) + sort_scales(1)
        vector += [weave_step("W", 0, 0, 2, "V"), quantise_step("W", 0, 0, 2), weave_step("X", 0, 0, 2, "V")] + sort_codes(1)
        for c in range(1, CHUNKS):
            before = quantise_step("X", 0, c - 1, 2)
            mine = weave_step("W", 0, c, 1 if c == LAST else 2, "V")
            vector += [before, mine] if c == 1 else [mine, before]
            vector += [w(("X", 0, c)), quantise_step("W", 0, c, 2)]
        vector += [q(("X", 0, LAST)), w(late_units[0]), q(("X", 1, LAST)), q(late_units[0])]
        for units, share, ahead in zip(new_units, shares, new_units[1:]):
            second, third, fourth = units[1:]
            if second in share:
                vector += [w(ahead[0]), q(second), w(fourth), q(third)]
            else:
                vector += [w(second), w(ahead[0]), q(second), q(third), w(fourth)]
            vector += [q(ahead[0]), q(fourth)]
        second, third, fourth = new_units[-1][1:]
        vector += [w(second), w(third), q(second), w(fourth), q(third), result_step("O", 0, 0, 2), q(fourth), result_step("O", 1, 0, 2)]
        vector += [result_step("C", h, 0, 2) for h in range(HALVES)]
        vector += [result_step("O", h, 2, 4) for h in range(HALVES)] + [result_step("C", h, 2, 3) for h in range(HALVES)]
        vector += [bank_out_step(*banks[-1], "V")] + [result_step("C", h, 3, 4) for h in range(HALVES)]
        vector.append(free_step(lambda: nc.vector.transpose(out=d_turned[:], in_=d_rows[:])))
        vector.append(piece_out_step(on_vector[0], "V"))
        vector.append(free_step(lambda: nc.vector.reciprocal(out=d_rec[:], in_=d_turned[:, 0:256:32])))
        vector.append(free_step(lambda: nc.vector.tensor_scalar(out=d_neg[:], in0=d_rec[:], scalar1=-1.0, scalar2=None, op0=ALU.mult)))
        vector.extend(piece_out_step(piece, "V") for piece in on_vector[1:])

        written = []
        queues = [tensor, vector, scalar, stores]
        while any(queues):
            moved = 0
            for queue in queues:
                while queue and all(w in written for w in queue[0][1]):
                    makes, waits, call = queue.pop(0)
                    call()
                    written.extend(makes)
                    moved += 1
            assert moved
